import numpy as np
import ml_dtypes


def mxq(x, axis, fmt="e4m3"):
    dtype, down = {"e4m3": (ml_dtypes.float8_e4m3fn, 7), "e5m2": (ml_dtypes.float8_e5m2, 14)}[fmt]
    v = np.moveaxis(np.asarray(x, np.float32).astype(ml_dtypes.bfloat16).astype(np.float64), axis, -1)
    blocks = v.reshape(v.shape[:-1] + (-1, 32))
    amax = np.abs(blocks).max(-1, keepdims=True)
    byte = np.maximum(np.where(amax > 0, np.frexp(amax)[1] - 1 + 127, 0) - down, 1)
    scale = np.exp2(byte - 127.0)
    codes = (blocks / scale).astype(np.float32).astype(dtype).astype(np.float64)
    return np.moveaxis((codes * scale).reshape(v.shape), -1, axis)


WIDE = False


def mx_kscale(k):
    if not WIDE:
        return np.ones(k)
    levels = np.array([18, -18])
    if k % 512:
        return np.exp2(np.random.permutation(np.resize(levels, k // 32))).repeat(32)
    a = np.empty((k // 512, 16))
    for p in range(k // 512):
        a[p, :8] = np.random.permutation(np.resize(levels, 8))
        for g in range(8):
            far = levels[np.abs(levels - a[p, g]) >= 10]
            a[p, g + 8] = far[np.random.randint(len(far))]
    return np.exp2(a.ravel()).repeat(32)


def f64(x):
    return np.asarray(x).astype(np.float64)


def striped(idx):
    return np.tile(np.asarray(idx).reshape(-1, 16).T, (8, 1)).astype(np.uint16)


def unstriped(offs):
    return offs[:16].T.reshape(-1).astype(np.int64)


B, N, T, D, R = 1, 512, 2048, 512, 1024


def setup_inputs():
    n = np.random.standard_normal
    idx = np.random.permutation(T)[:B * N]
    s = mx_kscale(D)[:, None]
    z = mx_kscale(R)[:, None]
    x = n((B, D, R))
    return {
        "xT": (x * s).astype(np.float32),
        "wT": (n((D, T)) * (1.00 / np.sqrt(D)) / s).astype(np.float32),
        "vT": (n((D, T)) / np.sqrt(D) / s).astype(np.float32),
        "wt": (np.random.uniform(0.5, 1.5, (B, R, 1)) * 1.0 / np.sqrt(R) * z).astype(np.float32),
        "xm": (x.transpose(0, 2, 1) / z).astype(np.float32),
        "offs": striped(idx),
    }


def reference(xT, wT, vT, wt, xm, offs):
    idx = unstriped(offs)
    pick = lambda x: x[:, idx].reshape(x.shape[0], B, N).transpose(1, 0, 2)
    xq = mxq(f64(xT), 1, "e4m3").transpose(0, 2, 1)
    a = xq @ mxq(pick(f64(wT)), 1, "e4m3")
    av = xq @ mxq(pick(f64(vT)), 1, "e4m3")
    g = f64(wt) * (a - av)
    dw = mxq(f64(xm), 1, "e4m3").transpose(0, 2, 1) @ mxq(g, 1, "e5m2")
    gw = np.zeros((D, T))
    gw[:, idx] = dw.transpose(1, 0, 2).reshape(D, B * N)
    return gw

@@ -1,0 +1,192 @@
+from contextlib import ExitStack
+
+import concourse.mybir as mybir
+
+N, T, D, R = 512, 2048, 512, 1024
+FLOPS = 3 * 2 * N * D * R
+
+F32 = mybir.dt.float32
+BF16 = mybir.dt.bfloat16
+U32 = mybir.dt.uint32
+U16 = mybir.dt.uint16
+U8 = mybir.dt.uint8
+E4M3 = mybir.dt.float8_e4m3fn_x4
+E5M2 = mybir.dt.float8_e5m2_x4
+COPY = mybir.ActivationFunctionType.Copy
+MULT = mybir.AluOpType.mult
+
+P = 128
+PACK = 4
+K_PASS = P * PACK
+ROW_PASSES = R // K_PASS
+BLOCKS = D // P
+QUARTERS = N // P
+LIST_ROWS = 16
+
+
+def tile_attend_gds_sq_kernel(tc, xT, wT, vT, wt, xm, offs, out):
+    nc = tc.nc
+    with ExitStack() as ctx:
+        keep = ctx.enter_context(tc.tile_pool(name="keep", bufs=1))
+        psum = ctx.enter_context(tc.psum_pool(name="psum", bufs=1))
+
+        def operand(name, width):
+            grouped = keep.tile([P, width, PACK], BF16, name=name + "_grouped", align_bytes=64)
+            codes = keep.tile([P, width], U32, name=name + "_codes", align_bytes=64)
+            scales = keep.tile([P, width], U8, name=name + "_scales", align_bytes=64)
+            return grouped, codes, scales
+
+        def quantize(op, c0, c1, fmt):
+            grouped, codes, scales = op
+            nc.vector.quantize_mx(
+                out=codes[:, c0:c1].bitcast(fmt),
+                scales=scales[:, c0:c1],
+                in_=grouped[:, c0:c1, :].rearrange("p w j -> p (w j)"),
+            )
+
+        def matmul(acc, lhs, l0, rhs, r0, r1, rhs_fmt, start, stop):
+            nc.tensor.matmul_mx(
+                out=acc,
+                lhsT=lhs[1][:, l0 : l0 + P].bitcast(E4M3),
+                lhsT_scale=lhs[2][:, l0 : l0 + P],
+                rhs=rhs[1][:, r0:r1].bitcast(rhs_fmt),
+                rhs_scale=rhs[2][:, r0:r1],
+                start=start,
+                stop=stop,
+            )
+
+        offsets = keep.tile([P, N // LIST_ROWS], U16, name="offsets")
+        nc.sync.dma_start(offsets[:], offs)
+
+        v_rows = vT.rearrange("(p j) t -> p j t", j=PACK)
+        w_rows = wT.rearrange("(p j) t -> p j t", j=PACK)
+        x_rows = xT[0].rearrange("(p j) r -> p j r", j=PACK)
+        xm_rows = xm[0].rearrange("(h p j) d -> h p j d", p=P, j=PACK)
+
+        v_planes = [keep.tile([P, T], F32, name=f"v_plane{j}") for j in range(PACK)]
+        w_planes = [keep.tile([P, T], F32, name=f"w_plane{j}") for j in range(PACK)]
+        x_pieces = [(0, 0, P), (1, 0, P // 2), (1, P // 2, P)]
+        x_raw = [keep.tile([P, PACK, PACK * (m1 - m0)], F32, name=f"x_raw{h}_{m0}") for h, m0, m1 in x_pieces]
+        xm_raw = [keep.tile([P, PACK, D], F32, name=f"xm_raw{h}") for h in range(ROW_PASSES)]
+        weights = keep.tile([P, ROW_PASSES, PACK], F32, name="weights")
+
+        def load_x(k):
+            h, m0, m1 = x_pieces[k]
+            nc.sync.dma_start(x_raw[k][:], x_rows[:, :, h * K_PASS + PACK * m0 : h * K_PASS + PACK * m1])
+
+        for j in range(PACK):
+            nc.sync.dma_start(v_planes[j][:], v_rows[:, j, :])
+        nc.sync.dma_start(weights[:], wt[0].rearrange("(h p t) o -> p h (t o)", p=P, t=PACK))
+        load_x(0)
+        for j in range(PACK):
+            nc.sync.dma_start(w_planes[j][:], w_rows[:, j, :])
+        load_x(1)
+        load_x(2)
+        for h in range(ROW_PASSES):
+            nc.sync.dma_start(xm_raw[h][:], xm_rows[h])
+
+        windows = [keep.tile([P, T], F32, name=f"window{b}") for b in range(BLOCKS)]
+
+        v_op = operand("v", N)
+        w_op = operand("w", N)
+        x_ops = [operand(f"x{h}", K_PASS) for h in range(ROW_PASSES)]
+        xm_ops = [operand(f"xm{h}", D) for h in range(ROW_PASSES)]
+        g_ops = [operand(f"g{h}", N) for h in range(ROW_PASSES)]
+
+        def group_x(k):
+            h, m0, m1 = x_pieces[k]
+            nc.scalar.copy(
+                out=x_ops[h][0][:].rearrange("p (t m) j -> p m j t", t=PACK)[:, m0:m1],
+                in_=x_raw[k][:].rearrange("p j (m t) -> p m j t", t=PACK),
+            )
+
+        def group_xm(h, b):
+            cols = slice(b * P, (b + 1) * P)
+            nc.scalar.copy(
+                out=xm_ops[h][0][:, cols, :].rearrange("p (c i) j -> p c j i", i=PACK),
+                in_=xm_raw[h][:, :, cols].rearrange("p j (c i) -> p c j i", i=PACK),
+            )
+
+        v_picked = keep.tile([P, PACK, N], F32, name="v_picked")
+        for j in range(PACK):
+            nc.vector.tensor_copy(v_picked[:, j, :], v_planes[j][:].indirect(offsets[:]))
+        nc.scalar.activation(
+            out=v_op[0][:].rearrange("p (c i) j -> p c j i", i=PACK),
+            in_=v_picked[:].rearrange("p j (c i) -> p c j i", i=PACK),
+            func=COPY,
+            scale=-1.0,
+        )
+        group_x(0)
+        quantize(v_op, 0, N, E4M3)
+        quantize(x_ops[0], 0, K_PASS, E4M3)
+
+        score = [
+            [psum.tile([P, PACK, P], F32, name=f"score{h}_{c}", tag=f"bank{QUARTERS * h + c}") for c in range(QUARTERS)]
+            for h in range(ROW_PASSES)
+        ]
+
+        def score_passes(h, c, table, first):
+            for t in range(PACK):
+                matmul(score[h][c][:, t, :], x_ops[h], t * P, table, c * P, (c + 1) * P, E4M3,
+                       first and t == 0, (not first) and t == PACK - 1)
+
+        def weigh(h, c):
+            nc.vector.tensor_tensor(
+                g_ops[h][0][:, c * P : (c + 1) * P, :],
+                score[h][c][:].rearrange("p t i -> p i t"),
+                weights[:, h : h + 1, :].to_broadcast([P, P, PACK]),
+                MULT,
+            )
+
+        for c in range(QUARTERS):
+            score_passes(0, c, v_op, True)
+
+        for j in range(PACK - 1):
+            nc.vector.tensor_copy(w_op[0][:, :, j], w_planes[j][:].indirect(offsets[:]))
+        half = N // 2
+        for u in range(2):
+            lst = offsets[:, u * half // LIST_ROWS : (u + 1) * half // LIST_ROWS]
+            nc.vector.tensor_copy(w_op[0][:, u * half : (u + 1) * half, PACK - 1], w_planes[PACK - 1][:].indirect(lst))
+        for u in range(2):
+            quantize(w_op, u * half, (u + 1) * half, E4M3)
+        group_x(1)
+        group_x(2)
+
+        for c in range(QUARTERS):
+            score_passes(0, c, w_op, False)
+        quantize(x_ops[1], 0, K_PASS, E4M3)
+        for c in range(QUARTERS):
+            weigh(0, c)
+        for c in range(QUARTERS):
+            score_passes(1, c, v_op, True)
+            score_passes(1, c, w_op, False)
+        quantize(g_ops[0], 0, N, E5M2)
+        for b in range(BLOCKS):
+            for h in range(ROW_PASSES):
+                group_xm(h, b)
+        for c in range(QUARTERS):
+            weigh(1, c)
+            if c > 0:
+                quantize(g_ops[1], (c - 1) * P, c * P, E5M2)
+        for h in range(ROW_PASSES):
+            quantize(xm_ops[h], 0, P, E4M3)
+        quantize(g_ops[1], N - P, N, E5M2)
+
+        for b in range(BLOCKS):
+            nc.vector.memset(windows[b][:], 0.0)
+        for b in range(BLOCKS):
+            if b > 0:
+                for h in range(ROW_PASSES):
+                    quantize(xm_ops[h], b * P, (b + 1) * P, E4M3)
+            acc = psum.tile([P, N], F32, name=f"grad{b}", tag=f"bank{b}")
+            for h in range(ROW_PASSES):
+                matmul(acc[:], xm_ops[h], b * P, g_ops[h], 0, N, E5M2, h == 0, h == ROW_PASSES - 1)
+            grad = keep.tile([P, N], F32, name=f"grad_sb{b}")
+            pieces = 2 if b == 0 else 1
+            width = N // pieces
+            for u in range(pieces):
+                nc.scalar.copy(out=grad[:, u * width : (u + 1) * width], in_=acc[:, u * width : (u + 1) * width])
+            for u in range(pieces):
+                lst = offsets[:, u * width // LIST_ROWS : (u + 1) * width // LIST_ROWS]
+                nc.vector.tensor_copy(windows[b][:].indirect(lst), grad[:, u * width : (u + 1) * width])
+            nc.sync.dma_start(out[b * P : (b + 1) * P, :], windows[b][:])

@@ -30,9 +30,9 @@ def tile_attend_gds_sq_kernel(tc, xT, wT, vT, wt, xm, offs, out):
         keep = ctx.enter_context(tc.tile_pool(name="keep", bufs=1))
         psum = ctx.enter_context(tc.psum_pool(name="psum", bufs=1))
 
-        def operand(name, width):
+        def operand(name, width, codes_tag=None):
             grouped = keep.tile([P, width, PACK], BF16, name=name + "_grouped", align_bytes=64)
-            codes = keep.tile([P, width], U32, name=name + "_codes", align_bytes=64)
+            codes = keep.tile([P, width], U32, name=name + "_codes", tag=codes_tag or name + "_codes", align_bytes=64)
             scales = keep.tile([P, width], U8, name=name + "_scales", align_bytes=64)
             return grouped, codes, scales
 
@@ -56,56 +56,87 @@ def tile_attend_gds_sq_kernel(tc, xT, wT, vT, wt, xm, offs, out):
             )
 
         offsets = keep.tile([P, N // LIST_ROWS], U16, name="offsets")
-        nc.sync.dma_start(offsets[:], offs)
-
         v_rows = vT.rearrange("(p j) t -> p j t", j=PACK)
         w_rows = wT.rearrange("(p j) t -> p j t", j=PACK)
         x_rows = xT[0].rearrange("(p j) r -> p j r", j=PACK)
         xm_rows = xm[0].rearrange("(h p j) d -> h p j d", p=P, j=PACK)
 
         v_planes = [keep.tile([P, T], F32, name=f"v_plane{j}") for j in range(PACK)]
-        w_planes = [keep.tile([P, T], F32, name=f"w_plane{j}") for j in range(PACK)]
-        x_pieces = [(0, 0, P), (1, 0, P // 2), (1, P // 2, P)]
-        x_raw = [keep.tile([P, PACK, PACK * (m1 - m0)], F32, name=f"x_raw{h}_{m0}") for h, m0, m1 in x_pieces]
+        w_planes = [keep.tile([P, T], F32, name=f"w_plane{j}", tag=f"w_plane{j}", align_bytes=64) for j in range(PACK)]
+        x_raw = keep.tile([P, PACK, R], F32, name="x_raw")
         xm_raw = [keep.tile([P, PACK, D], F32, name=f"xm_raw{h}") for h in range(ROW_PASSES)]
         weights = keep.tile([P, ROW_PASSES, PACK], F32, name="weights")
 
-        def load_x(k):
-            h, m0, m1 = x_pieces[k]
-            nc.sync.dma_start(x_raw[k][:], x_rows[:, :, h * K_PASS + PACK * m0 : h * K_PASS + PACK * m1])
-
+        nc.scalar.dma_start(weights[:], wt[0].rearrange("(h p t) o -> p h (t o)", p=P, t=PACK))
+        nc.sync.dma_start(x_raw[:], x_rows)
+        nc.sync.dma_start(offsets[:], offs)
         for j in range(PACK):
             nc.sync.dma_start(v_planes[j][:], v_rows[:, j, :])
-        nc.sync.dma_start(weights[:], wt[0].rearrange("(h p t) o -> p h (t o)", p=P, t=PACK))
-        load_x(0)
         for j in range(PACK):
             nc.sync.dma_start(w_planes[j][:], w_rows[:, j, :])
-        load_x(1)
-        load_x(2)
         for h in range(ROW_PASSES):
             nc.sync.dma_start(xm_raw[h][:], xm_rows[h])
 
         windows = [keep.tile([P, T], F32, name=f"window{b}") for b in range(BLOCKS)]
-
-        v_op = operand("v", N)
+        v_op = operand("v", N, "w_plane1")
         w_op = operand("w", N)
         x_ops = [operand(f"x{h}", K_PASS) for h in range(ROW_PASSES)]
-        xm_ops = [operand(f"xm{h}", D) for h in range(ROW_PASSES)]
         g_ops = [operand(f"g{h}", N) for h in range(ROW_PASSES)]
+        xm_ops = [operand(f"xm{b}", ROW_PASSES * P) for b in range(2)]
+        half = N // 2
 
-        def group_x(k):
-            h, m0, m1 = x_pieces[k]
-            nc.scalar.copy(
-                out=x_ops[h][0][:].rearrange("p (t m) j -> p m j t", t=PACK)[:, m0:m1],
-                in_=x_raw[k][:].rearrange("p j (m t) -> p m j t", t=PACK),
+        def group_xm(b, passes=range(ROW_PASSES)):
+            for h in passes:
+                nc.scalar.copy(
+                    out=xm_ops[b][0][:, h * P : (h + 1) * P, :].rearrange("p (c i) j -> p c j i", i=PACK),
+                    in_=xm_raw[h][:, :, b * P : (b + 1) * P].rearrange("p j (c i) -> p c j i", i=PACK),
+                )
+
+        direct = [
+            [psum.tile([P, PACK, P], F32, name=f"direct{h}_{c}", tag=f"bank{4 * h + c}") for c in range(2)]
+            for h in range(ROW_PASSES)
+        ]
+        paired = [
+            [psum.tile([P, 2, half], F32, name=f"paired{h}_{u}", tag=f"bank{4 * h + 2 + u}") for u in range(2)]
+            for h in range(ROW_PASSES)
+        ]
+        g_planes = [keep.tile([P, PACK, half], BF16, name=f"g_planes{h}") for h in range(ROW_PASSES)]
+
+        def score_passes(table, first):
+            for h in range(ROW_PASSES):
+                banks = [(direct[h][c], range(PACK), c * P, (c + 1) * P) for c in range(2)]
+                banks += [(paired[h][u], (2 * u, 2 * u + 1), half, N) for u in range(2)]
+                for bank, ts, c0, c1 in banks:
+                    for e, t in enumerate(ts):
+                        matmul(bank[:, e, :], x_ops[h], t * P, table, c0, c1, E4M3,
+                               first and e == 0, (not first) and e == len(ts) - 1)
+
+        def weigh_direct(h, c):
+            nc.vector.tensor_tensor(
+                g_ops[h][0][:, c * P : (c + 1) * P, :],
+                direct[h][c][:].rearrange("p t i -> p i t"),
+                weights[:, h : h + 1, :].to_broadcast([P, P, PACK]),
+                MULT,
             )
 
-        def group_xm(h, b):
-            cols = slice(b * P, (b + 1) * P)
-            nc.scalar.copy(
-                out=xm_ops[h][0][:, cols, :].rearrange("p (c i) j -> p c j i", i=PACK),
-                in_=xm_raw[h][:, :, cols].rearrange("p j (c i) -> p c j i", i=PACK),
+        def weigh_paired(h):
+            for t in range(PACK):
+                nc.scalar.activation(
+                    out=g_planes[h][:, t, :], in_=paired[h][t // 2][:, t % 2, :], func=COPY, scale=weights[:, h, t : t + 1]
+                )
+
+        def group_g(h):
+            nc.vector.tensor_copy(
+                out=g_ops[h][0][:, half:N, :].rearrange("p (c i) t -> p c t i", i=PACK),
+                in_=g_planes[h][:].rearrange("p t (c i) -> p c t i", i=PACK),
             )
+
+        for h in range(ROW_PASSES):
+            nc.scalar.copy(
+                out=x_ops[h][0][:].rearrange("p (t m) j -> p m j t", t=PACK),
+                in_=x_raw[:, :, h * K_PASS : (h + 1) * K_PASS].rearrange("p j (m t) -> p m j t", t=PACK),
+            )
+            quantize(x_ops[h], 0, K_PASS, E4M3)
 
         v_picked = keep.tile([P, PACK, N], F32, name="v_picked")
         for j in range(PACK):
@@ -116,77 +147,61 @@ def tile_attend_gds_sq_kernel(tc, xT, wT, vT, wt, xm, offs, out):
             func=COPY,
             scale=-1.0,
         )
-        group_x(0)
-        quantize(v_op, 0, N, E4M3)
-        quantize(x_ops[0], 0, K_PASS, E4M3)
 
-        score = [
-            [psum.tile([P, PACK, P], F32, name=f"score{h}_{c}", tag=f"bank{QUARTERS * h + c}") for c in range(QUARTERS)]
-            for h in range(ROW_PASSES)
-        ]
-
-        def score_passes(h, c, table, first):
-            for t in range(PACK):
-                matmul(score[h][c][:, t, :], x_ops[h], t * P, table, c * P, (c + 1) * P, E4M3,
-                       first and t == 0, (not first) and t == PACK - 1)
-
-        def weigh(h, c):
-            nc.vector.tensor_tensor(
-                g_ops[h][0][:, c * P : (c + 1) * P, :],
-                score[h][c][:].rearrange("p t i -> p i t"),
-                weights[:, h : h + 1, :].to_broadcast([P, P, PACK]),
-                MULT,
-            )
-
-        for c in range(QUARTERS):
-            score_passes(0, c, v_op, True)
-
-        for j in range(PACK - 1):
+        for j in range(PACK):
+            if j == 2:
+                quantize(v_op, 0, N, E4M3)
+                score_passes(v_op, True)
             nc.vector.tensor_copy(w_op[0][:, :, j], w_planes[j][:].indirect(offsets[:]))
-        half = N // 2
-        for u in range(2):
-            lst = offsets[:, u * half // LIST_ROWS : (u + 1) * half // LIST_ROWS]
-            nc.vector.tensor_copy(w_op[0][:, u * half : (u + 1) * half, PACK - 1], w_planes[PACK - 1][:].indirect(lst))
         for u in range(2):
             quantize(w_op, u * half, (u + 1) * half, E4M3)
-        group_x(1)
-        group_x(2)
+        score_passes(w_op, False)
 
-        for c in range(QUARTERS):
-            score_passes(0, c, w_op, False)
-        quantize(x_ops[1], 0, K_PASS, E4M3)
-        for c in range(QUARTERS):
-            weigh(0, c)
-        for c in range(QUARTERS):
-            score_passes(1, c, v_op, True)
-            score_passes(1, c, w_op, False)
-        quantize(g_ops[0], 0, N, E5M2)
-        for b in range(BLOCKS):
-            for h in range(ROW_PASSES):
-                group_xm(h, b)
-        for c in range(QUARTERS):
-            weigh(1, c)
-            if c > 0:
-                quantize(g_ops[1], (c - 1) * P, c * P, E5M2)
+        group_xm(0, [0])
         for h in range(ROW_PASSES):
-            quantize(xm_ops[h], 0, P, E4M3)
-        quantize(g_ops[1], N - P, N, E5M2)
+            weigh_paired(h)
+            for c in range(2):
+                weigh_direct(h, c)
+        group_xm(0, [1])
+        group_xm(1)
+        group_g(0)
+        quantize(g_ops[0], 0, half, E5M2)
+        quantize(xm_ops[0], 0, P, E4M3)
+        quantize(g_ops[0], half, N, E5M2)
+        quantize(g_ops[1], 0, half, E5M2)
+        group_g(1)
+        quantize(xm_ops[0], P, 2 * P, E4M3)
+        quantize(g_ops[1], half, N, E5M2)
 
         for b in range(BLOCKS):
             nc.vector.memset(windows[b][:], 0.0)
-        for b in range(BLOCKS):
-            if b > 0:
-                for h in range(ROW_PASSES):
-                    quantize(xm_ops[h], b * P, (b + 1) * P, E4M3)
-            acc = psum.tile([P, N], F32, name=f"grad{b}", tag=f"bank{b}")
+
+        def product(b, pieces):
+            acc = psum.tile([P, N], F32, name=f"grad{b}", tag="bank0")
             for h in range(ROW_PASSES):
-                matmul(acc[:], xm_ops[h], b * P, g_ops[h], 0, N, E5M2, h == 0, h == ROW_PASSES - 1)
-            grad = keep.tile([P, N], F32, name=f"grad_sb{b}")
-            pieces = 2 if b == 0 else 1
+                matmul(acc[:], xm_ops[b], h * P, g_ops[h], 0, N, E5M2, h == 0, h == ROW_PASSES - 1)
             width = N // pieces
+            staged = []
             for u in range(pieces):
-                nc.scalar.copy(out=grad[:, u * width : (u + 1) * width], in_=acc[:, u * width : (u + 1) * width])
-            for u in range(pieces):
-                lst = offsets[:, u * width // LIST_ROWS : (u + 1) * width // LIST_ROWS]
-                nc.vector.tensor_copy(windows[b][:].indirect(lst), grad[:, u * width : (u + 1) * width])
+                grad = keep.tile([P, width], F32, name=f"grad_sb{b}_{u}", tag=f"grad_sb{b}_{u}", align_bytes=64)
+                nc.scalar.copy(out=grad[:], in_=acc[:, u * width : (u + 1) * width])
+                staged.append((grad, offsets[:, u * width // LIST_ROWS : (u + 1) * width // LIST_ROWS]))
+            return staged
+
+        staged = [product(0, 2)]
+        quantize(xm_ops[1], 0, ROW_PASSES * P, E4M3)
+        late = keep.tile([P, 2, ROW_PASSES * P, PACK], BF16, name="xm_late", tag="grad_sb0_0", align_bytes=64)
+        for b in range(2, BLOCKS):
+            codes = keep.tile([P, ROW_PASSES * P], U32, name=f"xm{b}_codes", align_bytes=64)
+            scales = keep.tile([P, ROW_PASSES * P], U8, name=f"xm{b}_scales", align_bytes=64)
+            xm_ops.append((late[:, b - 2], codes, scales))
+
+        for b in range(BLOCKS):
+            for grad, lst in staged[b]:
+                nc.vector.tensor_copy(windows[b][:].indirect(lst), grad[:])
             nc.sync.dma_start(out[b * P : (b + 1) * P, :], windows[b][:])
+            if b + 2 < BLOCKS:
+                group_xm(b + 2)
+                quantize(xm_ops[b + 2], 0, ROW_PASSES * P, E4M3)
+            if b + 1 < BLOCKS:
+                staged.append(product(b + 1, 1))

@@ -64,7 +64,8 @@ def tile_attend_gds_sq_kernel(tc, xT, wT, vT, wt, xm, offs, out):
         v_planes = [keep.tile([P, T], F32, name=f"v_plane{j}") for j in range(PACK)]
         w_planes = [keep.tile([P, T], F32, name=f"w_plane{j}", tag=f"w_plane{j}", align_bytes=64) for j in range(PACK)]
         x_raw = keep.tile([P, PACK, R], F32, name="x_raw")
-        xm_raw = [keep.tile([P, PACK, D], F32, name=f"xm_raw{h}") for h in range(ROW_PASSES)]
+        xm_head = [keep.tile([P, PACK, P], F32, name=f"xm_head{h}") for h in range(ROW_PASSES)]
+        xm_rest = [keep.tile([P, PACK, D - P], F32, name=f"xm_rest{h}") for h in range(ROW_PASSES)]
         weights = keep.tile([P, ROW_PASSES, PACK], F32, name="weights")
 
         nc.scalar.dma_start(weights[:], wt[0].rearrange("(h p t) o -> p h (t o)", p=P, t=PACK))
@@ -75,21 +76,32 @@ def tile_attend_gds_sq_kernel(tc, xT, wT, vT, wt, xm, offs, out):
         for j in range(PACK):
             nc.sync.dma_start(w_planes[j][:], w_rows[:, j, :])
         for h in range(ROW_PASSES):
-            nc.sync.dma_start(xm_raw[h][:], xm_rows[h])
+            nc.sync.dma_start(xm_head[h][:], xm_rows[h][:, :, 0:P])
+        for h in range(ROW_PASSES):
+            nc.sync.dma_start(xm_rest[h][:], xm_rows[h][:, :, P:D])
 
         windows = [keep.tile([P, T], F32, name=f"window{b}") for b in range(BLOCKS)]
         v_op = operand("v", N, "w_plane1")
         w_op = operand("w", N)
         x_ops = [operand(f"x{h}", K_PASS) for h in range(ROW_PASSES)]
-        g_ops = [operand(f"g{h}", N) for h in range(ROW_PASSES)]
-        xm_ops = [operand(f"xm{b}", ROW_PASSES * P) for b in range(2)]
+        xm_ops = [operand(f"xm{b}", ROW_PASSES * P) for b in range(BLOCKS)]
         half = N // 2
+        g_ops, g_early = [], []
+        for h in range(ROW_PASSES):
+            grouped = keep.tile([P, N, PACK], BF16, name=f"g{h}_grouped", align_bytes=64)
+            codes = keep.tile([P, half + N], U32, name=f"g{h}_codes", align_bytes=64)
+            scales = keep.tile([P, half + N], U8, name=f"g{h}_scales", align_bytes=64)
+            nc.vector.memset(codes[:, 0:half], 0)
+            nc.vector.memset(scales[:, 0:half], 0)
+            g_ops.append((grouped, codes[:, half:], scales[:, half:]))
+            g_early.append((grouped, codes[:, 0:N], scales[:, 0:N]))
 
-        def group_xm(b, passes=range(ROW_PASSES)):
-            for h in passes:
+        def group_xm(b):
+            for h in range(ROW_PASSES):
+                raw = xm_head[h][:] if b == 0 else xm_rest[h][:, :, (b - 1) * P : b * P]
                 nc.scalar.copy(
                     out=xm_ops[b][0][:, h * P : (h + 1) * P, :].rearrange("p (c i) j -> p c j i", i=PACK),
-                    in_=xm_raw[h][:, :, b * P : (b + 1) * P].rearrange("p j (c i) -> p c j i", i=PACK),
+                    in_=raw.rearrange("p j (c i) -> p c j i", i=PACK),
                 )
 
         direct = [
@@ -157,51 +169,44 @@ def tile_attend_gds_sq_kernel(tc, xT, wT, vT, wt, xm, offs, out):
             quantize(w_op, u * half, (u + 1) * half, E4M3)
         score_passes(w_op, False)
 
-        group_xm(0, [0])
+        for b in range(BLOCKS):
+            nc.vector.memset(windows[b][:], 0.0)
+
+        def product(name, bank, b, g, c0, c1):
+            acc = psum.tile([P, N], F32, name=name, tag=f"bank{bank}")
+            for h in range(ROW_PASSES):
+                matmul(acc[:], xm_ops[b], h * P, g[h], 0, N, E5M2, h == 0, h == ROW_PASSES - 1)
+            grad = keep.tile([P, c1 - c0], F32, name=name + "_sb")
+            nc.scalar.copy(out=grad[:], in_=acc[:, c0:c1])
+            return grad
+
+        def scatter(b, grad, s0, s1):
+            nc.vector.tensor_copy(windows[b][:].indirect(offsets[:, s0 // LIST_ROWS : s1 // LIST_ROWS]), grad[:])
+
+        group_xm(0)
         for h in range(ROW_PASSES):
             weigh_paired(h)
             for c in range(2):
                 weigh_direct(h, c)
-        group_xm(0, [1])
-        group_xm(1)
-        group_g(0)
         quantize(g_ops[0], 0, half, E5M2)
         quantize(xm_ops[0], 0, P, E4M3)
-        quantize(g_ops[0], half, N, E5M2)
         quantize(g_ops[1], 0, half, E5M2)
-        group_g(1)
         quantize(xm_ops[0], P, 2 * P, E4M3)
-        quantize(g_ops[1], half, N, E5M2)
-
+        first_half = product("grad0_first", 0, 0, g_early, half, N)
+        for h in range(ROW_PASSES):
+            group_g(h)
+        for h in range(ROW_PASSES):
+            quantize(g_ops[h], half, N, E5M2)
+        group_xm(1)
+        grad = product("grad0_second", 1, 0, g_ops, half, N)
+        scatter(0, first_half, 0, half)
         for b in range(BLOCKS):
-            nc.vector.memset(windows[b][:], 0.0)
-
-        def product(b, pieces):
-            acc = psum.tile([P, N], F32, name=f"grad{b}", tag="bank0")
-            for h in range(ROW_PASSES):
-                matmul(acc[:], xm_ops[b], h * P, g_ops[h], 0, N, E5M2, h == 0, h == ROW_PASSES - 1)
-            width = N // pieces
-            staged = []
-            for u in range(pieces):
-                grad = keep.tile([P, width], F32, name=f"grad_sb{b}_{u}", tag=f"grad_sb{b}_{u}", align_bytes=64)
-                nc.scalar.copy(out=grad[:], in_=acc[:, u * width : (u + 1) * width])
-                staged.append((grad, offsets[:, u * width // LIST_ROWS : (u + 1) * width // LIST_ROWS]))
-            return staged
-
-        staged = [product(0, 2)]
-        quantize(xm_ops[1], 0, ROW_PASSES * P, E4M3)
-        late = keep.tile([P, 2, ROW_PASSES * P, PACK], BF16, name="xm_late", tag="grad_sb0_0", align_bytes=64)
-        for b in range(2, BLOCKS):
-            codes = keep.tile([P, ROW_PASSES * P], U32, name=f"xm{b}_codes", align_bytes=64)
-            scales = keep.tile([P, ROW_PASSES * P], U8, name=f"xm{b}_scales", align_bytes=64)
-            xm_ops.append((late[:, b - 2], codes, scales))
-
-        for b in range(BLOCKS):
-            for grad, lst in staged[b]:
-                nc.vector.tensor_copy(windows[b][:].indirect(lst), grad[:])
-            nc.sync.dma_start(out[b * P : (b + 1) * P, :], windows[b][:])
-            if b + 2 < BLOCKS:
-                group_xm(b + 2)
-                quantize(xm_ops[b + 2], 0, ROW_PASSES * P, E4M3)
+            following = None
             if b + 1 < BLOCKS:
-                staged.append(product(b + 1, 1))
+                quantize(xm_ops[b + 1], 0, ROW_PASSES * P, E4M3)
+                if b + 2 < BLOCKS:
+                    group_xm(b + 2)
+                following = product(f"grad{b + 1}", b % 2, b + 1, g_ops, 0, N)
+            scatter(b, grad, half if b == 0 else 0, N)
+            nc.sync.dma_start(out[b * P : (b + 1) * P, :], windows[b][:])
+            grad = following

@@ -30,8 +30,8 @@ def tile_attend_gds_sq_kernel(tc, xT, wT, vT, wt, xm, offs, out):
         keep = ctx.enter_context(tc.tile_pool(name="keep", bufs=1))
         psum = ctx.enter_context(tc.psum_pool(name="psum", bufs=1))
 
-        def operand(name, width, codes_tag=None):
-            grouped = keep.tile([P, width, PACK], BF16, name=name + "_grouped", align_bytes=64)
+        def operand(name, width, codes_tag=None, grouped_tag=None):
+            grouped = keep.tile([P, width, PACK], BF16, name=name + "_grouped", tag=grouped_tag or name + "_grouped", align_bytes=64)
             codes = keep.tile([P, width], U32, name=name + "_codes", tag=codes_tag or name + "_codes", align_bytes=64)
             scales = keep.tile([P, width], U8, name=name + "_scales", align_bytes=64)
             return grouped, codes, scales
@@ -61,44 +61,44 @@ def tile_attend_gds_sq_kernel(tc, xT, wT, vT, wt, xm, offs, out):
         x_rows = xT[0].rearrange("(p j) r -> p j r", j=PACK)
         xm_rows = xm[0].rearrange("(h p j) d -> h p j d", p=P, j=PACK)
 
-        v_planes = [keep.tile([P, T], F32, name=f"v_plane{j}") for j in range(PACK)]
+        v_pairs = [keep.tile([P, 2, T], F32, name=f"v_pair{u}") for u in range(2)]
         w_planes = [keep.tile([P, T], F32, name=f"w_plane{j}", tag=f"w_plane{j}", align_bytes=64) for j in range(PACK)]
         x_raw = keep.tile([P, PACK, R], F32, name="x_raw")
-        xm_head = [keep.tile([P, PACK, P], F32, name=f"xm_head{h}") for h in range(ROW_PASSES)]
-        xm_rest = [keep.tile([P, PACK, D - P], F32, name=f"xm_rest{h}") for h in range(ROW_PASSES)]
+        xm_cuts = ((0, P), (P, 2 * P), (2 * P, D))
+        xm_raw = [
+            [keep.tile([P, PACK, d1 - d0], F32, name=f"xm_raw{d0}_{h}") for h in range(ROW_PASSES)] for d0, d1 in xm_cuts
+        ]
         weights = keep.tile([P, ROW_PASSES, PACK], F32, name="weights")
 
         nc.scalar.dma_start(weights[:], wt[0].rearrange("(h p t) o -> p h (t o)", p=P, t=PACK))
         nc.sync.dma_start(x_raw[:], x_rows)
         nc.sync.dma_start(offsets[:], offs)
-        for j in range(PACK):
-            nc.sync.dma_start(v_planes[j][:], v_rows[:, j, :])
+        for u in range(2):
+            nc.sync.dma_start(v_pairs[u][:], v_rows[:, 2 * u : 2 * u + 2, :])
         for j in range(PACK):
             nc.sync.dma_start(w_planes[j][:], w_rows[:, j, :])
-        for h in range(ROW_PASSES):
-            nc.sync.dma_start(xm_head[h][:], xm_rows[h][:, :, 0:P])
-        for h in range(ROW_PASSES):
-            nc.sync.dma_start(xm_rest[h][:], xm_rows[h][:, :, P:D])
+        for s, (d0, d1) in enumerate(xm_cuts):
+            for h in range(ROW_PASSES):
+                nc.sync.dma_start(xm_raw[s][h][:], xm_rows[h][:, :, d0:d1])
 
         windows = [keep.tile([P, T], F32, name=f"window{b}") for b in range(BLOCKS)]
         v_op = operand("v", N, "w_plane1")
         w_op = operand("w", N)
         x_ops = [operand(f"x{h}", K_PASS) for h in range(ROW_PASSES)]
-        xm_ops = [operand(f"xm{b}", ROW_PASSES * P) for b in range(BLOCKS)]
+        xm_ops = [operand(f"xm{b}", ROW_PASSES * P) for b in range(2)]
         half = N // 2
         g_ops, g_early = [], []
         for h in range(ROW_PASSES):
-            grouped = keep.tile([P, N, PACK], BF16, name=f"g{h}_grouped", align_bytes=64)
             codes = keep.tile([P, half + N], U32, name=f"g{h}_codes", align_bytes=64)
             scales = keep.tile([P, half + N], U8, name=f"g{h}_scales", align_bytes=64)
             nc.vector.memset(codes[:, 0:half], 0)
             nc.vector.memset(scales[:, 0:half], 0)
-            g_ops.append((grouped, codes[:, half:], scales[:, half:]))
-            g_early.append((grouped, codes[:, 0:N], scales[:, 0:N]))
+            g_ops.append((None, codes[:, half:], scales[:, half:]))
+            g_early.append((None, codes[:, 0:N], scales[:, 0:N]))
 
         def group_xm(b):
             for h in range(ROW_PASSES):
-                raw = xm_head[h][:] if b == 0 else xm_rest[h][:, :, (b - 1) * P : b * P]
+                raw = xm_raw[b][h][:] if b < 2 else xm_raw[2][h][:, :, (b - 2) * P : (b - 1) * P]
                 nc.scalar.copy(
                     out=xm_ops[b][0][:, h * P : (h + 1) * P, :].rearrange("p (c i) j -> p c j i", i=PACK),
                     in_=raw.rearrange("p j (c i) -> p c j i", i=PACK),
@@ -112,7 +112,8 @@ def tile_attend_gds_sq_kernel(tc, xT, wT, vT, wt, xm, offs, out):
             [psum.tile([P, 2, half], F32, name=f"paired{h}_{u}", tag=f"bank{4 * h + 2 + u}") for u in range(2)]
             for h in range(ROW_PASSES)
         ]
-        g_planes = [keep.tile([P, PACK, half], BF16, name=f"g_planes{h}") for h in range(ROW_PASSES)]
+        g_planes = [keep.tile([P, PACK, half], BF16, name=f"g_planes{h}", align_bytes=64) for h in range(ROW_PASSES)]
+        g_first = [keep.tile([P, half, PACK], BF16, name=f"g{h}_first", align_bytes=64) for h in range(ROW_PASSES)]
 
         def score_passes(table, first):
             for h in range(ROW_PASSES):
@@ -125,7 +126,7 @@ def tile_attend_gds_sq_kernel(tc, xT, wT, vT, wt, xm, offs, out):
 
         def weigh_direct(h, c):
             nc.vector.tensor_tensor(
-                g_ops[h][0][:, c * P : (c + 1) * P, :],
+                g_first[h][:, c * P : (c + 1) * P, :],
                 direct[h][c][:].rearrange("p t i -> p i t"),
                 weights[:, h : h + 1, :].to_broadcast([P, P, PACK]),
                 MULT,
@@ -137,10 +138,19 @@ def tile_attend_gds_sq_kernel(tc, xT, wT, vT, wt, xm, offs, out):
                     out=g_planes[h][:, t, :], in_=paired[h][t // 2][:, t % 2, :], func=COPY, scale=weights[:, h, t : t + 1]
                 )
 
-        def group_g(h):
-            nc.vector.tensor_copy(
-                out=g_ops[h][0][:, half:N, :].rearrange("p (c i) t -> p c t i", i=PACK),
+        def group_g(h, copy):
+            grouped = keep.tile([P, half, PACK], BF16, name=f"g{h}_second", tag="g_second", align_bytes=64)
+            copy(
+                out=grouped[:].rearrange("p (c i) t -> p c t i", i=PACK),
                 in_=g_planes[h][:].rearrange("p t (c i) -> p c t i", i=PACK),
+            )
+            return grouped
+
+        def quantize_g(h, grouped, c0):
+            nc.vector.quantize_mx(
+                out=g_ops[h][1][:, c0 : c0 + half].bitcast(E5M2),
+                scales=g_ops[h][2][:, c0 : c0 + half],
+                in_=grouped[:].rearrange("p w j -> p (w j)"),
             )
 
         for h in range(ROW_PASSES):
@@ -152,7 +162,7 @@ def tile_attend_gds_sq_kernel(tc, xT, wT, vT, wt, xm, offs, out):
 
         v_picked = keep.tile([P, PACK, N], F32, name="v_picked")
         for j in range(PACK):
-            nc.vector.tensor_copy(v_picked[:, j, :], v_planes[j][:].indirect(offsets[:]))
+            nc.vector.tensor_copy(v_picked[:, j, :], v_pairs[j // 2][:, j % 2, :].indirect(offsets[:]))
         nc.scalar.activation(
             out=v_op[0][:].rearrange("p (c i) j -> p c j i", i=PACK),
             in_=v_picked[:].rearrange("p j (c i) -> p c j i", i=PACK),
@@ -164,7 +174,10 @@ def tile_attend_gds_sq_kernel(tc, xT, wT, vT, wt, xm, offs, out):
             if j == 2:
                 quantize(v_op, 0, N, E4M3)
                 score_passes(v_op, True)
-            nc.vector.tensor_copy(w_op[0][:, :, j], w_planes[j][:].indirect(offsets[:]))
+            for s0, s1 in ((0, N),) if j < PACK - 1 else ((0, half), (half, N)):
+                nc.vector.tensor_copy(
+                    w_op[0][:, s0:s1, j], w_planes[j][:].indirect(offsets[:, s0 // LIST_ROWS : s1 // LIST_ROWS])
+                )
         for u in range(2):
             quantize(w_op, u * half, (u + 1) * half, E4M3)
         score_passes(w_op, False)
@@ -172,11 +185,11 @@ def tile_attend_gds_sq_kernel(tc, xT, wT, vT, wt, xm, offs, out):
         for b in range(BLOCKS):
             nc.vector.memset(windows[b][:], 0.0)
 
-        def product(name, bank, b, g, c0, c1):
+        def product(name, bank, b, g, c0, c1, tag=None):
             acc = psum.tile([P, N], F32, name=name, tag=f"bank{bank}")
             for h in range(ROW_PASSES):
                 matmul(acc[:], xm_ops[b], h * P, g[h], 0, N, E5M2, h == 0, h == ROW_PASSES - 1)
-            grad = keep.tile([P, c1 - c0], F32, name=name + "_sb")
+            grad = keep.tile([P, c1 - c0], F32, name=name + "_sb", tag=tag or name + "_sb", align_bytes=64)
             nc.scalar.copy(out=grad[:], in_=acc[:, c0:c1])
             return grad
 
@@ -184,29 +197,34 @@ def tile_attend_gds_sq_kernel(tc, xT, wT, vT, wt, xm, offs, out):
             nc.vector.tensor_copy(windows[b][:].indirect(offsets[:, s0 // LIST_ROWS : s1 // LIST_ROWS]), grad[:])
 
         group_xm(0)
+        group_xm(1)
         for h in range(ROW_PASSES):
             weigh_paired(h)
             for c in range(2):
                 weigh_direct(h, c)
-        quantize(g_ops[0], 0, half, E5M2)
         quantize(xm_ops[0], 0, P, E4M3)
-        quantize(g_ops[1], 0, half, E5M2)
+        quantize_g(0, g_first[0], 0)
         quantize(xm_ops[0], P, 2 * P, E4M3)
-        first_half = product("grad0_first", 0, 0, g_early, half, N)
-        for h in range(ROW_PASSES):
-            group_g(h)
-        for h in range(ROW_PASSES):
-            quantize(g_ops[h], half, N, E5M2)
-        group_xm(1)
-        grad = product("grad0_second", 1, 0, g_ops, half, N)
-        scatter(0, first_half, 0, half)
-        for b in range(BLOCKS):
-            following = None
-            if b + 1 < BLOCKS:
-                quantize(xm_ops[b + 1], 0, ROW_PASSES * P, E4M3)
-                if b + 2 < BLOCKS:
-                    group_xm(b + 2)
-                following = product(f"grad{b + 1}", b % 2, b + 1, g_ops, 0, N)
-            scatter(b, grad, half if b == 0 else 0, N)
+        quantize_g(1, g_first[1], 0)
+        early0 = product("grad0_first", 0, 0, g_early, half, N)
+        second0 = group_g(0, nc.vector.tensor_copy)
+        quantize(xm_ops[1], 0, 2 * P, E4M3)
+        quantize_g(0, second0, half)
+        second1 = group_g(1, nc.scalar.copy)
+        early1 = product("grad1_first", 1, 1, g_early, half, N, "g_planes1")
+        scatter(0, early0, 0, half)
+        quantize_g(1, second1, half)
+        scatter(1, early1, 0, half)
+        xm_ops.append(operand("xm2", ROW_PASSES * P, grouped_tag="g_second"))
+        group_xm(2)
+        quantize(xm_ops[2], 0, 2 * P, E4M3)
+        late0 = product("grad0_second", 4, 0, g_ops, half, N)
+        xm_ops.append(operand("xm3", ROW_PASSES * P, grouped_tag="g_second"))
+        group_xm(3)
+        quantize(xm_ops[3], 0, 2 * P, E4M3)
+        late1 = product("grad1_second", 5, 1, g_ops, half, N)
+        grad2 = product("grad2", 0, 2, g_ops, 0, N)
+        grad3 = product("grad3", 1, 3, g_ops, 0, N)
+        for b, grad, s0 in ((0, late0, half), (1, late1, half), (2, grad2, 0), (3, grad3, 0)):
+            scatter(b, grad, s0, N)
             nc.sync.dma_start(out[b * P : (b + 1) * P, :], windows[b][:])
-            grad = following

@@ -85,7 +85,8 @@ def tile_attend_gds_sq_kernel(tc, xT, wT, vT, wt, xm, offs, out):
         v_op = operand("v", N, "w_plane1")
         w_op = operand("w", N)
         x_ops = [operand(f"x{h}", K_PASS) for h in range(ROW_PASSES)]
-        xm_ops = [operand(f"xm{b}", ROW_PASSES * P) for b in range(2)]
+        xm_ops = [None, operand("xm1", ROW_PASSES * P)]
+        xm0_ops = [operand(f"xm0_{h}", P) for h in range(ROW_PASSES)]
         half = N // 2
         g_ops, g_early = [], []
         for h in range(ROW_PASSES):
@@ -100,7 +101,7 @@ def tile_attend_gds_sq_kernel(tc, xT, wT, vT, wt, xm, offs, out):
             for h in range(ROW_PASSES):
                 raw = xm_raw[b][h][:] if b < 2 else xm_raw[2][h][:, :, (b - 2) * P : (b - 1) * P]
                 nc.scalar.copy(
-                    out=xm_ops[b][0][:, h * P : (h + 1) * P, :].rearrange("p (c i) j -> p c j i", i=PACK),
+                    out=(xm_ops[b][0][:, h * P : (h + 1) * P, :] if b else xm0_ops[h][0][:]).rearrange("p (c i) j -> p c j i", i=PACK),
                     in_=raw.rearrange("p j (c i) -> p c j i", i=PACK),
                 )
 
@@ -113,7 +114,6 @@ def tile_attend_gds_sq_kernel(tc, xT, wT, vT, wt, xm, offs, out):
             for h in range(ROW_PASSES)
         ]
         g_planes = [keep.tile([P, PACK, half], BF16, name=f"g_planes{h}", align_bytes=64) for h in range(ROW_PASSES)]
-        g_first = [keep.tile([P, half, PACK], BF16, name=f"g{h}_first", align_bytes=64) for h in range(ROW_PASSES)]
 
         def score_passes(table, first):
             for h in range(ROW_PASSES):
@@ -138,8 +138,8 @@ def tile_attend_gds_sq_kernel(tc, xT, wT, vT, wt, xm, offs, out):
                     out=g_planes[h][:, t, :], in_=paired[h][t // 2][:, t % 2, :], func=COPY, scale=weights[:, h, t : t + 1]
                 )
 
-        def group_g(h, copy):
-            grouped = keep.tile([P, half, PACK], BF16, name=f"g{h}_second", tag="g_second", align_bytes=64)
+        def group_g(h, copy, tag):
+            grouped = keep.tile([P, half, PACK], BF16, name=f"g{h}_second", tag=tag, align_bytes=64)
             copy(
                 out=grouped[:].rearrange("p (c i) t -> p c t i", i=PACK),
                 in_=g_planes[h][:].rearrange("p t (c i) -> p c t i", i=PACK),
@@ -188,7 +188,8 @@ def tile_attend_gds_sq_kernel(tc, xT, wT, vT, wt, xm, offs, out):
         def product(name, bank, b, g, c0, c1, tag=None):
             acc = psum.tile([P, N], F32, name=name, tag=f"bank{bank}")
             for h in range(ROW_PASSES):
-                matmul(acc[:], xm_ops[b], h * P, g[h], 0, N, E5M2, h == 0, h == ROW_PASSES - 1)
+                lhs, l0 = (xm_ops[b], h * P) if b else (xm0_ops[h], 0)
+                matmul(acc[:], lhs, l0, g[h], 0, N, E5M2, h == 0, h == ROW_PASSES - 1)
             grad = keep.tile([P, c1 - c0], F32, name=name + "_sb", tag=tag or name + "_sb", align_bytes=64)
             nc.scalar.copy(out=grad[:], in_=acc[:, c0:c1])
             return grad
@@ -197,34 +198,38 @@ def tile_attend_gds_sq_kernel(tc, xT, wT, vT, wt, xm, offs, out):
             nc.vector.tensor_copy(windows[b][:].indirect(offsets[:, s0 // LIST_ROWS : s1 // LIST_ROWS]), grad[:])
 
         group_xm(0)
+        for h in range(ROW_PASSES):
+            quantize(xm0_ops[h], 0, P, E4M3)
+        g_first = [
+            keep.tile([P, half, PACK], BF16, name="g0_first", tag="xm0_0_grouped", align_bytes=64),
+            keep.tile([P, half, PACK], BF16, name="g1_first", align_bytes=64),
+        ]
         group_xm(1)
         for h in range(ROW_PASSES):
             weigh_paired(h)
             for c in range(2):
                 weigh_direct(h, c)
-        quantize(xm_ops[0], 0, P, E4M3)
         quantize_g(0, g_first[0], 0)
-        quantize(xm_ops[0], P, 2 * P, E4M3)
         quantize_g(1, g_first[1], 0)
         early0 = product("grad0_first", 0, 0, g_early, half, N)
-        second0 = group_g(0, nc.vector.tensor_copy)
+        second0 = group_g(0, nc.vector.tensor_copy, "g0_second")
         quantize(xm_ops[1], 0, 2 * P, E4M3)
         quantize_g(0, second0, half)
-        second1 = group_g(1, nc.scalar.copy)
-        early1 = product("grad1_first", 1, 1, g_early, half, N, "g_planes1")
+        second1 = group_g(1, nc.scalar.copy, "xm1_grouped")
+        early1 = product("grad1_first", 7, 1, g_early, half, N)
         scatter(0, early0, 0, half)
         quantize_g(1, second1, half)
         scatter(1, early1, 0, half)
-        xm_ops.append(operand("xm2", ROW_PASSES * P, grouped_tag="g_second"))
+        xm_ops.append(operand("xm2", ROW_PASSES * P, grouped_tag="g0_second"))
         group_xm(2)
         quantize(xm_ops[2], 0, 2 * P, E4M3)
-        late0 = product("grad0_second", 4, 0, g_ops, half, N)
-        xm_ops.append(operand("xm3", ROW_PASSES * P, grouped_tag="g_second"))
+        late0 = product("grad0_second", 0, 0, g_ops, half, N)
+        xm_ops.append(operand("xm3", ROW_PASSES * P, grouped_tag="grad0_first_sb"))
         group_xm(3)
         quantize(xm_ops[3], 0, 2 * P, E4M3)
-        late1 = product("grad1_second", 5, 1, g_ops, half, N)
-        grad2 = product("grad2", 0, 2, g_ops, 0, N)
-        grad3 = product("grad3", 1, 3, g_ops, 0, N)
+        late1 = product("grad1_second", 7, 1, g_ops, half, N)
+        grad2 = product("grad2", 4, 2, g_ops, 0, N)
+        grad3 = product("grad3", 5, 3, g_ops, 0, N)
         for b, grad, s0 in ((0, late0, half), (1, late1, half), (2, grad2, 0), (3, grad3, 0)):
             scatter(b, grad, s0, N)
             nc.sync.dma_start(out[b * P : (b + 1) * P, :], windows[b][:])

@@ -85,8 +85,7 @@ def tile_attend_gds_sq_kernel(tc, xT, wT, vT, wt, xm, offs, out):
         v_op = operand("v", N, "w_plane1")
         w_op = operand("w", N)
         x_ops = [operand(f"x{h}", K_PASS) for h in range(ROW_PASSES)]
-        xm_ops = [None, operand("xm1", ROW_PASSES * P)]
-        xm0_ops = [operand(f"xm0_{h}", P) for h in range(ROW_PASSES)]
+        xm_ops = [operand(f"xm{b}", ROW_PASSES * P) for b in range(2)]
         half = N // 2
         g_ops, g_early = [], []
         for h in range(ROW_PASSES):
@@ -101,7 +100,7 @@ def tile_attend_gds_sq_kernel(tc, xT, wT, vT, wt, xm, offs, out):
             for h in range(ROW_PASSES):
                 raw = xm_raw[b][h][:] if b < 2 else xm_raw[2][h][:, :, (b - 2) * P : (b - 1) * P]
                 nc.scalar.copy(
-                    out=(xm_ops[b][0][:, h * P : (h + 1) * P, :] if b else xm0_ops[h][0][:]).rearrange("p (c i) j -> p c j i", i=PACK),
+                    out=xm_ops[b][0][:, h * P : (h + 1) * P, :].rearrange("p (c i) j -> p c j i", i=PACK),
                     in_=raw.rearrange("p j (c i) -> p c j i", i=PACK),
                 )
 
@@ -114,6 +113,7 @@ def tile_attend_gds_sq_kernel(tc, xT, wT, vT, wt, xm, offs, out):
             for h in range(ROW_PASSES)
         ]
         g_planes = [keep.tile([P, PACK, half], BF16, name=f"g_planes{h}", align_bytes=64) for h in range(ROW_PASSES)]
+        g_first = [keep.tile([P, half, PACK], BF16, name=f"g{h}_first", align_bytes=64) for h in range(ROW_PASSES)]
 
         def score_passes(table, first):
             for h in range(ROW_PASSES):
@@ -188,8 +188,7 @@ def tile_attend_gds_sq_kernel(tc, xT, wT, vT, wt, xm, offs, out):
         def product(name, bank, b, g, c0, c1, tag=None):
             acc = psum.tile([P, N], F32, name=name, tag=f"bank{bank}")
             for h in range(ROW_PASSES):
-                lhs, l0 = (xm_ops[b], h * P) if b else (xm0_ops[h], 0)
-                matmul(acc[:], lhs, l0, g[h], 0, N, E5M2, h == 0, h == ROW_PASSES - 1)
+                matmul(acc[:], xm_ops[b], h * P, g[h], 0, N, E5M2, h == 0, h == ROW_PASSES - 1)
             grad = keep.tile([P, c1 - c0], F32, name=name + "_sb", tag=tag or name + "_sb", align_bytes=64)
             nc.scalar.copy(out=grad[:], in_=acc[:, c0:c1])
             return grad
@@ -198,18 +197,14 @@ def tile_attend_gds_sq_kernel(tc, xT, wT, vT, wt, xm, offs, out):
             nc.vector.tensor_copy(windows[b][:].indirect(offsets[:, s0 // LIST_ROWS : s1 // LIST_ROWS]), grad[:])
 
         group_xm(0)
-        for h in range(ROW_PASSES):
-            quantize(xm0_ops[h], 0, P, E4M3)
-        g_first = [
-            keep.tile([P, half, PACK], BF16, name="g0_first", tag="xm0_0_grouped", align_bytes=64),
-            keep.tile([P, half, PACK], BF16, name="g1_first", align_bytes=64),
-        ]
         group_xm(1)
         for h in range(ROW_PASSES):
             weigh_paired(h)
             for c in range(2):
                 weigh_direct(h, c)
+        quantize(xm_ops[0], 0, P, E4M3)
         quantize_g(0, g_first[0], 0)
+        quantize(xm_ops[0], P, 2 * P, E4M3)
         quantize_g(1, g_first[1], 0)
         early0 = product("grad0_first", 0, 0, g_early, half, N)
         second0 = group_g(0, nc.vector.tensor_copy, "g0_second")

@@ -66,7 +66,7 @@ def tile_attend_gds_sq_kernel(tc, xT, wT, vT, wt, xm, offs, out):
         x_raw = keep.tile([P, PACK, R], F32, name="x_raw")
         xm_cuts = ((0, P), (P, 2 * P), (2 * P, D))
         xm_raw = [
-            [keep.tile([P, PACK, d1 - d0], F32, name=f"xm_raw{d0}_{h}") for h in range(ROW_PASSES)] for d0, d1 in xm_cuts
+            [keep.tile([P, PACK, d1 - d0], F32, name=f"xm_raw{d0}_{h}", align_bytes=64) for h in range(ROW_PASSES)] for d0, d1 in xm_cuts
         ]
         weights = keep.tile([P, ROW_PASSES, PACK], F32, name="weights")
 
@@ -219,11 +219,11 @@ def tile_attend_gds_sq_kernel(tc, xT, wT, vT, wt, xm, offs, out):
         group_xm(2)
         quantize(xm_ops[2], 0, 2 * P, E4M3)
         late0 = product("grad0_second", 0, 0, g_ops, half, N)
-        xm_ops.append(operand("xm3", ROW_PASSES * P, grouped_tag="grad0_first_sb"))
+        xm_ops.append(operand("xm3", ROW_PASSES * P, grouped_tag="g0_second"))
         group_xm(3)
         quantize(xm_ops[3], 0, 2 * P, E4M3)
         late1 = product("grad1_second", 7, 1, g_ops, half, N)
-        grad2 = product("grad2", 4, 2, g_ops, 0, N)
+        grad2 = product("grad2", 4, 2, g_ops, 0, N, "xm_raw256_1")
         grad3 = product("grad3", 5, 3, g_ops, 0, N)
         for b, grad, s0 in ((0, late0, half), (1, late1, half), (2, grad2, 0), (3, grad3, 0)):
             scatter(b, grad, s0, N)

@@ -30,8 +30,9 @@ def tile_attend_gds_sq_kernel(tc, xT, wT, vT, wt, xm, offs, out):
         keep = ctx.enter_context(tc.tile_pool(name="keep", bufs=1))
         psum = ctx.enter_context(tc.psum_pool(name="psum", bufs=1))
 
-        def operand(name, width, codes_tag=None, grouped_tag=None):
-            grouped = keep.tile([P, width, PACK], BF16, name=name + "_grouped", tag=grouped_tag or name + "_grouped", align_bytes=64)
+        def operand(name, width, codes_tag=None, grouped_tag=None, grouped=None):
+            if grouped is None:
+                grouped = keep.tile([P, width, PACK], BF16, name=name + "_grouped", tag=grouped_tag or name + "_grouped", align_bytes=64)
             codes = keep.tile([P, width], U32, name=name + "_codes", tag=codes_tag or name + "_codes", align_bytes=64)
             scales = keep.tile([P, width], U8, name=name + "_scales", align_bytes=64)
             return grouped, codes, scales
@@ -63,7 +64,13 @@ def tile_attend_gds_sq_kernel(tc, xT, wT, vT, wt, xm, offs, out):
 
         v_pairs = [keep.tile([P, 2, T], F32, name=f"v_pair{u}") for u in range(2)]
         w_planes = [keep.tile([P, T], F32, name=f"w_plane{j}", tag=f"w_plane{j}", align_bytes=64) for j in range(PACK)]
-        x_raw = keep.tile([P, PACK, R], F32, name="x_raw")
+        half = N // 2
+        x_cut = K_PASS // 2
+        x0_raw = keep.tile([P, PACK, K_PASS], F32, name="x0_raw")
+        front = keep.tile([P, PACK * x_cut], F32, name="front", align_bytes=64)
+        x1_front = front[:].rearrange("p (j r) -> p j r", j=PACK)
+        shared = keep.tile([P, PACK * x_cut], F32, name="shared", align_bytes=64)
+        x1_back = shared[:].rearrange("p (j r) -> p j r", j=PACK)
         xm_cuts = ((0, P), (P, 2 * P), (2 * P, D))
         xm_raw = [
             [keep.tile([P, PACK, d1 - d0], F32, name=f"xm_raw{d0}_{h}", align_bytes=64) for h in range(ROW_PASSES)] for d0, d1 in xm_cuts
@@ -71,12 +78,14 @@ def tile_attend_gds_sq_kernel(tc, xT, wT, vT, wt, xm, offs, out):
         weights = keep.tile([P, ROW_PASSES, PACK], F32, name="weights")
 
         nc.scalar.dma_start(weights[:], wt[0].rearrange("(h p t) o -> p h (t o)", p=P, t=PACK))
-        nc.sync.dma_start(x_raw[:], x_rows)
+        nc.sync.dma_start(x0_raw[:], x_rows[:, :, 0:K_PASS])
         nc.sync.dma_start(offsets[:], offs)
         for u in range(2):
             nc.sync.dma_start(v_pairs[u][:], v_rows[:, 2 * u : 2 * u + 2, :])
         for j in range(PACK):
             nc.sync.dma_start(w_planes[j][:], w_rows[:, j, :])
+        nc.sync.dma_start(x1_front, x_rows[:, :, K_PASS : K_PASS + x_cut])
+        nc.sync.dma_start(x1_back, x_rows[:, :, K_PASS + x_cut :])
         for s, (d0, d1) in enumerate(xm_cuts):
             for h in range(ROW_PASSES):
                 nc.sync.dma_start(xm_raw[s][h][:], xm_rows[h][:, :, d0:d1])
@@ -85,8 +94,8 @@ def tile_attend_gds_sq_kernel(tc, xT, wT, vT, wt, xm, offs, out):
         v_op = operand("v", N, "w_plane1")
         w_op = operand("w", N)
         x_ops = [operand(f"x{h}", K_PASS) for h in range(ROW_PASSES)]
-        xm_ops = [operand(f"xm{b}", ROW_PASSES * P) for b in range(2)]
-        half = N // 2
+        late = keep.tile([P, 2 * half + ROW_PASSES * P * PACK], BF16, name="late", align_bytes=64)
+        xm_ops = [operand("xm0", ROW_PASSES * P), operand("xm1", ROW_PASSES * P, grouped=late[:, 2 * half :].rearrange("p (w j) -> p w j", j=PACK))]
         g_ops, g_early = [], []
         for h in range(ROW_PASSES):
             codes = keep.tile([P, half + N], U32, name=f"g{h}_codes", align_bytes=64)
@@ -96,13 +105,12 @@ def tile_attend_gds_sq_kernel(tc, xT, wT, vT, wt, xm, offs, out):
             g_ops.append((None, codes[:, half:], scales[:, half:]))
             g_early.append((None, codes[:, 0:N], scales[:, 0:N]))
 
-        def group_xm(b):
-            for h in range(ROW_PASSES):
-                raw = xm_raw[b][h][:] if b < 2 else xm_raw[2][h][:, :, (b - 2) * P : (b - 1) * P]
-                nc.scalar.copy(
-                    out=xm_ops[b][0][:, h * P : (h + 1) * P, :].rearrange("p (c i) j -> p c j i", i=PACK),
-                    in_=raw.rearrange("p j (c i) -> p c j i", i=PACK),
-                )
+        def group_xm(b, h):
+            raw = xm_raw[b][h][:] if b < 2 else xm_raw[2][h][:, :, (b - 2) * P : (b - 1) * P]
+            nc.scalar.copy(
+                out=xm_ops[b][0][:, h * P : (h + 1) * P, :].rearrange("p (c i) j -> p c j i", i=PACK),
+                in_=raw.rearrange("p j (c i) -> p c j i", i=PACK),
+            )
 
         direct = [
             [psum.tile([P, PACK, P], F32, name=f"direct{h}_{c}", tag=f"bank{4 * h + c}") for c in range(2)]
@@ -112,17 +120,19 @@ def tile_attend_gds_sq_kernel(tc, xT, wT, vT, wt, xm, offs, out):
             [psum.tile([P, 2, half], F32, name=f"paired{h}_{u}", tag=f"bank{4 * h + 2 + u}") for u in range(2)]
             for h in range(ROW_PASSES)
         ]
-        g_planes = [keep.tile([P, PACK, half], BF16, name=f"g_planes{h}", align_bytes=64) for h in range(ROW_PASSES)]
-        g_first = [keep.tile([P, half, PACK], BF16, name=f"g{h}_first", align_bytes=64) for h in range(ROW_PASSES)]
+        g0_planes = front[:, 0 : PACK * half // 2].bitcast(BF16).rearrange("p (t i) -> p t i", t=PACK)
+        g_planes = [g0_planes, late[:, 0 : PACK * half].rearrange("p (t i) -> p t i", t=PACK)]
+        g1_first = keep.tile([P, half, PACK], BF16, name="g1_first", align_bytes=64)
+        g_first = [shared[:, 0 : half * PACK // 2].bitcast(BF16).rearrange("p (w j) -> p w j", j=PACK), g1_first[:]]
 
-        def score_passes(table, first):
-            for h in range(ROW_PASSES):
-                banks = [(direct[h][c], range(PACK), c * P, (c + 1) * P) for c in range(2)]
-                banks += [(paired[h][u], (2 * u, 2 * u + 1), half, N) for u in range(2)]
-                for bank, ts, c0, c1 in banks:
-                    for e, t in enumerate(ts):
-                        matmul(bank[:, e, :], x_ops[h], t * P, table, c0, c1, E4M3,
-                               first and e == 0, (not first) and e == len(ts) - 1)
+        def score_passes(h, tables, start, stop):
+            early = [(direct[h][c], range(PACK), c * P, (c + 1) * P) for c in range(2)]
+            late = [(paired[h][u], (2 * u, 2 * u + 1), half, N) for u in range(2)]
+            banks = late + early if h == 0 else early + late
+            for bank, ts, c0, c1 in banks:
+                passes = [(e, t, table) for e, t in enumerate(ts) for table in tables]
+                for n, (e, t, table) in enumerate(passes):
+                    matmul(bank[:, e, :], x_ops[h], t * P, table, c0, c1, E4M3, start and n == 0, stop and n == len(passes) - 1)
 
         def weigh_direct(h, c):
             nc.vector.tensor_tensor(
@@ -138,27 +148,27 @@ def tile_attend_gds_sq_kernel(tc, xT, wT, vT, wt, xm, offs, out):
                     out=g_planes[h][:, t, :], in_=paired[h][t // 2][:, t % 2, :], func=COPY, scale=weights[:, h, t : t + 1]
                 )
 
-        def group_g(h, copy, tag):
-            grouped = keep.tile([P, half, PACK], BF16, name=f"g{h}_second", tag=tag, align_bytes=64)
+        def group_g(h, copy, grouped):
             copy(
-                out=grouped[:].rearrange("p (c i) t -> p c t i", i=PACK),
-                in_=g_planes[h][:].rearrange("p t (c i) -> p c t i", i=PACK),
+                out=grouped.rearrange("p (c i) t -> p c t i", i=PACK),
+                in_=g_planes[h].rearrange("p t (c i) -> p c t i", i=PACK),
             )
-            return grouped
 
         def quantize_g(h, grouped, c0):
             nc.vector.quantize_mx(
                 out=g_ops[h][1][:, c0 : c0 + half].bitcast(E5M2),
                 scales=g_ops[h][2][:, c0 : c0 + half],
-                in_=grouped[:].rearrange("p w j -> p (w j)"),
+                in_=grouped.rearrange("p w j -> p (w j)"),
             )
 
-        for h in range(ROW_PASSES):
-            nc.scalar.copy(
-                out=x_ops[h][0][:].rearrange("p (t m) j -> p m j t", t=PACK),
-                in_=x_raw[:, :, h * K_PASS : (h + 1) * K_PASS].rearrange("p j (m t) -> p m j t", t=PACK),
+        def group_x(copy, h, raw, m0, m1, t0, t1):
+            copy(
+                out=x_ops[h][0][:].rearrange("p (t m) j -> p m j t", t=PACK)[:, m0:m1, :, t0:t1],
+                in_=raw.rearrange("p j (m t) -> p m j t", t=PACK)[:, :, :, t0:t1],
             )
-            quantize(x_ops[h], 0, K_PASS, E4M3)
+
+        group_x(nc.scalar.copy, 0, x0_raw[:], 0, P, 0, PACK)
+        quantize(x_ops[0], 0, K_PASS, E4M3)
 
         v_picked = keep.tile([P, PACK, N], F32, name="v_picked")
         for j in range(PACK):
@@ -173,14 +183,14 @@ def tile_attend_gds_sq_kernel(tc, xT, wT, vT, wt, xm, offs, out):
         for j in range(PACK):
             if j == 2:
                 quantize(v_op, 0, N, E4M3)
-                score_passes(v_op, True)
-            for s0, s1 in ((0, N),) if j < PACK - 1 else ((0, half), (half, N)):
+                score_passes(0, [v_op], True, False)
+            for s0, s1 in ((0, N),) if j < PACK - 1 else ((half, N), (0, half)):
                 nc.vector.tensor_copy(
                     w_op[0][:, s0:s1, j], w_planes[j][:].indirect(offsets[:, s0 // LIST_ROWS : s1 // LIST_ROWS])
                 )
-        for u in range(2):
+        for u in (1, 0):
             quantize(w_op, u * half, (u + 1) * half, E4M3)
-        score_passes(w_op, False)
+        score_passes(0, [w_op], False, True)
 
         for b in range(BLOCKS):
             nc.vector.memset(windows[b][:], 0.0)
@@ -196,34 +206,45 @@ def tile_attend_gds_sq_kernel(tc, xT, wT, vT, wt, xm, offs, out):
         def scatter(b, grad, s0, s1):
             nc.vector.tensor_copy(windows[b][:].indirect(offsets[:, s0 // LIST_ROWS : s1 // LIST_ROWS]), grad[:])
 
-        group_xm(0)
-        group_xm(1)
+        group_x(nc.scalar.copy, 1, x1_front, 0, P // 2, 0, PACK)
+        for u in range(2):
+            group_x(nc.vector.tensor_copy, 1, x1_back, P // 2, P, 2 * u, 2 * u + 2)
+        for u in range(2):
+            quantize(x_ops[1], 2 * u * P, (2 * u + 2) * P, E4M3)
+        score_passes(1, [v_op, w_op], True, True)
+        weigh_paired(0)
+        group_xm(0, 0)
+        group_xm(0, 1)
+        group_xm(1, 0)
+        group_xm(1, 1)
         for h in range(ROW_PASSES):
-            weigh_paired(h)
             for c in range(2):
                 weigh_direct(h, c)
-        quantize(xm_ops[0], 0, P, E4M3)
         quantize_g(0, g_first[0], 0)
-        quantize(xm_ops[0], P, 2 * P, E4M3)
+        quantize(xm_ops[0], 0, 2 * P, E4M3)
         quantize_g(1, g_first[1], 0)
         early0 = product("grad0_first", 0, 0, g_early, half, N)
-        second0 = group_g(0, nc.vector.tensor_copy, "g0_second")
+        group_g(0, nc.vector.tensor_copy, g_first[0])
         quantize(xm_ops[1], 0, 2 * P, E4M3)
-        quantize_g(0, second0, half)
-        second1 = group_g(1, nc.scalar.copy, "xm1_grouped")
+        weigh_paired(1)
+        quantize_g(0, g_first[0], half)
+        second1 = keep.tile([P, half, PACK], BF16, name="g1_second", align_bytes=64)
+        group_g(1, nc.scalar.copy, second1[:])
         early1 = product("grad1_first", 7, 1, g_early, half, N)
         scatter(0, early0, 0, half)
-        quantize_g(1, second1, half)
+        quantize_g(1, second1[:], half)
         scatter(1, early1, 0, half)
-        xm_ops.append(operand("xm2", ROW_PASSES * P, grouped_tag="g0_second"))
-        group_xm(2)
+        xm_ops.append(operand("xm2", ROW_PASSES * P, grouped_tag="late"))
+        group_xm(2, 0)
+        group_xm(2, 1)
         quantize(xm_ops[2], 0, 2 * P, E4M3)
         late0 = product("grad0_second", 0, 0, g_ops, half, N)
-        xm_ops.append(operand("xm3", ROW_PASSES * P, grouped_tag="g0_second"))
-        group_xm(3)
+        xm_ops.append(operand("xm3", ROW_PASSES * P, grouped_tag="late"))
+        group_xm(3, 0)
+        group_xm(3, 1)
         quantize(xm_ops[3], 0, 2 * P, E4M3)
         late1 = product("grad1_second", 7, 1, g_ops, half, N)
-        grad2 = product("grad2", 4, 2, g_ops, 0, N, "xm_raw256_1")
+        grad2 = product("grad2", 4, 2, g_ops, 0, N)
         grad3 = product("grad3", 5, 3, g_ops, 0, N)
         for b, grad, s0 in ((0, late0, half), (1, late1, half), (2, grad2, 0), (3, grad3, 0)):
             scatter(b, grad, s0, N)

@@ -78,10 +78,10 @@ def tile_attend_gds_sq_kernel(tc, xT, wT, vT, wt, xm, offs, out):
         weights = keep.tile([P, ROW_PASSES, PACK], F32, name="weights")
 
         nc.scalar.dma_start(weights[:], wt[0].rearrange("(h p t) o -> p h (t o)", p=P, t=PACK))
-        nc.sync.dma_start(x0_raw[:], x_rows[:, :, 0:K_PASS])
+        nc.sync.dma_start(v_pairs[0][:], v_rows[:, 0:2, :])
         nc.sync.dma_start(offsets[:], offs)
-        for u in range(2):
-            nc.sync.dma_start(v_pairs[u][:], v_rows[:, 2 * u : 2 * u + 2, :])
+        nc.sync.dma_start(v_pairs[1][:], v_rows[:, 2:4, :])
+        nc.sync.dma_start(x0_raw[:], x_rows[:, :, 0:K_PASS])
         for j in range(PACK):
             nc.sync.dma_start(w_planes[j][:], w_rows[:, j, :])
         nc.sync.dma_start(x1_front, x_rows[:, :, K_PASS : K_PASS + x_cut])
@@ -91,11 +91,10 @@ def tile_attend_gds_sq_kernel(tc, xT, wT, vT, wt, xm, offs, out):
                 nc.sync.dma_start(xm_raw[s][h][:], xm_rows[h][:, :, d0:d1])
 
         windows = [keep.tile([P, T], F32, name=f"window{b}") for b in range(BLOCKS)]
-        v_op = operand("v", N, "w_plane1")
+        v_op = operand("v", N, "w_plane0")
         w_op = operand("w", N)
         x_ops = [operand(f"x{h}", K_PASS) for h in range(ROW_PASSES)]
-        late = keep.tile([P, 2 * half + ROW_PASSES * P * PACK], BF16, name="late", align_bytes=64)
-        xm_ops = [operand("xm0", ROW_PASSES * P), operand("xm1", ROW_PASSES * P, grouped=late[:, 2 * half :].rearrange("p (w j) -> p w j", j=PACK))]
+        xm_ops = [operand(f"xm{b}", ROW_PASSES * P) for b in range(2)]
         g_ops, g_early = [], []
         for h in range(ROW_PASSES):
             codes = keep.tile([P, half + N], U32, name=f"g{h}_codes", align_bytes=64)
@@ -121,7 +120,8 @@ def tile_attend_gds_sq_kernel(tc, xT, wT, vT, wt, xm, offs, out):
             for h in range(ROW_PASSES)
         ]
         g0_planes = front[:, 0 : PACK * half // 2].bitcast(BF16).rearrange("p (t i) -> p t i", t=PACK)
-        g_planes = [g0_planes, late[:, 0 : PACK * half].rearrange("p (t i) -> p t i", t=PACK)]
+        late = keep.tile([P, PACK, half], BF16, name="late", align_bytes=64)
+        g_planes = [g0_planes, late[:]]
         g1_first = keep.tile([P, half, PACK], BF16, name="g1_first", align_bytes=64)
         g_first = [shared[:, 0 : half * PACK // 2].bitcast(BF16).rearrange("p (w j) -> p w j", j=PACK), g1_first[:]]
 
@@ -132,7 +132,7 @@ def tile_attend_gds_sq_kernel(tc, xT, wT, vT, wt, xm, offs, out):
             for bank, ts, c0, c1 in banks:
                 passes = [(e, t, table) for e, t in enumerate(ts) for table in tables]
                 for n, (e, t, table) in enumerate(passes):
-                    matmul(bank[:, e, :], x_ops[h], t * P, table, c0, c1, E4M3, start and n == 0, stop and n == len(passes) - 1)
+                    matmul(bank[:, e, :], x_lead if (h, t) == (0, 0) else x_ops[h], t * P, table, c0, c1, E4M3, start and n == 0, stop and n == len(passes) - 1)
 
         def weigh_direct(h, c):
             nc.vector.tensor_tensor(
@@ -167,9 +167,6 @@ def tile_attend_gds_sq_kernel(tc, xT, wT, vT, wt, xm, offs, out):
                 in_=raw.rearrange("p j (m t) -> p m j t", t=PACK)[:, :, :, t0:t1],
             )
 
-        group_x(nc.scalar.copy, 0, x0_raw[:], 0, P, 0, PACK)
-        quantize(x_ops[0], 0, K_PASS, E4M3)
-
         v_picked = keep.tile([P, PACK, N], F32, name="v_picked")
         for j in range(PACK):
             nc.vector.tensor_copy(v_picked[:, j, :], v_pairs[j // 2][:, j % 2, :].indirect(offsets[:]))
@@ -180,9 +177,17 @@ def tile_attend_gds_sq_kernel(tc, xT, wT, vT, wt, xm, offs, out):
             scale=-1.0,
         )
 
+        group_x(nc.vector.tensor_copy, 0, x0_raw[:], 0, P, 0, PACK)
+        quantize(x_ops[0], P, 2 * P, E4M3)
+        quantize(x_ops[0], 2 * P, K_PASS, E4M3)
+
         for j in range(PACK):
-            if j == 2:
+            if j == 1:
                 quantize(v_op, 0, N, E4M3)
+            if j == 3:
+                lead_codes = keep.tile([P, P], U32, name="lead_codes", tag="w_plane2", align_bytes=64)
+                x_lead = (x_ops[0][0], lead_codes, x_ops[0][2])
+                quantize(x_lead, 0, P, E4M3)
                 score_passes(0, [v_op], True, False)
             for s0, s1 in ((0, N),) if j < PACK - 1 else ((half, N), (0, half)):
                 nc.vector.tensor_copy(
@@ -228,7 +233,7 @@ def tile_attend_gds_sq_kernel(tc, xT, wT, vT, wt, xm, offs, out):
         quantize(xm_ops[1], 0, 2 * P, E4M3)
         weigh_paired(1)
         quantize_g(0, g_first[0], half)
-        second1 = keep.tile([P, half, PACK], BF16, name="g1_second", align_bytes=64)
+        second1 = xm_ops[1][0]
         group_g(1, nc.scalar.copy, second1[:])
         early1 = product("grad1_first", 7, 1, g_early, half, N)
         scatter(0, early0, 0, half)

@@ -1,6 +1,7 @@
 from contextlib import ExitStack
 
 import concourse.mybir as mybir
+from concourse.masks import make_identity
 
 N, T, D, R = 512, 2048, 512, 1024
 FLOPS = 3 * 2 * N * D * R
@@ -77,7 +78,17 @@ def tile_attend_gds_sq_kernel(tc, xT, wT, vT, wt, xm, offs, out):
         ]
         weights = keep.tile([P, ROW_PASSES, PACK], F32, name="weights")
 
-        nc.scalar.dma_start(weights[:], wt[0].rearrange("(h p t) o -> p h (t o)", p=P, t=PACK))
+        identity = keep.tile([P, P], F32, name="identity")
+        make_identity(nc, identity[:])
+        weight_rows = keep.tile([P, K_PASS], F32, name="weight_rows")
+        weight_in = keep.tile([ROW_PASSES, K_PASS], F32, name="weight_in")
+        nc.scalar.dma_start(weight_in[:], wt[0].rearrange("(h r) o -> h (r o)", h=ROW_PASSES))
+        nc.gpsimd.memset(weight_rows[:], 0.0)
+        nc.scalar.copy(out=weight_rows[0:ROW_PASSES, :], in_=weight_in[:])
+        turned = psum.tile([P, PACK, P], F32, name="turned", tag="bank7")
+        for t in range(PACK):
+            nc.tensor.transpose(turned[:, t, :], weight_rows[:, t::PACK], identity[:])
+        nc.scalar.copy(out=weights[:], in_=turned[:, :, 0:ROW_PASSES].rearrange("p t h -> p h t"))
         nc.sync.dma_start(v_pairs[0][:], v_rows[:, 0:2, :])
         nc.sync.dma_start(offsets[:], offs)
         nc.sync.dma_start(v_pairs[1][:], v_rows[:, 2:4, :])

@@ -209,7 +209,8 @@ def tile_attend_gds_sq_kernel(tc, xT, wT, vT, wt, xm, offs, out):
         score_passes(0, [w_op], False, True)
 
         for b in range(BLOCKS):
-            nc.vector.memset(windows[b][:], 0.0)
+            engine = nc.vector if b < BLOCKS // 2 else nc.gpsimd
+            engine.memset(windows[b][:], 0.0)
 
         def product(name, bank, b, g, c0, c1, tag=None):
             acc = psum.tile([P, N], F32, name=name, tag=f"bank{bank}")

@@ -21,8 +21,11 @@ PACK = 4
 K_PASS = P * PACK
 ROW_PASSES = R // K_PASS
 BLOCKS = D // P
-QUARTERS = N // P
+HALF = N // 2
 LIST_ROWS = 16
+EARLY = (0, HALF)
+LATE = (HALF, N)
+WHOLE = (0, N)
 
 
 def tile_attend_gds_sq_kernel(tc, xT, wT, vT, wt, xm, offs, out):
@@ -31,31 +34,33 @@ def tile_attend_gds_sq_kernel(tc, xT, wT, vT, wt, xm, offs, out):
         keep = ctx.enter_context(tc.tile_pool(name="keep", bufs=1))
         psum = ctx.enter_context(tc.psum_pool(name="psum", bufs=1))
 
-        def operand(name, width, codes_tag=None, grouped_tag=None, grouped=None):
-            if grouped is None:
-                grouped = keep.tile([P, width, PACK], BF16, name=name + "_grouped", tag=grouped_tag or name + "_grouped", align_bytes=64)
-            codes = keep.tile([P, width], U32, name=name + "_codes", tag=codes_tag or name + "_codes", align_bytes=64)
-            scales = keep.tile([P, width], U8, name=name + "_scales", align_bytes=64)
-            return grouped, codes, scales
+        def sbuf(name, shape, dtype, tag=None):
+            return keep.tile(shape, dtype, name=name, tag=tag or name, align_bytes=64)
 
-        def quantize(op, c0, c1, fmt):
-            grouped, codes, scales = op
+        def planes(name, width, codes_tag=None):
+            return sbuf(name + "_codes", [P, width], U32, codes_tag), sbuf(name + "_scales", [P, width], U8)
+
+        def quantize(op, c0, c1, grouped, fmt):
             nc.vector.quantize_mx(
-                out=codes[:, c0:c1].bitcast(fmt),
-                scales=scales[:, c0:c1],
-                in_=grouped[:, c0:c1, :].rearrange("p w j -> p (w j)"),
+                out=op[0][:, c0:c1].bitcast(fmt), scales=op[1][:, c0:c1], in_=grouped.rearrange("p w j -> p (w j)")
             )
 
         def matmul(acc, lhs, l0, rhs, r0, r1, rhs_fmt, start, stop):
             nc.tensor.matmul_mx(
                 out=acc,
-                lhsT=lhs[1][:, l0 : l0 + P].bitcast(E4M3),
-                lhsT_scale=lhs[2][:, l0 : l0 + P],
-                rhs=rhs[1][:, r0:r1].bitcast(rhs_fmt),
-                rhs_scale=rhs[2][:, r0:r1],
+                lhsT=lhs[0][:, l0 : l0 + P].bitcast(E4M3),
+                lhsT_scale=lhs[1][:, l0 : l0 + P],
+                rhs=rhs[0][:, r0:r1].bitcast(rhs_fmt),
+                rhs_scale=rhs[1][:, r0:r1],
                 start=start,
                 stop=stop,
             )
+
+        def listed(window, slots):
+            return window.indirect(offsets[:, slots[0] // LIST_ROWS : slots[1] // LIST_ROWS])
+
+        def interleave(copy, grouped, rows):
+            copy(out=grouped.rearrange("p (c i) j -> p c j i", i=PACK), in_=rows.rearrange("p j (c i) -> p c j i", i=PACK))
 
         offsets = keep.tile([P, N // LIST_ROWS], U16, name="offsets")
         v_rows = vT.rearrange("(p j) t -> p j t", j=PACK)
@@ -63,24 +68,21 @@ def tile_attend_gds_sq_kernel(tc, xT, wT, vT, wt, xm, offs, out):
         x_rows = xT[0].rearrange("(p j) r -> p j r", j=PACK)
         xm_rows = xm[0].rearrange("(h p j) d -> h p j d", p=P, j=PACK)
 
-        v_pairs = [keep.tile([P, 2, T], F32, name=f"v_pair{u}") for u in range(2)]
-        w_planes = [keep.tile([P, T], F32, name=f"w_plane{j}", tag=f"w_plane{j}", align_bytes=64) for j in range(PACK)]
-        half = N // 2
+        v_pairs = [sbuf(f"v_pair{u}", [P, 2, T], F32) for u in range(2)]
+        w_planes = [sbuf(f"w_plane{j}", [P, T], F32) for j in range(PACK)]
         x_cut = K_PASS // 2
-        x0_raw = keep.tile([P, PACK, K_PASS], F32, name="x0_raw")
-        front = keep.tile([P, PACK * x_cut], F32, name="front", align_bytes=64)
+        x0_raw = sbuf("x0_raw", [P, PACK, K_PASS], F32)
+        front = sbuf("front", [P, PACK * x_cut], F32)
+        back = sbuf("back", [P, PACK * x_cut], F32)
         x1_front = front[:].rearrange("p (j r) -> p j r", j=PACK)
-        shared = keep.tile([P, PACK * x_cut], F32, name="shared", align_bytes=64)
-        x1_back = shared[:].rearrange("p (j r) -> p j r", j=PACK)
+        x1_back = back[:].rearrange("p (j r) -> p j r", j=PACK)
         xm_cuts = ((0, P), (P, 2 * P), (2 * P, D))
-        xm_raw = [
-            [keep.tile([P, PACK, d1 - d0], F32, name=f"xm_raw{d0}_{h}", align_bytes=64) for h in range(ROW_PASSES)] for d0, d1 in xm_cuts
-        ]
-        weights = keep.tile([P, ROW_PASSES, PACK], F32, name="weights")
+        xm_raw = [[sbuf(f"xm_raw{d0}_{h}", [P, PACK, d1 - d0], F32) for h in range(ROW_PASSES)] for d0, d1 in xm_cuts]
+        weights = sbuf("weights", [P, ROW_PASSES, PACK], F32)
 
-        identity = keep.tile([P, P], F32, name="identity")
+        identity = sbuf("identity", [P, P], F32)
         make_identity(nc, identity[:])
-        weight_rows = keep.tile([P, K_PASS], F32, name="weight_rows")
+        weight_rows = sbuf("weight_rows", [P, K_PASS], F32)
         weight_in = keep.tile([ROW_PASSES, K_PASS], F32, name="weight_in")
         nc.scalar.dma_start(weight_in[:], wt[0].rearrange("(h r) o -> h (r o)", h=ROW_PASSES))
         nc.gpsimd.memset(weight_rows[:], 0.0)
@@ -89,6 +91,7 @@ def tile_attend_gds_sq_kernel(tc, xT, wT, vT, wt, xm, offs, out):
         for t in range(PACK):
             nc.tensor.transpose(turned[:, t, :], weight_rows[:, t::PACK], identity[:])
         nc.scalar.copy(out=weights[:], in_=turned[:, :, 0:ROW_PASSES].rearrange("p t h -> p h t"))
+
         nc.sync.dma_start(v_pairs[0][:], v_rows[:, 0:2, :])
         nc.sync.dma_start(offsets[:], offs)
         nc.sync.dma_start(v_pairs[1][:], v_rows[:, 2:4, :])
@@ -102,167 +105,159 @@ def tile_attend_gds_sq_kernel(tc, xT, wT, vT, wt, xm, offs, out):
                 nc.sync.dma_start(xm_raw[s][h][:], xm_rows[h][:, :, d0:d1])
 
         windows = [keep.tile([P, T], F32, name=f"window{b}") for b in range(BLOCKS)]
-        v_op = operand("v", N, "w_plane0")
-        w_op = operand("w", N)
-        x_ops = [operand(f"x{h}", K_PASS) for h in range(ROW_PASSES)]
-        xm_ops = [operand(f"xm{b}", ROW_PASSES * P) for b in range(2)]
-        g_ops, g_early = [], []
-        for h in range(ROW_PASSES):
-            codes = keep.tile([P, half + N], U32, name=f"g{h}_codes", align_bytes=64)
-            scales = keep.tile([P, half + N], U8, name=f"g{h}_scales", align_bytes=64)
-            nc.vector.memset(codes[:, 0:half], 0)
-            nc.vector.memset(scales[:, 0:half], 0)
-            g_ops.append((None, codes[:, half:], scales[:, half:]))
-            g_early.append((None, codes[:, 0:N], scales[:, 0:N]))
-
-        def group_xm(b, h):
-            raw = xm_raw[b][h][:] if b < 2 else xm_raw[2][h][:, :, (b - 2) * P : (b - 1) * P]
-            nc.scalar.copy(
-                out=xm_ops[b][0][:, h * P : (h + 1) * P, :].rearrange("p (c i) j -> p c j i", i=PACK),
-                in_=raw.rearrange("p j (c i) -> p c j i", i=PACK),
-            )
+        for b in range(BLOCKS):
+            engine = nc.vector if b < BLOCKS // 2 else nc.gpsimd
+            engine.memset(windows[b][:], 0.0)
 
         direct = [
             [psum.tile([P, PACK, P], F32, name=f"direct{h}_{c}", tag=f"bank{4 * h + c}") for c in range(2)]
             for h in range(ROW_PASSES)
         ]
         paired = [
-            [psum.tile([P, 2, half], F32, name=f"paired{h}_{u}", tag=f"bank{4 * h + 2 + u}") for u in range(2)]
+            [psum.tile([P, 2, HALF], F32, name=f"paired{h}_{u}", tag=f"bank{4 * h + 2 + u}") for u in range(2)]
             for h in range(ROW_PASSES)
         ]
-        g0_planes = front[:, 0 : PACK * half // 2].bitcast(BF16).rearrange("p (t i) -> p t i", t=PACK)
-        late = keep.tile([P, PACK, half], BF16, name="late", align_bytes=64)
-        g_planes = [g0_planes, late[:]]
-        g1_first = keep.tile([P, half, PACK], BF16, name="g1_first", align_bytes=64)
-        g_first = [shared[:, 0 : half * PACK // 2].bitcast(BF16).rearrange("p (w j) -> p w j", j=PACK), g1_first[:]]
+        x_grouped = [sbuf(f"x{h}_grouped", [P, K_PASS, PACK], BF16) for h in range(ROW_PASSES)]
+        x_ops = [planes(f"x{h}", K_PASS) for h in range(ROW_PASSES)]
 
         def score_passes(h, tables, start, stop):
             early = [(direct[h][c], range(PACK), c * P, (c + 1) * P) for c in range(2)]
-            late = [(paired[h][u], (2 * u, 2 * u + 1), half, N) for u in range(2)]
-            banks = late + early if h == 0 else early + late
-            for bank, ts, c0, c1 in banks:
+            late = [(paired[h][u], (2 * u, 2 * u + 1), HALF, N) for u in range(2)]
+            for bank, ts, c0, c1 in late + early if h == 0 else early + late:
                 passes = [(e, t, table) for e, t in enumerate(ts) for table in tables]
                 for n, (e, t, table) in enumerate(passes):
-                    matmul(bank[:, e, :], x_lead if (h, t) == (0, 0) else x_ops[h], t * P, table, c0, c1, E4M3, start and n == 0, stop and n == len(passes) - 1)
-
-        def weigh_direct(h, c):
-            nc.vector.tensor_tensor(
-                g_first[h][:, c * P : (c + 1) * P, :],
-                direct[h][c][:].rearrange("p t i -> p i t"),
-                weights[:, h : h + 1, :].to_broadcast([P, P, PACK]),
-                MULT,
-            )
-
-        def weigh_paired(h):
-            for t in range(PACK):
-                nc.scalar.activation(
-                    out=g_planes[h][:, t, :], in_=paired[h][t // 2][:, t % 2, :], func=COPY, scale=weights[:, h, t : t + 1]
-                )
-
-        def group_g(h, copy, grouped):
-            copy(
-                out=grouped.rearrange("p (c i) t -> p c t i", i=PACK),
-                in_=g_planes[h].rearrange("p t (c i) -> p c t i", i=PACK),
-            )
-
-        def quantize_g(h, grouped, c0):
-            nc.vector.quantize_mx(
-                out=g_ops[h][1][:, c0 : c0 + half].bitcast(E5M2),
-                scales=g_ops[h][2][:, c0 : c0 + half],
-                in_=grouped.rearrange("p w j -> p (w j)"),
-            )
+                    lhs = x_lead if (h, t) == (0, 0) else x_ops[h]
+                    matmul(bank[:, e, :], lhs, t * P, table, c0, c1, E4M3, start and n == 0, stop and n == len(passes) - 1)
 
         def group_x(copy, h, raw, m0, m1, t0, t1):
             copy(
-                out=x_ops[h][0][:].rearrange("p (t m) j -> p m j t", t=PACK)[:, m0:m1, :, t0:t1],
+                out=x_grouped[h][:].rearrange("p (t m) j -> p m j t", t=PACK)[:, m0:m1, :, t0:t1],
                 in_=raw.rearrange("p j (m t) -> p m j t", t=PACK)[:, :, :, t0:t1],
             )
 
-        v_picked = keep.tile([P, PACK, N], F32, name="v_picked")
+        v_picked = sbuf("v_picked", [P, PACK, N], F32)
+        v_grouped = sbuf("v_grouped", [P, N, PACK], BF16)
+        v_op = planes("v", N, "w_plane0")
         for j in range(PACK):
-            nc.vector.tensor_copy(v_picked[:, j, :], v_pairs[j // 2][:, j % 2, :].indirect(offsets[:]))
+            nc.vector.tensor_copy(v_picked[:, j, :], listed(v_pairs[j // 2][:, j % 2, :], WHOLE))
         nc.scalar.activation(
-            out=v_op[0][:].rearrange("p (c i) j -> p c j i", i=PACK),
+            out=v_grouped[:].rearrange("p (c i) j -> p c j i", i=PACK),
             in_=v_picked[:].rearrange("p j (c i) -> p c j i", i=PACK),
             func=COPY,
             scale=-1.0,
         )
 
         group_x(nc.vector.tensor_copy, 0, x0_raw[:], 0, P, 0, PACK)
-        quantize(x_ops[0], P, 2 * P, E4M3)
-        quantize(x_ops[0], 2 * P, K_PASS, E4M3)
+        quantize(x_ops[0], P, 2 * P, x_grouped[0][:, P : 2 * P, :], E4M3)
+        quantize(x_ops[0], 2 * P, K_PASS, x_grouped[0][:, 2 * P :, :], E4M3)
 
+        w_grouped = sbuf("w_grouped", [P, N, PACK], BF16)
+        w_op = planes("w", N)
         for j in range(PACK):
             if j == 1:
-                quantize(v_op, 0, N, E4M3)
+                quantize(v_op, 0, N, v_grouped[:], E4M3)
             if j == 3:
-                lead_codes = keep.tile([P, P], U32, name="lead_codes", tag="w_plane2", align_bytes=64)
-                x_lead = (x_ops[0][0], lead_codes, x_ops[0][2])
-                quantize(x_lead, 0, P, E4M3)
+                x_lead = (sbuf("lead_codes", [P, P], U32, "w_plane2"), x_ops[0][1])
+                quantize(x_lead, 0, P, x_grouped[0][:, 0:P, :], E4M3)
                 score_passes(0, [v_op], True, False)
-            for s0, s1 in ((0, N),) if j < PACK - 1 else ((half, N), (0, half)):
-                nc.vector.tensor_copy(
-                    w_op[0][:, s0:s1, j], w_planes[j][:].indirect(offsets[:, s0 // LIST_ROWS : s1 // LIST_ROWS])
-                )
-        for u in (1, 0):
-            quantize(w_op, u * half, (u + 1) * half, E4M3)
+            for slots in (WHOLE,) if j < PACK - 1 else (LATE, EARLY):
+                nc.vector.tensor_copy(w_grouped[:, slots[0] : slots[1], j], listed(w_planes[j][:], slots))
+        for s0, s1 in (LATE, EARLY):
+            quantize(w_op, s0, s1, w_grouped[:, s0:s1, :], E4M3)
         score_passes(0, [w_op], False, True)
-
-        for b in range(BLOCKS):
-            engine = nc.vector if b < BLOCKS // 2 else nc.gpsimd
-            engine.memset(windows[b][:], 0.0)
-
-        def product(name, bank, b, g, c0, c1, tag=None):
-            acc = psum.tile([P, N], F32, name=name, tag=f"bank{bank}")
-            for h in range(ROW_PASSES):
-                matmul(acc[:], xm_ops[b], h * P, g[h], 0, N, E5M2, h == 0, h == ROW_PASSES - 1)
-            grad = keep.tile([P, c1 - c0], F32, name=name + "_sb", tag=tag or name + "_sb", align_bytes=64)
-            nc.scalar.copy(out=grad[:], in_=acc[:, c0:c1])
-            return grad
-
-        def scatter(b, grad, s0, s1):
-            nc.vector.tensor_copy(windows[b][:].indirect(offsets[:, s0 // LIST_ROWS : s1 // LIST_ROWS]), grad[:])
 
         group_x(nc.scalar.copy, 1, x1_front, 0, P // 2, 0, PACK)
         for u in range(2):
             group_x(nc.vector.tensor_copy, 1, x1_back, P // 2, P, 2 * u, 2 * u + 2)
         for u in range(2):
-            quantize(x_ops[1], 2 * u * P, (2 * u + 2) * P, E4M3)
+            quantize(x_ops[1], 2 * u * P, (2 * u + 2) * P, x_grouped[1][:, 2 * u * P : (2 * u + 2) * P, :], E4M3)
         score_passes(1, [v_op, w_op], True, True)
-        weigh_paired(0)
-        group_xm(0, 0)
-        group_xm(0, 1)
-        group_xm(1, 0)
-        group_xm(1, 1)
+
+        g_ops = [planes(f"g{h}", N) for h in range(ROW_PASSES)]
+        g_words = [
+            back[:, 0 : HALF * PACK // 2].bitcast(BF16).rearrange("p (w j) -> p w j", j=PACK),
+            sbuf("g1_words", [P, HALF, PACK], BF16)[:],
+        ]
+        g_rows = [
+            front[:, 0 : PACK * HALF // 2].bitcast(BF16).rearrange("p (t i) -> p t i", t=PACK),
+            sbuf("g1_rows", [P, PACK, HALF], BF16)[:],
+        ]
+
+        def weigh_early(h, c):
+            nc.vector.tensor_tensor(
+                g_words[h][:, c * P : (c + 1) * P, :],
+                direct[h][c][:].rearrange("p t i -> p i t"),
+                weights[:, h : h + 1, :].to_broadcast([P, P, PACK]),
+                MULT,
+            )
+
+        def weigh_late(h):
+            for t in range(PACK):
+                nc.scalar.activation(
+                    out=g_rows[h][:, t, :], in_=paired[h][t // 2][:, t % 2, :], func=COPY, scale=weights[:, h, t : t + 1]
+                )
+
+        xm_ops = [planes(f"xm{b}", ROW_PASSES * P) for b in range(2)]
+        rest_ops = [planes(f"rest{h}", 2 * P) for h in range(ROW_PASSES)]
+
+        def product(name, bank, b, slots, copy, tag=None):
+            s0, s1 = slots
+            acc = psum.tile([P, s1 - s0], F32, name=name, tag=f"bank{bank}")
+            for h in range(ROW_PASSES):
+                lhs, l0 = (xm_ops[b], h * P) if b < 2 else (rest_ops[h], (b - 2) * P)
+                matmul(acc[:], lhs, l0, g_ops[h], s0, s1, E5M2, h == 0, h == ROW_PASSES - 1)
+            grad = sbuf(name + "_sb", [P, s1 - s0], F32, tag)
+            copy(out=grad[:], in_=acc[:])
+            return grad
+
+        def scatter_vector(b, grad, slots):
+            nc.vector.tensor_copy(listed(windows[b][:], slots), grad)
+
+        def scatter_scalar(b, grad, slots):
+            nc.scalar.activation(out=listed(windows[b][:], slots), in_=grad, func=COPY)
+
+        def store(b):
+            nc.sync.dma_start(out[b * P : (b + 1) * P, :], windows[b][:])
+
+        weigh_late(0)
+        xm0_grouped = sbuf("xm0_grouped", [P, ROW_PASSES * P, PACK], BF16)
+        for h in range(ROW_PASSES):
+            interleave(nc.scalar.copy, xm0_grouped[:, h * P : (h + 1) * P, :], xm_raw[0][h][:])
+        weigh_late(1)
+        xm1_grouped = sbuf("xm1_grouped", [P, ROW_PASSES * P, PACK], BF16, "x1_codes")
+        for h in range(ROW_PASSES):
+            interleave(nc.scalar.copy, xm1_grouped[:, h * P : (h + 1) * P, :], xm_raw[1][h][:])
+
         for h in range(ROW_PASSES):
             for c in range(2):
-                weigh_direct(h, c)
-        quantize_g(0, g_first[0], 0)
-        quantize(xm_ops[0], 0, 2 * P, E4M3)
-        quantize_g(1, g_first[1], 0)
-        early0 = product("grad0_first", 0, 0, g_early, half, N)
-        group_g(0, nc.vector.tensor_copy, g_first[0])
-        quantize(xm_ops[1], 0, 2 * P, E4M3)
-        weigh_paired(1)
-        quantize_g(0, g_first[0], half)
-        second1 = xm_ops[1][0]
-        group_g(1, nc.scalar.copy, second1[:])
-        early1 = product("grad1_first", 7, 1, g_early, half, N)
-        scatter(0, early0, 0, half)
-        quantize_g(1, second1[:], half)
-        scatter(1, early1, 0, half)
-        xm_ops.append(operand("xm2", ROW_PASSES * P, grouped_tag="late"))
-        group_xm(2, 0)
-        group_xm(2, 1)
-        quantize(xm_ops[2], 0, 2 * P, E4M3)
-        late0 = product("grad0_second", 0, 0, g_ops, half, N)
-        xm_ops.append(operand("xm3", ROW_PASSES * P, grouped_tag="late"))
-        group_xm(3, 0)
-        group_xm(3, 1)
-        quantize(xm_ops[3], 0, 2 * P, E4M3)
-        late1 = product("grad1_second", 7, 1, g_ops, half, N)
-        grad2 = product("grad2", 4, 2, g_ops, 0, N)
-        grad3 = product("grad3", 5, 3, g_ops, 0, N)
-        for b, grad, s0 in ((0, late0, half), (1, late1, half), (2, grad2, 0), (3, grad3, 0)):
-            scatter(b, grad, s0, N)
-            nc.sync.dma_start(out[b * P : (b + 1) * P, :], windows[b][:])
+                weigh_early(h, c)
+        quantize(g_ops[0], 0, HALF, g_words[0], E5M2)
+        quantize(xm_ops[0], 0, 2 * P, xm0_grouped[:], E4M3)
+        quantize(g_ops[1], 0, HALF, g_words[1], E5M2)
+        early0 = product("early0", 0, 0, EARLY, nc.scalar.copy)
+        scatter_scalar(0, early0[:], EARLY)
+
+        for h in range(ROW_PASSES):
+            interleave(nc.vector.tensor_copy, g_words[h], g_rows[h])
+        for h in range(ROW_PASSES):
+            quantize(g_ops[h], HALF, N, g_words[h], E5M2)
+        late0 = product("late0", 1, 0, LATE, nc.scalar.copy)
+        scatter_scalar(0, late0[:], LATE)
+        store(0)
+
+        quantize(xm_ops[1], 0, 2 * P, xm1_grouped[:], E4M3)
+        rest_grouped = [sbuf(f"rest_grouped{h}", [P, 2 * P, PACK], BF16, tag) for h, tag in enumerate(("g1_words", "g1_rows"))]
+        for h in range(ROW_PASSES):
+            interleave(nc.vector.tensor_copy, rest_grouped[h][:], xm_raw[2][h][:])
+        quantize(rest_ops[0], 0, 2 * P, rest_grouped[0][:], E4M3)
+        grad1 = product("grad1", 2, 1, WHOLE, nc.vector.tensor_copy, f"xm_raw{2 * P}_1")
+        quantize(rest_ops[1], 0, 2 * P, rest_grouped[1][:], E4M3)
+        scatter_vector(1, grad1[:], WHOLE)
+        store(1)
+        grad2 = product("grad2", 3, 2, WHOLE, nc.scalar.copy)
+        for s0, s1 in (EARLY, LATE):
+            scatter_scalar(2, grad2[:, s0:s1], (s0, s1))
+        store(2)
+        grad3 = product("grad3", 4, 3, WHOLE, nc.vector.tensor_copy, f"xm_raw{2 * P}_1")
+        scatter_vector(3, grad3[:], WHOLE)
+        store(3)

@@ -15,6 +15,7 @@ E4M3 = mybir.dt.float8_e4m3fn_x4
 E5M2 = mybir.dt.float8_e5m2_x4
 COPY = mybir.ActivationFunctionType.Copy
 MULT = mybir.AluOpType.mult
+ADD = mybir.AluOpType.add
 
 P = 128
 PACK = 4
@@ -61,6 +62,9 @@ def tile_attend_gds_sq_kernel(tc, xT, wT, vT, wt, xm, offs, out):
 
         def interleave(copy, grouped, rows):
             copy(out=grouped.rearrange("p (c i) j -> p c j i", i=PACK), in_=rows.rearrange("p j (c i) -> p c j i", i=PACK))
+
+        def gpsimd_copy(out, in_):
+            nc.gpsimd.tensor_scalar(out=out, in0=in_, scalar1=1.0, scalar2=0.0, op0=MULT, op1=ADD)
 
         offsets = keep.tile([P, N // LIST_ROWS], U16, name="offsets")
         v_rows = vT.rearrange("(p j) t -> p j t", j=PACK)
@@ -220,6 +224,8 @@ def tile_attend_gds_sq_kernel(tc, xT, wT, vT, wt, xm, offs, out):
             nc.sync.dma_start(out[b * P : (b + 1) * P, :], windows[b][:])
 
         weigh_late(0)
+        g0_late_words = sbuf("g0_late_words", [P, HALF, PACK], BF16)
+        gpsimd_copy(g0_late_words[:], g_rows[0].rearrange("p t i -> p i t"))
         xm0_grouped = sbuf("xm0_grouped", [P, ROW_PASSES * P, PACK], BF16)
         for h in range(ROW_PASSES):
             interleave(nc.scalar.copy, xm0_grouped[:, h * P : (h + 1) * P, :], xm_raw[0][h][:])
@@ -237,10 +243,9 @@ def tile_attend_gds_sq_kernel(tc, xT, wT, vT, wt, xm, offs, out):
         early0 = product("early0", 0, 0, EARLY, nc.scalar.copy)
         scatter_scalar(0, early0[:], EARLY)
 
-        for h in range(ROW_PASSES):
-            interleave(nc.vector.tensor_copy, g_words[h], g_rows[h])
-        for h in range(ROW_PASSES):
-            quantize(g_ops[h], HALF, N, g_words[h], E5M2)
+        interleave(nc.vector.tensor_copy, g_words[1], g_rows[1])
+        quantize(g_ops[0], HALF, N, g0_late_words[:], E5M2)
+        quantize(g_ops[1], HALF, N, g_words[1], E5M2)
         late0 = product("late0", 1, 0, LATE, nc.scalar.copy)
         scatter_scalar(0, late0[:], LATE)
         store(0)

@@ -80,7 +80,7 @@ def tile_attend_gds_sq_kernel(tc, xT, wT, vT, wt, xm, offs, out):
         back = sbuf("back", [P, PACK * x_cut], F32)
         x1_front = front[:].rearrange("p (j r) -> p j r", j=PACK)
         x1_back = back[:].rearrange("p (j r) -> p j r", j=PACK)
-        xm_cuts = ((0, P), (P, 2 * P), (2 * P, D))
+        xm_cuts = ((0, 2 * P), (2 * P, D))
         xm_raw = [[sbuf(f"xm_raw{d0}_{h}", [P, PACK, d1 - d0], F32) for h in range(ROW_PASSES)] for d0, d1 in xm_cuts]
         weights = sbuf("weights", [P, ROW_PASSES, PACK], F32)
 
@@ -114,20 +114,18 @@ def tile_attend_gds_sq_kernel(tc, xT, wT, vT, wt, xm, offs, out):
             engine.memset(windows[b][:], 0.0)
 
         direct = [
-            [psum.tile([P, PACK, P], F32, name=f"direct{h}_{c}", tag=f"bank{4 * h + c}") for c in range(2)]
+            [psum.tile([P, PACK, P], F32, name=f"direct{h}_{c}", tag=f"bank{4 * h + c}") for c in range(2 + 2 * h)]
             for h in range(ROW_PASSES)
         ]
-        paired = [
-            [psum.tile([P, 2, HALF], F32, name=f"paired{h}_{u}", tag=f"bank{4 * h + 2 + u}") for u in range(2)]
-            for h in range(ROW_PASSES)
-        ]
+        paired = [psum.tile([P, 2, HALF], F32, name=f"paired{u}", tag=f"bank{2 + u}") for u in range(2)]
         x_grouped = [sbuf(f"x{h}_grouped", [P, K_PASS, PACK], BF16) for h in range(ROW_PASSES)]
         x_ops = [planes(f"x{h}", K_PASS) for h in range(ROW_PASSES)]
 
         def score_passes(h, tables, start, stop):
-            early = [(direct[h][c], range(PACK), c * P, (c + 1) * P) for c in range(2)]
-            late = [(paired[h][u], (2 * u, 2 * u + 1), HALF, N) for u in range(2)]
-            for bank, ts, c0, c1 in late + early if h == 0 else early + late:
+            banks = [(bank, range(PACK), c * P, (c + 1) * P) for c, bank in enumerate(direct[h])]
+            if h == 0:
+                banks = [(paired[u], (2 * u, 2 * u + 1), HALF, N) for u in range(2)] + banks
+            for bank, ts, c0, c1 in banks:
                 passes = [(e, t, table) for e, t in enumerate(ts) for table in tables]
                 for n, (e, t, table) in enumerate(passes):
                     lhs = x_lead if (h, t) == (0, 0) else x_ops[h]
@@ -178,38 +176,48 @@ def tile_attend_gds_sq_kernel(tc, xT, wT, vT, wt, xm, offs, out):
         score_passes(1, [v_op, w_op], True, True)
 
         g_ops = [planes(f"g{h}", N) for h in range(ROW_PASSES)]
-        g_words = [
-            back[:, 0 : HALF * PACK // 2].bitcast(BF16).rearrange("p (w j) -> p w j", j=PACK),
-            sbuf("g1_words", [P, HALF, PACK], BF16)[:],
-        ]
-        g_rows = [
-            front[:, 0 : PACK * HALF // 2].bitcast(BF16).rearrange("p (t i) -> p t i", t=PACK),
-            sbuf("g1_rows", [P, PACK, HALF], BF16)[:],
-        ]
+        xm_ops = [planes(f"xm{b}", ROW_PASSES * P) for b in range(BLOCKS - 1)]
+        first_grouped = sbuf("first_grouped", [P, 2 * ROW_PASSES * P, PACK], BF16, "x1_grouped")
+        rest_grouped = sbuf("rest_grouped", [P, 2 * ROW_PASSES * P, PACK], BF16)
+        back_words = back[:, 0 : HALF * PACK // 2].bitcast(BF16).rearrange("p (w j) -> p w j", j=PACK)
+        g1_early_words = rest_grouped[:, P : P + HALF, :]
+        g0_late_rows = front[:, 0 : PACK * HALF // 2].bitcast(BF16).rearrange("p (t i) -> p t i", t=PACK)
+        g0_late_words = sbuf("g0_late_words", [P, HALF, PACK], BF16)
 
-        def weigh_early(h, c):
+        def xm_place(b, h):
+            return ROW_PASSES * (b % 2) + (1 - h if b == 3 else h)
+
+        def xm_words(b, h):
+            place = xm_place(b, h)
+            return (first_grouped, rest_grouped)[b // 2][:, place * P : (place + 1) * P, :]
+
+        def xm_source(b, h):
+            return xm_raw[b // 2][h][:, :, (b % 2) * P : (b % 2 + 1) * P]
+
+        def group_xm(copy, b, h):
+            interleave(copy, xm_words(b, h), xm_source(b, h))
+
+        def group_xm_gpsimd(b, h):
+            gpsimd_copy(xm_words(b, h), xm_source(b, h).rearrange("p j d -> p d j"))
+
+        def quantize_xm(b):
+            w0 = ROW_PASSES * P * (b % 2)
+            quantize(xm_ops[b], 0, ROW_PASSES * P, (first_grouped, rest_grouped)[b // 2][:, w0 : w0 + ROW_PASSES * P, :], E4M3)
+
+        def weigh_direct(h, c, words):
             nc.vector.tensor_tensor(
-                g_words[h][:, c * P : (c + 1) * P, :],
+                words[:, (c % 2) * P : (c % 2 + 1) * P, :],
                 direct[h][c][:].rearrange("p t i -> p i t"),
                 weights[:, h : h + 1, :].to_broadcast([P, P, PACK]),
                 MULT,
             )
 
-        def weigh_late(h):
-            for t in range(PACK):
-                nc.scalar.activation(
-                    out=g_rows[h][:, t, :], in_=paired[h][t // 2][:, t % 2, :], func=COPY, scale=weights[:, h, t : t + 1]
-                )
-
-        xm_ops = [planes(f"xm{b}", ROW_PASSES * P) for b in range(2)]
-        rest_ops = [planes(f"rest{h}", 2 * P) for h in range(ROW_PASSES)]
-
         def product(name, bank, b, slots, copy, tag=None):
             s0, s1 = slots
             acc = psum.tile([P, s1 - s0], F32, name=name, tag=f"bank{bank}")
             for h in range(ROW_PASSES):
-                lhs, l0 = (xm_ops[b], h * P) if b < 2 else (rest_ops[h], (b - 2) * P)
-                matmul(acc[:], lhs, l0, g_ops[h], s0, s1, E5M2, h == 0, h == ROW_PASSES - 1)
+                l0 = xm_place(b, h) % ROW_PASSES * P
+                matmul(acc[:], xm_ops[b], l0, g_ops[h], s0, s1, E5M2, h == 0, h == ROW_PASSES - 1)
             grad = sbuf(name + "_sb", [P, s1 - s0], F32, tag)
             copy(out=grad[:], in_=acc[:])
             return grad
@@ -223,46 +231,51 @@ def tile_attend_gds_sq_kernel(tc, xT, wT, vT, wt, xm, offs, out):
         def store(b):
             nc.sync.dma_start(out[b * P : (b + 1) * P, :], windows[b][:])
 
-        weigh_late(0)
-        g0_late_words = sbuf("g0_late_words", [P, HALF, PACK], BF16)
-        gpsimd_copy(g0_late_words[:], g_rows[0].rearrange("p t i -> p i t"))
-        xm0_grouped = sbuf("xm0_grouped", [P, ROW_PASSES * P, PACK], BF16)
-        for h in range(ROW_PASSES):
-            interleave(nc.scalar.copy, xm0_grouped[:, h * P : (h + 1) * P, :], xm_raw[0][h][:])
-        weigh_late(1)
-        xm1_grouped = sbuf("xm1_grouped", [P, ROW_PASSES * P, PACK], BF16, "x1_codes")
-        for h in range(ROW_PASSES):
-            interleave(nc.scalar.copy, xm1_grouped[:, h * P : (h + 1) * P, :], xm_raw[1][h][:])
+        for t in range(PACK):
+            nc.scalar.activation(
+                out=g0_late_rows[:, t, :], in_=paired[t // 2][:, t % 2, :], func=COPY, scale=weights[:, 0, t : t + 1]
+            )
+        group_xm_gpsimd(0, 0)
+        gpsimd_copy(g0_late_words[:], g0_late_rows.rearrange("p t i -> p i t"))
+        for b, h in ((1, 0), (0, 1), (1, 1), (2, 0), (3, 0)):
+            group_xm(nc.scalar.copy, b, h)
 
-        for h in range(ROW_PASSES):
-            for c in range(2):
-                weigh_early(h, c)
-        quantize(g_ops[0], 0, HALF, g_words[0], E5M2)
-        quantize(xm_ops[0], 0, 2 * P, xm0_grouped[:], E4M3)
-        quantize(g_ops[1], 0, HALF, g_words[1], E5M2)
+        for c in range(2):
+            weigh_direct(0, c, back_words)
+        for c in range(2):
+            weigh_direct(1, c, g1_early_words)
+        quantize_xm(0)
+        quantize(g_ops[0], 0, HALF, back_words, E5M2)
+        quantize(g_ops[1], 0, HALF, g1_early_words, E5M2)
+        quantize_xm(1)
         early0 = product("early0", 0, 0, EARLY, nc.scalar.copy)
+        early1 = product("early1", 2, 1, EARLY, nc.scalar.copy)
         scatter_scalar(0, early0[:], EARLY)
+        scatter_scalar(1, early1[:], EARLY)
 
-        interleave(nc.vector.tensor_copy, g_words[1], g_rows[1])
+        group_xm_gpsimd(2, 1)
+        for c in range(2, 4):
+            weigh_direct(1, c, back_words)
         quantize(g_ops[0], HALF, N, g0_late_words[:], E5M2)
-        quantize(g_ops[1], HALF, N, g_words[1], E5M2)
-        late0 = product("late0", 1, 0, LATE, nc.scalar.copy)
-        scatter_scalar(0, late0[:], LATE)
+        quantize(g_ops[1], HALF, N, back_words, E5M2)
+        group_xm(nc.vector.tensor_copy, 3, 1)
+        quantize_xm(2)
+        late0 = product("late0", 1, 0, LATE, nc.vector.tensor_copy)
+        xm_ops.append(planes("xm3", ROW_PASSES * P, "back"))
+        quantize_xm(3)
+        scatter_vector(0, late0[:], LATE)
         store(0)
 
-        quantize(xm_ops[1], 0, 2 * P, xm1_grouped[:], E4M3)
-        rest_grouped = [sbuf(f"rest_grouped{h}", [P, 2 * P, PACK], BF16, tag) for h, tag in enumerate(("g1_words", "g1_rows"))]
-        for h in range(ROW_PASSES):
-            interleave(nc.vector.tensor_copy, rest_grouped[h][:], xm_raw[2][h][:])
-        quantize(rest_ops[0], 0, 2 * P, rest_grouped[0][:], E4M3)
-        grad1 = product("grad1", 2, 1, WHOLE, nc.vector.tensor_copy, f"xm_raw{2 * P}_1")
-        quantize(rest_ops[1], 0, 2 * P, rest_grouped[1][:], E4M3)
-        scatter_vector(1, grad1[:], WHOLE)
+        late1 = product("late1", 3, 1, LATE, nc.scalar.copy)
+        early2 = product("early2", 4, 2, EARLY, nc.vector.tensor_copy)
+        late2 = product("late2", 5, 2, LATE, nc.scalar.copy)
+        early3 = product("early3", 6, 3, EARLY, nc.vector.tensor_copy)
+        scatter_scalar(1, late1[:], LATE)
         store(1)
-        grad2 = product("grad2", 3, 2, WHOLE, nc.scalar.copy)
-        for s0, s1 in (EARLY, LATE):
-            scatter_scalar(2, grad2[:, s0:s1], (s0, s1))
+        scatter_vector(2, early2[:], EARLY)
+        scatter_vector(3, early3[:], EARLY)
+        late3 = product("late3", 7, 3, LATE, nc.scalar.copy)
+        scatter_scalar(2, late2[:], LATE)
         store(2)
-        grad3 = product("grad3", 4, 3, WHOLE, nc.vector.tensor_copy, f"xm_raw{2 * P}_1")
-        scatter_vector(3, grad3[:], WHOLE)
+        scatter_scalar(3, late3[:], LATE)
         store(3)

@@ -80,8 +80,8 @@ def tile_attend_gds_sq_kernel(tc, xT, wT, vT, wt, xm, offs, out):
         back = sbuf("back", [P, PACK * x_cut], F32)
         x1_front = front[:].rearrange("p (j r) -> p j r", j=PACK)
         x1_back = back[:].rearrange("p (j r) -> p j r", j=PACK)
-        xm_cuts = ((0, 2 * P), (2 * P, D))
-        xm_raw = [[sbuf(f"xm_raw{d0}_{h}", [P, PACK, d1 - d0], F32) for h in range(ROW_PASSES)] for d0, d1 in xm_cuts]
+        xm_cuts = ((0, 0, 2), (1, 0, 2), (0, 2, 4), (1, 2, 3), (1, 3, 4))
+        xm_raw = [sbuf(f"xm_raw{h}_{b0}", [P, PACK, (b1 - b0) * P], F32) for h, b0, b1 in xm_cuts]
         weights = sbuf("weights", [P, ROW_PASSES, PACK], F32)
 
         identity = sbuf("identity", [P, P], F32)
@@ -104,9 +104,8 @@ def tile_attend_gds_sq_kernel(tc, xT, wT, vT, wt, xm, offs, out):
             nc.sync.dma_start(w_planes[j][:], w_rows[:, j, :])
         nc.sync.dma_start(x1_front, x_rows[:, :, K_PASS : K_PASS + x_cut])
         nc.sync.dma_start(x1_back, x_rows[:, :, K_PASS + x_cut :])
-        for s, (d0, d1) in enumerate(xm_cuts):
-            for h in range(ROW_PASSES):
-                nc.sync.dma_start(xm_raw[s][h][:], xm_rows[h][:, :, d0:d1])
+        for raw, (h, b0, b1) in zip(xm_raw, xm_cuts):
+            nc.sync.dma_start(raw[:], xm_rows[h][:, :, b0 * P : b1 * P])
 
         windows = [keep.tile([P, T], F32, name=f"window{b}") for b in range(BLOCKS)]
         for b in range(BLOCKS):
@@ -176,23 +175,24 @@ def tile_attend_gds_sq_kernel(tc, xT, wT, vT, wt, xm, offs, out):
         score_passes(1, [v_op, w_op], True, True)
 
         g_ops = [planes(f"g{h}", N) for h in range(ROW_PASSES)]
-        xm_ops = [planes(f"xm{b}", ROW_PASSES * P) for b in range(BLOCKS - 1)]
-        first_grouped = sbuf("first_grouped", [P, 2 * ROW_PASSES * P, PACK], BF16, "x1_grouped")
-        rest_grouped = sbuf("rest_grouped", [P, 2 * ROW_PASSES * P, PACK], BF16)
+        xm_ops = [planes(f"xm{b}", ROW_PASSES * P) for b in range(BLOCKS)]
+        first_grouped = sbuf("first_grouped", [P, 2 * ROW_PASSES * P, PACK], BF16)
+        rest_grouped = sbuf("rest_grouped", [P, 3 * P + P // 2, PACK], BF16)
         back_words = back[:, 0 : HALF * PACK // 2].bitcast(BF16).rearrange("p (w j) -> p w j", j=PACK)
-        g1_early_words = rest_grouped[:, P : P + HALF, :]
+        g1_early_words = rest_grouped[:, 3 * P // 2 : 3 * P // 2 + HALF, :]
         g0_late_rows = front[:, 0 : PACK * HALF // 2].bitcast(BF16).rearrange("p (t i) -> p t i", t=PACK)
         g0_late_words = sbuf("g0_late_words", [P, HALF, PACK], BF16)
 
         def xm_place(b, h):
-            return ROW_PASSES * (b % 2) + (1 - h if b == 3 else h)
+            return 2 - h if b == 3 else ROW_PASSES * (b % 2) + h
 
         def xm_words(b, h):
             place = xm_place(b, h)
             return (first_grouped, rest_grouped)[b // 2][:, place * P : (place + 1) * P, :]
 
         def xm_source(b, h):
-            return xm_raw[b // 2][h][:, :, (b % 2) * P : (b % 2 + 1) * P]
+            raw, b0 = [(raw, b0) for raw, (g, b0, b1) in zip(xm_raw, xm_cuts) if g == h and b0 <= b < b1][0]
+            return raw[:, :, (b - b0) * P : (b - b0 + 1) * P]
 
         def group_xm(copy, b, h):
             interleave(copy, xm_words(b, h), xm_source(b, h))
@@ -201,7 +201,7 @@ def tile_attend_gds_sq_kernel(tc, xT, wT, vT, wt, xm, offs, out):
             gpsimd_copy(xm_words(b, h), xm_source(b, h).rearrange("p j d -> p d j"))
 
         def quantize_xm(b):
-            w0 = ROW_PASSES * P * (b % 2)
+            w0 = min(xm_place(b, h) for h in range(ROW_PASSES)) * P
             quantize(xm_ops[b], 0, ROW_PASSES * P, (first_grouped, rest_grouped)[b // 2][:, w0 : w0 + ROW_PASSES * P, :], E4M3)
 
         def weigh_direct(h, c, words):
@@ -216,7 +216,7 @@ def tile_attend_gds_sq_kernel(tc, xT, wT, vT, wt, xm, offs, out):
             s0, s1 = slots
             acc = psum.tile([P, s1 - s0], F32, name=name, tag=f"bank{bank}")
             for h in range(ROW_PASSES):
-                l0 = xm_place(b, h) % ROW_PASSES * P
+                l0 = (1 - h if b == 3 else h) * P
                 matmul(acc[:], xm_ops[b], l0, g_ops[h], s0, s1, E5M2, h == 0, h == ROW_PASSES - 1)
             grad = sbuf(name + "_sb", [P, s1 - s0], F32, tag)
             copy(out=grad[:], in_=acc[:])
@@ -235,9 +235,8 @@ def tile_attend_gds_sq_kernel(tc, xT, wT, vT, wt, xm, offs, out):
             nc.scalar.activation(
                 out=g0_late_rows[:, t, :], in_=paired[t // 2][:, t % 2, :], func=COPY, scale=weights[:, 0, t : t + 1]
             )
-        group_xm_gpsimd(0, 0)
         gpsimd_copy(g0_late_words[:], g0_late_rows.rearrange("p t i -> p i t"))
-        for b, h in ((1, 0), (0, 1), (1, 1), (2, 0), (3, 0)):
+        for b, h in ((0, 0), (1, 0), (0, 1), (1, 1), (2, 0)):
             group_xm(nc.scalar.copy, b, h)
 
         for c in range(2):
@@ -258,24 +257,23 @@ def tile_attend_gds_sq_kernel(tc, xT, wT, vT, wt, xm, offs, out):
             weigh_direct(1, c, back_words)
         quantize(g_ops[0], HALF, N, g0_late_words[:], E5M2)
         quantize(g_ops[1], HALF, N, back_words, E5M2)
-        group_xm(nc.vector.tensor_copy, 3, 1)
-        quantize_xm(2)
+        group_xm(nc.vector.tensor_copy, 3, 0)
         late0 = product("late0", 1, 0, LATE, nc.vector.tensor_copy)
-        xm_ops.append(planes("xm3", ROW_PASSES * P, "back"))
-        quantize_xm(3)
+        quantize_xm(2)
+        group_xm_gpsimd(3, 1)
         scatter_vector(0, late0[:], LATE)
         store(0)
 
-        late1 = product("late1", 3, 1, LATE, nc.scalar.copy)
-        early2 = product("early2", 4, 2, EARLY, nc.vector.tensor_copy)
-        late2 = product("late2", 5, 2, LATE, nc.scalar.copy)
-        early3 = product("early3", 6, 3, EARLY, nc.vector.tensor_copy)
-        scatter_scalar(1, late1[:], LATE)
+        late1 = product("late1", 3, 1, LATE, nc.scalar.copy, "xm_raw1_3")
+        early2 = product("early2", 4, 2, EARLY, nc.scalar.copy)
+        scatter_scalar(2, early2[:], EARLY)
+        quantize_xm(3)
+        scatter_vector(1, late1[:], LATE)
         store(1)
-        scatter_vector(2, early2[:], EARLY)
-        scatter_vector(3, early3[:], EARLY)
-        late3 = product("late3", 7, 3, LATE, nc.scalar.copy)
-        scatter_scalar(2, late2[:], LATE)
-        store(2)
-        scatter_scalar(3, late3[:], LATE)
-        store(3)
+        early3 = product("early3", 6, 3, EARLY, nc.scalar.copy)
+        scatter_scalar(3, early3[:], EARLY)
+        late2 = product("late2", 5, 2, LATE, nc.vector.tensor_copy)
+        late3 = product("late3", 7, 3, LATE, nc.vector.tensor_copy)
+        for b, late in ((2, late2), (3, late3)):
+            scatter_vector(b, late[:], LATE)
+            store(b)

@@ -81,7 +81,9 @@ def tile_attend_gds_sq_kernel(tc, xT, wT, vT, wt, xm, offs, out):
         x1_front = front[:].rearrange("p (j r) -> p j r", j=PACK)
         x1_back = back[:].rearrange("p (j r) -> p j r", j=PACK)
         xm_cuts = ((0, 0, 2), (1, 0, 2), (0, 2, 4), (1, 2, 3), (1, 3, 4))
-        xm_raw = [sbuf(f"xm_raw{h}_{b0}", [P, PACK, (b1 - b0) * P], F32) for h, b0, b1 in xm_cuts]
+        xm_raw = [sbuf(f"xm_raw{h}_{b0}", [P, PACK, (b1 - b0) * P], F32)[:] for h, b0, b1 in xm_cuts[:-1]]
+        last_piece = sbuf("last_piece", [P, 3 * HALF], F32)
+        xm_raw.append(last_piece[:, HALF // 2 : HALF // 2 + PACK * P].rearrange("p (j d) -> p j d", j=PACK))
         weights = sbuf("weights", [P, ROW_PASSES, PACK], F32)
 
         identity = sbuf("identity", [P, P], F32)
@@ -105,7 +107,7 @@ def tile_attend_gds_sq_kernel(tc, xT, wT, vT, wt, xm, offs, out):
         nc.sync.dma_start(x1_front, x_rows[:, :, K_PASS : K_PASS + x_cut])
         nc.sync.dma_start(x1_back, x_rows[:, :, K_PASS + x_cut :])
         for raw, (h, b0, b1) in zip(xm_raw, xm_cuts):
-            nc.sync.dma_start(raw[:], xm_rows[h][:, :, b0 * P : b1 * P])
+            nc.sync.dma_start(raw, xm_rows[h][:, :, b0 * P : b1 * P])
 
         windows = [keep.tile([P, T], F32, name=f"window{b}") for b in range(BLOCKS)]
         for b in range(BLOCKS):
@@ -175,7 +177,7 @@ def tile_attend_gds_sq_kernel(tc, xT, wT, vT, wt, xm, offs, out):
         score_passes(1, [v_op, w_op], True, True)
 
         g_ops = [planes(f"g{h}", N) for h in range(ROW_PASSES)]
-        xm_ops = [planes(f"xm{b}", ROW_PASSES * P) for b in range(BLOCKS)]
+        xm_ops = [planes(f"xm{b}", ROW_PASSES * P) for b in range(2)]
         first_grouped = sbuf("first_grouped", [P, 2 * ROW_PASSES * P, PACK], BF16)
         rest_grouped = sbuf("rest_grouped", [P, 3 * P + P // 2, PACK], BF16)
         back_words = back[:, 0 : HALF * PACK // 2].bitcast(BF16).rearrange("p (w j) -> p w j", j=PACK)
@@ -212,14 +214,25 @@ def tile_attend_gds_sq_kernel(tc, xT, wT, vT, wt, xm, offs, out):
                 MULT,
             )
 
-        def product(name, bank, b, slots, copy, tag=None):
+        def product(name, bank, b, slots, copy, grad=None):
             s0, s1 = slots
             acc = psum.tile([P, s1 - s0], F32, name=name, tag=f"bank{bank}")
             for h in range(ROW_PASSES):
                 l0 = (1 - h if b == 3 else h) * P
                 matmul(acc[:], xm_ops[b], l0, g_ops[h], s0, s1, E5M2, h == 0, h == ROW_PASSES - 1)
-            grad = sbuf(name + "_sb", [P, s1 - s0], F32, tag)
-            copy(out=grad[:], in_=acc[:])
+            if grad is None:
+                grad = sbuf(name + "_sb", [P, s1 - s0], F32)[:]
+            copy(out=grad, in_=acc[:])
+            return grad
+
+        def product_by_quarters(name, banks, slots, copy):
+            grad = sbuf(name + "_sb", [P, HALF], F32)
+            for c, bank in enumerate(banks):
+                s0 = slots[0] + c * P
+                acc = psum.tile([P, P], F32, name=f"{name}_{c}", tag=f"bank{bank}")
+                for h in range(ROW_PASSES):
+                    matmul(acc[:], xm_ops[0], h * P, g_ops[h], s0, s0 + P, E5M2, h == 0, h == ROW_PASSES - 1)
+                copy(out=grad[:, c * P : (c + 1) * P], in_=acc[:])
             return grad
 
         def scatter_vector(b, grad, slots):
@@ -241,39 +254,44 @@ def tile_attend_gds_sq_kernel(tc, xT, wT, vT, wt, xm, offs, out):
 
         for c in range(2):
             weigh_direct(0, c, back_words)
+        quantize(g_ops[0], 0, P, back_words[:, 0:P, :], E5M2)
         for c in range(2):
             weigh_direct(1, c, g1_early_words)
         quantize_xm(0)
-        quantize(g_ops[0], 0, HALF, back_words, E5M2)
-        quantize(g_ops[1], 0, HALF, g1_early_words, E5M2)
+        quantize(g_ops[0], P, HALF, back_words[:, P:HALF, :], E5M2)
+        for c in range(2):
+            quantize(g_ops[1], c * P, (c + 1) * P, g1_early_words[:, c * P : (c + 1) * P, :], E5M2)
         quantize_xm(1)
-        early0 = product("early0", 0, 0, EARLY, nc.scalar.copy)
+        early0 = product_by_quarters("early0", (0, 1), EARLY, nc.scalar.copy)
         early1 = product("early1", 2, 1, EARLY, nc.scalar.copy)
         scatter_scalar(0, early0[:], EARLY)
-        scatter_scalar(1, early1[:], EARLY)
+        scatter_scalar(1, early1, EARLY)
 
         group_xm_gpsimd(2, 1)
         for c in range(2, 4):
             weigh_direct(1, c, back_words)
         quantize(g_ops[0], HALF, N, g0_late_words[:], E5M2)
-        quantize(g_ops[1], HALF, N, back_words, E5M2)
+        for c in range(2):
+            quantize(g_ops[1], HALF + c * P, HALF + (c + 1) * P, back_words[:, c * P : (c + 1) * P, :], E5M2)
         group_xm(nc.vector.tensor_copy, 3, 0)
-        late0 = product("late0", 1, 0, LATE, nc.vector.tensor_copy)
+        late0 = product_by_quarters("late0", (4, 5), LATE, nc.vector.tensor_copy)
+        xm_ops.append(planes("xm2", ROW_PASSES * P, "xm0_codes"))
+        xm_ops.append(planes("xm3", ROW_PASSES * P))
         quantize_xm(2)
         group_xm_gpsimd(3, 1)
         scatter_vector(0, late0[:], LATE)
         store(0)
 
-        late1 = product("late1", 3, 1, LATE, nc.scalar.copy, "xm_raw1_3")
-        early2 = product("early2", 4, 2, EARLY, nc.scalar.copy)
-        scatter_scalar(2, early2[:], EARLY)
+        late1 = product("late1", 3, 1, LATE, nc.scalar.copy, last_piece[:, 0:HALF])
+        early2 = product("early2", 0, 2, EARLY, nc.scalar.copy, last_piece[:, HALF : 2 * HALF])
+        late2 = product("late2", 1, 2, LATE, nc.scalar.copy, last_piece[:, 2 * HALF :])
+        scatter_scalar(2, early2, EARLY)
         quantize_xm(3)
-        scatter_vector(1, late1[:], LATE)
+        scatter_vector(1, late1, LATE)
         store(1)
-        early3 = product("early3", 6, 3, EARLY, nc.scalar.copy)
-        scatter_scalar(3, early3[:], EARLY)
-        late2 = product("late2", 5, 2, LATE, nc.vector.tensor_copy)
+        early3 = product("early3", 6, 3, EARLY, nc.vector.tensor_copy)
         late3 = product("late3", 7, 3, LATE, nc.vector.tensor_copy)
+        scatter_scalar(3, early3, EARLY)
         for b, late in ((2, late2), (3, late3)):
-            scatter_vector(b, late[:], LATE)
+            scatter_vector(b, late, LATE)
             store(b)

@@ -80,10 +80,7 @@ def tile_attend_gds_sq_kernel(tc, xT, wT, vT, wt, xm, offs, out):
         back = sbuf("back", [P, PACK * x_cut], F32)
         x1_front = front[:].rearrange("p (j r) -> p j r", j=PACK)
         x1_back = back[:].rearrange("p (j r) -> p j r", j=PACK)
-        xm_cuts = ((0, 0, 2), (1, 0, 2), (0, 2, 4), (1, 2, 3), (1, 3, 4))
-        xm_raw = [sbuf(f"xm_raw{h}_{b0}", [P, PACK, (b1 - b0) * P], F32)[:] for h, b0, b1 in xm_cuts[:-1]]
-        last_piece = sbuf("last_piece", [P, 3 * HALF], F32)
-        xm_raw.append(last_piece[:, HALF // 2 : HALF // 2 + PACK * P].rearrange("p (j d) -> p j d", j=PACK))
+        xm_raw = [[sbuf(f"xm_raw{b}_{h}", [P, PACK, P], F32) for h in range(ROW_PASSES)] for b in range(BLOCKS)]
         weights = sbuf("weights", [P, ROW_PASSES, PACK], F32)
 
         identity = sbuf("identity", [P, P], F32)
@@ -106,8 +103,9 @@ def tile_attend_gds_sq_kernel(tc, xT, wT, vT, wt, xm, offs, out):
             nc.sync.dma_start(w_planes[j][:], w_rows[:, j, :])
         nc.sync.dma_start(x1_front, x_rows[:, :, K_PASS : K_PASS + x_cut])
         nc.sync.dma_start(x1_back, x_rows[:, :, K_PASS + x_cut :])
-        for raw, (h, b0, b1) in zip(xm_raw, xm_cuts):
-            nc.sync.dma_start(raw, xm_rows[h][:, :, b0 * P : b1 * P])
+        for b in range(BLOCKS):
+            for h in range(ROW_PASSES):
+                nc.sync.dma_start(xm_raw[b][h][:], xm_rows[h][:, :, b * P : (b + 1) * P])
 
         windows = [keep.tile([P, T], F32, name=f"window{b}") for b in range(BLOCKS)]
         for b in range(BLOCKS):
@@ -179,22 +177,21 @@ def tile_attend_gds_sq_kernel(tc, xT, wT, vT, wt, xm, offs, out):
         g_ops = [planes(f"g{h}", N) for h in range(ROW_PASSES)]
         xm_ops = [planes(f"xm{b}", ROW_PASSES * P) for b in range(2)]
         first_grouped = sbuf("first_grouped", [P, 2 * ROW_PASSES * P, PACK], BF16)
-        rest_grouped = sbuf("rest_grouped", [P, 3 * P + P // 2, PACK], BF16)
+        rest_grouped = sbuf("rest_grouped", [P, 2 * ROW_PASSES * P, PACK], BF16)
         back_words = back[:, 0 : HALF * PACK // 2].bitcast(BF16).rearrange("p (w j) -> p w j", j=PACK)
         g1_early_words = rest_grouped[:, 3 * P // 2 : 3 * P // 2 + HALF, :]
         g0_late_rows = front[:, 0 : PACK * HALF // 2].bitcast(BF16).rearrange("p (t i) -> p t i", t=PACK)
         g0_late_words = sbuf("g0_late_words", [P, HALF, PACK], BF16)
 
         def xm_place(b, h):
-            return 2 - h if b == 3 else ROW_PASSES * (b % 2) + h
+            return ROW_PASSES * (b % 2) + h
 
         def xm_words(b, h):
             place = xm_place(b, h)
             return (first_grouped, rest_grouped)[b // 2][:, place * P : (place + 1) * P, :]
 
         def xm_source(b, h):
-            raw, b0 = [(raw, b0) for raw, (g, b0, b1) in zip(xm_raw, xm_cuts) if g == h and b0 <= b < b1][0]
-            return raw[:, :, (b - b0) * P : (b - b0 + 1) * P]
+            return xm_raw[b][h][:]
 
         def group_xm(copy, b, h):
             interleave(copy, xm_words(b, h), xm_source(b, h))
@@ -218,7 +215,7 @@ def tile_attend_gds_sq_kernel(tc, xT, wT, vT, wt, xm, offs, out):
             s0, s1 = slots
             acc = psum.tile([P, s1 - s0], F32, name=name, tag=f"bank{bank}")
             for h in range(ROW_PASSES):
-                l0 = (1 - h if b == 3 else h) * P
+                l0 = h * P
                 matmul(acc[:], xm_ops[b], l0, g_ops[h], s0, s1, E5M2, h == 0, h == ROW_PASSES - 1)
             if grad is None:
                 grad = sbuf(name + "_sb", [P, s1 - s0], F32)[:]
@@ -249,7 +246,7 @@ def tile_attend_gds_sq_kernel(tc, xT, wT, vT, wt, xm, offs, out):
                 out=g0_late_rows[:, t, :], in_=paired[t // 2][:, t % 2, :], func=COPY, scale=weights[:, 0, t : t + 1]
             )
         gpsimd_copy(g0_late_words[:], g0_late_rows.rearrange("p t i -> p i t"))
-        for b, h in ((0, 0), (1, 0), (0, 1), (1, 1), (2, 0)):
+        for b, h in ((0, 0), (0, 1), (1, 0), (1, 1), (2, 0)):
             group_xm(nc.scalar.copy, b, h)
 
         for c in range(2):
@@ -257,8 +254,8 @@ def tile_attend_gds_sq_kernel(tc, xT, wT, vT, wt, xm, offs, out):
         quantize(g_ops[0], 0, P, back_words[:, 0:P, :], E5M2)
         for c in range(2):
             weigh_direct(1, c, g1_early_words)
-        quantize_xm(0)
         quantize(g_ops[0], P, HALF, back_words[:, P:HALF, :], E5M2)
+        quantize_xm(0)
         for c in range(2):
             quantize(g_ops[1], c * P, (c + 1) * P, g1_early_words[:, c * P : (c + 1) * P, :], E5M2)
         quantize_xm(1)
@@ -273,19 +270,19 @@ def tile_attend_gds_sq_kernel(tc, xT, wT, vT, wt, xm, offs, out):
         quantize(g_ops[0], HALF, N, g0_late_words[:], E5M2)
         for c in range(2):
             quantize(g_ops[1], HALF + c * P, HALF + (c + 1) * P, back_words[:, c * P : (c + 1) * P, :], E5M2)
-        group_xm(nc.vector.tensor_copy, 3, 0)
+        for h in range(ROW_PASSES):
+            group_xm(nc.vector.tensor_copy, 3, h)
         late0 = product_by_quarters("late0", (4, 5), LATE, nc.vector.tensor_copy)
         xm_ops.append(planes("xm2", ROW_PASSES * P, "xm0_codes"))
-        xm_ops.append(planes("xm3", ROW_PASSES * P))
         quantize_xm(2)
-        group_xm_gpsimd(3, 1)
         scatter_vector(0, late0[:], LATE)
         store(0)
 
-        late1 = product("late1", 3, 1, LATE, nc.scalar.copy, last_piece[:, 0:HALF])
-        early2 = product("early2", 0, 2, EARLY, nc.scalar.copy, last_piece[:, HALF : 2 * HALF])
-        late2 = product("late2", 1, 2, LATE, nc.scalar.copy, last_piece[:, 2 * HALF :])
+        late1 = product("late1", 3, 1, LATE, nc.scalar.copy)
+        early2 = product("early2", 0, 2, EARLY, nc.scalar.copy)
+        late2 = product("late2", 1, 2, LATE, nc.scalar.copy)
         scatter_scalar(2, early2, EARLY)
+        xm_ops.append(planes("xm3", ROW_PASSES * P, "xm1_codes"))
         quantize_xm(3)
         scatter_vector(1, late1, LATE)
         store(1)

@@ -94,6 +94,8 @@ def tile_attend_gds_sq_kernel(tc, xT, wT, vT, wt, xm, offs, out):
         for t in range(PACK):
             nc.tensor.transpose(turned[:, t, :], weight_rows[:, t::PACK], identity[:])
         nc.scalar.copy(out=weights[:], in_=turned[:, :, 0:ROW_PASSES].rearrange("p t h -> p h t"))
+        early_weights = sbuf("early_weights", [P, 1, PACK], F32)
+        nc.scalar.copy(out=early_weights[:], in_=turned[:, :, 1:2].rearrange("p t h -> p h t"))
 
         nc.sync.dma_start(v_pairs[0][:], v_rows[:, 0:2, :])
         nc.sync.dma_start(offsets[:], offs)
@@ -174,69 +176,64 @@ def tile_attend_gds_sq_kernel(tc, xT, wT, vT, wt, xm, offs, out):
             quantize(x_ops[1], 2 * u * P, (2 * u + 2) * P, x_grouped[1][:, 2 * u * P : (2 * u + 2) * P, :], E4M3)
         score_passes(1, [v_op, w_op], True, True)
 
-        g_ops = [planes(f"g{h}", N) for h in range(ROW_PASSES)]
-        xm_ops = [planes(f"xm{b}", ROW_PASSES * P) for b in range(2)]
-        first_grouped = sbuf("first_grouped", [P, 2 * ROW_PASSES * P, PACK], BF16)
-        rest_grouped = sbuf("rest_grouped", [P, 2 * ROW_PASSES * P, PACK], BF16)
-        back_words = back[:, 0 : HALF * PACK // 2].bitcast(BF16).rearrange("p (w j) -> p w j", j=PACK)
-        g1_early_words = rest_grouped[:, 3 * P // 2 : 3 * P // 2 + HALF, :]
+        g_op = planes("g", ROW_PASSES * N)
+        back_words = back[:].bitcast(BF16).rearrange("p (w j) -> p w j", j=PACK)
+        late_words = sbuf("late_words", [P, ROW_PASSES * HALF, PACK], BF16)
         g0_late_rows = front[:, 0 : PACK * HALF // 2].bitcast(BF16).rearrange("p (t i) -> p t i", t=PACK)
-        g0_late_words = sbuf("g0_late_words", [P, HALF, PACK], BF16)
+        first_grouped = sbuf("first_grouped", [P, 5 * P, PACK], BF16)
+        xm_grouped = [
+            first_grouped[:, 0 : 2 * P, :],
+            first_grouped[:, 2 * P : 4 * P, :],
+            first_grouped[:, 3 * P :, :],
+            back_words[:, 2 * P :, :],
+        ]
+        xm_ops = {}
+
+        def g_words(c, h0, h1):
+            w0 = (c % 2) * ROW_PASSES * P
+            return (back_words, late_words)[c // 2][:, w0 + h0 * P : w0 + h1 * P, :]
 
         def xm_place(b, h):
-            return ROW_PASSES * (b % 2) + h
+            return (1 - h if b == 2 else h) * P
 
         def xm_words(b, h):
-            place = xm_place(b, h)
-            return (first_grouped, rest_grouped)[b // 2][:, place * P : (place + 1) * P, :]
-
-        def xm_source(b, h):
-            return xm_raw[b][h][:]
+            return xm_grouped[b][:, xm_place(b, h) : xm_place(b, h) + P, :]
 
         def group_xm(copy, b, h):
-            interleave(copy, xm_words(b, h), xm_source(b, h))
+            interleave(copy, xm_words(b, h), xm_raw[b][h][:])
 
-        def group_xm_gpsimd(b, h):
-            gpsimd_copy(xm_words(b, h), xm_source(b, h).rearrange("p j d -> p d j"))
+        def quantize_xm(b, codes_tag=None):
+            xm_ops[b] = planes(f"xm{b}", ROW_PASSES * P, codes_tag)
+            quantize(xm_ops[b], 0, ROW_PASSES * P, xm_grouped[b], E4M3)
 
-        def quantize_xm(b):
-            w0 = min(xm_place(b, h) for h in range(ROW_PASSES)) * P
-            quantize(xm_ops[b], 0, ROW_PASSES * P, (first_grouped, rest_grouped)[b // 2][:, w0 : w0 + ROW_PASSES * P, :], E4M3)
+        def quantize_g(c):
+            quantize(g_op, c * ROW_PASSES * P, (c + 1) * ROW_PASSES * P, g_words(c, 0, ROW_PASSES), E5M2)
 
-        def weigh_direct(h, c, words):
+        def weigh_direct(h, c, factors):
             nc.vector.tensor_tensor(
-                words[:, (c % 2) * P : (c % 2 + 1) * P, :],
-                direct[h][c][:].rearrange("p t i -> p i t"),
-                weights[:, h : h + 1, :].to_broadcast([P, P, PACK]),
-                MULT,
+                g_words(c, h, h + 1), direct[h][c][:].rearrange("p t i -> p i t"), factors.to_broadcast([P, P, PACK]), MULT
             )
 
-        def product(name, bank, b, slots, copy, grad=None):
-            s0, s1 = slots
-            acc = psum.tile([P, s1 - s0], F32, name=name, tag=f"bank{bank}")
+        def multiply(acc, b, c):
             for h in range(ROW_PASSES):
-                l0 = h * P
-                matmul(acc[:], xm_ops[b], l0, g_ops[h], s0, s1, E5M2, h == 0, h == ROW_PASSES - 1)
-            if grad is None:
-                grad = sbuf(name + "_sb", [P, s1 - s0], F32)[:]
-            copy(out=grad, in_=acc[:])
-            return grad
+                g0 = (c * ROW_PASSES + h) * P
+                matmul(acc, xm_ops[b], xm_place(b, h), g_op, g0, g0 + P, E5M2, h == 0, h == ROW_PASSES - 1)
 
-        def product_by_quarters(name, banks, slots, copy):
+        def product(name, banks, b, slots, copy):
             grad = sbuf(name + "_sb", [P, HALF], F32)
-            for c, bank in enumerate(banks):
-                s0 = slots[0] + c * P
-                acc = psum.tile([P, P], F32, name=f"{name}_{c}", tag=f"bank{bank}")
-                for h in range(ROW_PASSES):
-                    matmul(acc[:], xm_ops[0], h * P, g_ops[h], s0, s0 + P, E5M2, h == 0, h == ROW_PASSES - 1)
-                copy(out=grad[:, c * P : (c + 1) * P], in_=acc[:])
+            width = HALF // len(banks)
+            for n, bank in enumerate(banks):
+                acc = psum.tile([P, width], F32, name=f"{name}_{n}", tag=f"bank{bank}")
+                for s0 in range(0, width, P):
+                    multiply(acc[:, s0 : s0 + P], b, (slots[0] + n * width + s0) // P)
+                copy(out=grad[:, n * width : (n + 1) * width], in_=acc[:])
             return grad
 
         def scatter_vector(b, grad, slots):
-            nc.vector.tensor_copy(listed(windows[b][:], slots), grad)
+            nc.vector.tensor_copy(listed(windows[b][:], slots), grad[:])
 
         def scatter_scalar(b, grad, slots):
-            nc.scalar.activation(out=listed(windows[b][:], slots), in_=grad, func=COPY)
+            nc.scalar.activation(out=listed(windows[b][:], slots), in_=grad[:], func=COPY)
 
         def store(b):
             nc.sync.dma_start(out[b * P : (b + 1) * P, :], windows[b][:])
@@ -245,49 +242,47 @@ def tile_attend_gds_sq_kernel(tc, xT, wT, vT, wt, xm, offs, out):
             nc.scalar.activation(
                 out=g0_late_rows[:, t, :], in_=paired[t // 2][:, t % 2, :], func=COPY, scale=weights[:, 0, t : t + 1]
             )
-        gpsimd_copy(g0_late_words[:], g0_late_rows.rearrange("p t i -> p i t"))
+        gpsimd_copy(
+            late_words[:].rearrange("p (c h i) t -> p c h i t", c=2, h=ROW_PASSES)[:, :, 0],
+            g0_late_rows.rearrange("p t (c i) -> p c i t", c=2),
+        )
         for b, h in ((0, 0), (0, 1), (1, 0), (1, 1), (2, 0)):
             group_xm(nc.scalar.copy, b, h)
 
         for c in range(2):
-            weigh_direct(0, c, back_words)
-        quantize(g_ops[0], 0, P, back_words[:, 0:P, :], E5M2)
+            weigh_direct(0, c, weights[:, 0:1, :])
         for c in range(2):
-            weigh_direct(1, c, g1_early_words)
-        quantize(g_ops[0], P, HALF, back_words[:, P:HALF, :], E5M2)
-        quantize_xm(0)
-        for c in range(2):
-            quantize(g_ops[1], c * P, (c + 1) * P, g1_early_words[:, c * P : (c + 1) * P, :], E5M2)
+            weigh_direct(1, c, early_weights[:])
+        quantize_g(0)
+        quantize_xm(0, "early_weights")
+        quantize_g(1)
         quantize_xm(1)
-        early0 = product_by_quarters("early0", (0, 1), EARLY, nc.scalar.copy)
-        early1 = product("early1", 2, 1, EARLY, nc.scalar.copy)
-        scatter_scalar(0, early0[:], EARLY)
+        early0 = product("early0", (0, 1), 0, EARLY, nc.scalar.copy)
+        early1 = product("early1", (2,), 1, EARLY, nc.scalar.copy)
+        scatter_scalar(0, early0, EARLY)
         scatter_scalar(1, early1, EARLY)
 
-        group_xm_gpsimd(2, 1)
+        gpsimd_copy(xm_words(2, 1), xm_raw[2][1][:].rearrange("p j d -> p d j"))
         for c in range(2, 4):
-            weigh_direct(1, c, back_words)
-        quantize(g_ops[0], HALF, N, g0_late_words[:], E5M2)
-        for c in range(2):
-            quantize(g_ops[1], HALF + c * P, HALF + (c + 1) * P, back_words[:, c * P : (c + 1) * P, :], E5M2)
+            weigh_direct(1, c, weights[:, 1:2, :])
+        for c in range(2, 4):
+            quantize_g(c)
         for h in range(ROW_PASSES):
             group_xm(nc.vector.tensor_copy, 3, h)
-        late0 = product_by_quarters("late0", (4, 5), LATE, nc.vector.tensor_copy)
-        xm_ops.append(planes("xm2", ROW_PASSES * P, "xm0_codes"))
-        quantize_xm(2)
-        scatter_vector(0, late0[:], LATE)
+        late0 = product("late0", (4, 5), 0, LATE, nc.vector.tensor_copy)
+        quantize_xm(2, "early_weights")
+        scatter_vector(0, late0, LATE)
         store(0)
 
-        late1 = product("late1", 3, 1, LATE, nc.scalar.copy)
-        early2 = product("early2", 0, 2, EARLY, nc.scalar.copy)
-        late2 = product("late2", 1, 2, LATE, nc.scalar.copy)
+        late1 = product("late1", (3,), 1, LATE, nc.scalar.copy)
+        early2 = product("early2", (0,), 2, EARLY, nc.scalar.copy)
+        late2 = product("late2", (1,), 2, LATE, nc.scalar.copy)
         scatter_scalar(2, early2, EARLY)
-        xm_ops.append(planes("xm3", ROW_PASSES * P, "xm1_codes"))
-        quantize_xm(3)
+        quantize_xm(3, "xm1_codes")
         scatter_vector(1, late1, LATE)
         store(1)
-        early3 = product("early3", 6, 3, EARLY, nc.vector.tensor_copy)
-        late3 = product("late3", 7, 3, LATE, nc.vector.tensor_copy)
+        early3 = product("early3", (6,), 3, EARLY, nc.vector.tensor_copy)
+        late3 = product("late3", (7,), 3, LATE, nc.vector.tensor_copy)
         scatter_scalar(3, early3, EARLY)
         for b, late in ((2, late2), (3, late3)):
             scatter_vector(b, late, LATE)

@@ -80,7 +80,10 @@ def tile_attend_gds_sq_kernel(tc, xT, wT, vT, wt, xm, offs, out):
         back = sbuf("back", [P, PACK * x_cut], F32)
         x1_front = front[:].rearrange("p (j r) -> p j r", j=PACK)
         x1_back = back[:].rearrange("p (j r) -> p j r", j=PACK)
-        xm_raw = [[sbuf(f"xm_raw{b}_{h}", [P, PACK, P], F32) for h in range(ROW_PASSES)] for b in range(BLOCKS)]
+        pieces = [(b, h) for b in range(BLOCKS) for h in range(ROW_PASSES)]
+        xm_raw = {(b, h): sbuf(f"xm_raw{b}_{h}", [P, PACK, P], F32)[:] for b, h in pieces[:-1]}
+        last_piece = sbuf("last_piece", [P, 3 * HALF], F32)
+        xm_raw[pieces[-1]] = last_piece[:, HALF // 2 : HALF // 2 + PACK * P].rearrange("p (j d) -> p j d", j=PACK)
         weights = sbuf("weights", [P, ROW_PASSES, PACK], F32)
 
         identity = sbuf("identity", [P, P], F32)
@@ -105,9 +108,8 @@ def tile_attend_gds_sq_kernel(tc, xT, wT, vT, wt, xm, offs, out):
             nc.sync.dma_start(w_planes[j][:], w_rows[:, j, :])
         nc.sync.dma_start(x1_front, x_rows[:, :, K_PASS : K_PASS + x_cut])
         nc.sync.dma_start(x1_back, x_rows[:, :, K_PASS + x_cut :])
-        for b in range(BLOCKS):
-            for h in range(ROW_PASSES):
-                nc.sync.dma_start(xm_raw[b][h][:], xm_rows[h][:, :, b * P : (b + 1) * P])
+        for b, h in pieces:
+            nc.sync.dma_start(xm_raw[b, h], xm_rows[h][:, :, b * P : (b + 1) * P])
 
         windows = [keep.tile([P, T], F32, name=f"window{b}") for b in range(BLOCKS)]
         for b in range(BLOCKS):
@@ -185,7 +187,7 @@ def tile_attend_gds_sq_kernel(tc, xT, wT, vT, wt, xm, offs, out):
             first_grouped[:, 0 : 2 * P, :],
             first_grouped[:, 2 * P : 4 * P, :],
             first_grouped[:, 3 * P :, :],
-            back_words[:, 2 * P :, :],
+            first_grouped[:, 3 * P :, :],
         ]
         xm_ops = {}
 
@@ -200,7 +202,10 @@ def tile_attend_gds_sq_kernel(tc, xT, wT, vT, wt, xm, offs, out):
             return xm_grouped[b][:, xm_place(b, h) : xm_place(b, h) + P, :]
 
         def group_xm(copy, b, h):
-            interleave(copy, xm_words(b, h), xm_raw[b][h][:])
+            interleave(copy, xm_words(b, h), xm_raw[b, h])
+
+        def group_xm_gpsimd(b, h):
+            gpsimd_copy(xm_words(b, h), xm_raw[b, h].rearrange("p j d -> p d j"))
 
         def quantize_xm(b, codes_tag=None):
             xm_ops[b] = planes(f"xm{b}", ROW_PASSES * P, codes_tag)
@@ -219,8 +224,9 @@ def tile_attend_gds_sq_kernel(tc, xT, wT, vT, wt, xm, offs, out):
                 g0 = (c * ROW_PASSES + h) * P
                 matmul(acc, xm_ops[b], xm_place(b, h), g_op, g0, g0 + P, E5M2, h == 0, h == ROW_PASSES - 1)
 
-        def product(name, banks, b, slots, copy):
-            grad = sbuf(name + "_sb", [P, HALF], F32)
+        def product(name, banks, b, slots, copy, grad=None):
+            if grad is None:
+                grad = sbuf(name + "_sb", [P, HALF], F32)[:]
             width = HALF // len(banks)
             for n, bank in enumerate(banks):
                 acc = psum.tile([P, width], F32, name=f"{name}_{n}", tag=f"bank{bank}")
@@ -230,10 +236,10 @@ def tile_attend_gds_sq_kernel(tc, xT, wT, vT, wt, xm, offs, out):
             return grad
 
         def scatter_vector(b, grad, slots):
-            nc.vector.tensor_copy(listed(windows[b][:], slots), grad[:])
+            nc.vector.tensor_copy(listed(windows[b][:], slots), grad)
 
         def scatter_scalar(b, grad, slots):
-            nc.scalar.activation(out=listed(windows[b][:], slots), in_=grad[:], func=COPY)
+            nc.scalar.activation(out=listed(windows[b][:], slots), in_=grad, func=COPY)
 
         def store(b):
             nc.sync.dma_start(out[b * P : (b + 1) * P, :], windows[b][:])
@@ -258,31 +264,31 @@ def tile_attend_gds_sq_kernel(tc, xT, wT, vT, wt, xm, offs, out):
         quantize_g(1)
         quantize_xm(1)
         early0 = product("early0", (0, 1), 0, EARLY, nc.scalar.copy)
-        early1 = product("early1", (2,), 1, EARLY, nc.scalar.copy)
         scatter_scalar(0, early0, EARLY)
-        scatter_scalar(1, early1, EARLY)
 
-        gpsimd_copy(xm_words(2, 1), xm_raw[2][1][:].rearrange("p j d -> p d j"))
+        group_xm_gpsimd(2, 1)
         for c in range(2, 4):
             weigh_direct(1, c, weights[:, 1:2, :])
         for c in range(2, 4):
             quantize_g(c)
+        early1 = product("early1", (2,), 1, EARLY, nc.vector.tensor_copy)
+        scatter_scalar(1, early1, EARLY)
+        quantize_xm(2)
         for h in range(ROW_PASSES):
-            group_xm(nc.vector.tensor_copy, 3, h)
+            group_xm_gpsimd(3, h)
         late0 = product("late0", (4, 5), 0, LATE, nc.vector.tensor_copy)
-        quantize_xm(2, "early_weights")
         scatter_vector(0, late0, LATE)
         store(0)
 
-        late1 = product("late1", (3,), 1, LATE, nc.scalar.copy)
-        early2 = product("early2", (0,), 2, EARLY, nc.scalar.copy)
-        late2 = product("late2", (1,), 2, LATE, nc.scalar.copy)
+        late1 = product("late1", (3,), 1, LATE, nc.scalar.copy, last_piece[:, 0:HALF])
+        early2 = product("early2", (0,), 2, EARLY, nc.scalar.copy, last_piece[:, HALF : 2 * HALF])
         scatter_scalar(2, early2, EARLY)
-        quantize_xm(3, "xm1_codes")
+        quantize_xm(3)
         scatter_vector(1, late1, LATE)
         store(1)
         early3 = product("early3", (6,), 3, EARLY, nc.vector.tensor_copy)
-        late3 = product("late3", (7,), 3, LATE, nc.vector.tensor_copy)
+        late2 = product("late2", (1,), 2, LATE, nc.vector.tensor_copy, last_piece[:, 2 * HALF :])
+        late3 = product("late3", (7,), 3, LATE, nc.scalar.copy)
         scatter_scalar(3, early3, EARLY)
         for b, late in ((2, late2), (3, late3)):
             scatter_vector(b, late, LATE)

@@ -271,23 +271,24 @@ def tile_attend_gds_sq_kernel(tc, xT, wT, vT, wt, xm, offs, out):
             weigh_direct(1, c, weights[:, 1:2, :])
         for c in range(2, 4):
             quantize_g(c)
-        early1 = product("early1", (2,), 1, EARLY, nc.vector.tensor_copy)
-        scatter_scalar(1, early1, EARLY)
         quantize_xm(2)
         for h in range(ROW_PASSES):
             group_xm_gpsimd(3, h)
+        early1 = product("early1", (2,), 1, EARLY, nc.vector.tensor_copy)
+        scatter_scalar(1, early1, EARLY)
         late0 = product("late0", (4, 5), 0, LATE, nc.vector.tensor_copy)
         scatter_vector(0, late0, LATE)
         store(0)
 
         late1 = product("late1", (3,), 1, LATE, nc.scalar.copy, last_piece[:, 0:HALF])
         early2 = product("early2", (0,), 2, EARLY, nc.scalar.copy, last_piece[:, HALF : 2 * HALF])
-        scatter_scalar(2, early2, EARLY)
         quantize_xm(3)
+        spent_words = xm_words(3, 0).rearrange("p w j -> p (w j)").bitcast(F32)
+        late2 = product("late2", (1,), 2, LATE, nc.scalar.copy, spent_words)
+        scatter_scalar(2, early2, EARLY)
         scatter_vector(1, late1, LATE)
         store(1)
         early3 = product("early3", (6,), 3, EARLY, nc.vector.tensor_copy)
-        late2 = product("late2", (1,), 2, LATE, nc.vector.tensor_copy, last_piece[:, 2 * HALF :])
         late3 = product("late3", (7,), 3, LATE, nc.scalar.copy)
         scatter_scalar(3, early3, EARLY)
         for b, late in ((2, late2), (3, late3)):

@@ -38,7 +38,7 @@ def tile_attend_gds_sq_kernel(tc, xT, wT, vT, wt, xm, offs, out):
         def sbuf(name, shape, dtype, tag=None):
             return keep.tile(shape, dtype, name=name, tag=tag or name, align_bytes=64)
 
-        def planes(name, width, codes_tag=None):
+        def operand(name, width, codes_tag=None):
             return sbuf(name + "_codes", [P, width], U32, codes_tag), sbuf(name + "_scales", [P, width], U8)
 
         def quantize(op, c0, c1, grouped, fmt):
@@ -60,8 +60,8 @@ def tile_attend_gds_sq_kernel(tc, xT, wT, vT, wt, xm, offs, out):
         def listed(window, slots):
             return window.indirect(offsets[:, slots[0] // LIST_ROWS : slots[1] // LIST_ROWS])
 
-        def interleave(copy, grouped, rows):
-            copy(out=grouped.rearrange("p (c i) j -> p c j i", i=PACK), in_=rows.rearrange("p j (c i) -> p c j i", i=PACK))
+        def four_by_four(grouped, rows):
+            return grouped.rearrange("p (c i) j -> p c j i", i=PACK), rows.rearrange("p j (c i) -> p c j i", i=PACK)
 
         def gpsimd_copy(out, in_):
             nc.gpsimd.tensor_scalar(out=out, in0=in_, scalar1=1.0, scalar2=0.0, op0=MULT, op1=ADD)
@@ -74,18 +74,18 @@ def tile_attend_gds_sq_kernel(tc, xT, wT, vT, wt, xm, offs, out):
 
         v_pairs = [sbuf(f"v_pair{u}", [P, 2, T], F32) for u in range(2)]
         w_planes = [sbuf(f"w_plane{j}", [P, T], F32) for j in range(PACK)]
-        x_cut = K_PASS // 2
         x0_raw = sbuf("x0_raw", [P, PACK, K_PASS], F32)
+        x_cut = K_PASS // 2
         front = sbuf("front", [P, PACK * x_cut], F32)
         back = sbuf("back", [P, PACK * x_cut], F32)
         x1_front = front[:].rearrange("p (j r) -> p j r", j=PACK)
         x1_back = back[:].rearrange("p (j r) -> p j r", j=PACK)
         pieces = [(b, h) for b in range(BLOCKS) for h in range(ROW_PASSES)]
         xm_raw = {(b, h): sbuf(f"xm_raw{b}_{h}", [P, PACK, P], F32)[:] for b, h in pieces[:-1]}
-        last_piece = sbuf("last_piece", [P, 3 * HALF], F32)
-        xm_raw[pieces[-1]] = last_piece[:, HALF // 2 : HALF // 2 + PACK * P].rearrange("p (j d) -> p j d", j=PACK)
-        weights = sbuf("weights", [P, ROW_PASSES, PACK], F32)
+        last_piece = sbuf("last_piece", [P, PACK * P], F32)
+        xm_raw[pieces[-1]] = last_piece[:].rearrange("p (j d) -> p j d", j=PACK)
 
+        weights = sbuf("weights", [P, ROW_PASSES, PACK], F32)
         identity = sbuf("identity", [P, P], F32)
         make_identity(nc, identity[:])
         weight_rows = sbuf("weight_rows", [P, K_PASS], F32)
@@ -116,23 +116,23 @@ def tile_attend_gds_sq_kernel(tc, xT, wT, vT, wt, xm, offs, out):
             engine = nc.vector if b < BLOCKS // 2 else nc.gpsimd
             engine.memset(windows[b][:], 0.0)
 
-        direct = [
-            [psum.tile([P, PACK, P], F32, name=f"direct{h}_{c}", tag=f"bank{4 * h + c}") for c in range(2 + 2 * h)]
-            for h in range(ROW_PASSES)
+        quarter_banks = [
+            [psum.tile([P, PACK, P], F32, name=f"scores{h}_{c}", tag=f"bank{4 * h + c}") for c in range(quarters)]
+            for h, quarters in enumerate((2, 4))
         ]
-        paired = [psum.tile([P, 2, HALF], F32, name=f"paired{u}", tag=f"bank{2 + u}") for u in range(2)]
+        pair_banks = [psum.tile([P, 2, HALF], F32, name=f"late_scores{u}", tag=f"bank{2 + u}") for u in range(2)]
         x_grouped = [sbuf(f"x{h}_grouped", [P, K_PASS, PACK], BF16) for h in range(ROW_PASSES)]
-        x_ops = [planes(f"x{h}", K_PASS) for h in range(ROW_PASSES)]
+        x_ops = [operand(f"x{h}", K_PASS) for h in range(ROW_PASSES)]
 
         def score_passes(h, tables, start, stop):
-            banks = [(bank, range(PACK), c * P, (c + 1) * P) for c, bank in enumerate(direct[h])]
+            banks = [(bank, range(PACK), c * P, (c + 1) * P) for c, bank in enumerate(quarter_banks[h])]
             if h == 0:
-                banks = [(paired[u], (2 * u, 2 * u + 1), HALF, N) for u in range(2)] + banks
-            for bank, ts, c0, c1 in banks:
-                passes = [(e, t, table) for e, t in enumerate(ts) for table in tables]
+                banks = [(pair_banks[u], (2 * u, 2 * u + 1), HALF, N) for u in range(2)] + banks
+            for bank, tiles, s0, s1 in banks:
+                passes = [(e, t, table) for e, t in enumerate(tiles) for table in tables]
                 for n, (e, t, table) in enumerate(passes):
                     lhs = x_lead if (h, t) == (0, 0) else x_ops[h]
-                    matmul(bank[:, e, :], lhs, t * P, table, c0, c1, E4M3, start and n == 0, stop and n == len(passes) - 1)
+                    matmul(bank[:, e, :], lhs, t * P, table, s0, s1, E4M3, start and n == 0, stop and n == len(passes) - 1)
 
         def group_x(copy, h, raw, m0, m1, t0, t1):
             copy(
@@ -142,31 +142,31 @@ def tile_attend_gds_sq_kernel(tc, xT, wT, vT, wt, xm, offs, out):
 
         v_picked = sbuf("v_picked", [P, PACK, N], F32)
         v_grouped = sbuf("v_grouped", [P, N, PACK], BF16)
-        v_op = planes("v", N, "w_plane0")
+        v_op = operand("v", N, "w_plane0")
         for j in range(PACK):
             nc.vector.tensor_copy(v_picked[:, j, :], listed(v_pairs[j // 2][:, j % 2, :], WHOLE))
-        nc.scalar.activation(
-            out=v_grouped[:].rearrange("p (c i) j -> p c j i", i=PACK),
-            in_=v_picked[:].rearrange("p j (c i) -> p c j i", i=PACK),
-            func=COPY,
-            scale=-1.0,
-        )
+        v_out, v_in = four_by_four(v_grouped[:], v_picked[:])
+        nc.scalar.activation(out=v_out, in_=v_in, func=COPY, scale=-1.0)
 
         group_x(nc.vector.tensor_copy, 0, x0_raw[:], 0, P, 0, PACK)
         quantize(x_ops[0], P, 2 * P, x_grouped[0][:, P : 2 * P, :], E4M3)
         quantize(x_ops[0], 2 * P, K_PASS, x_grouped[0][:, 2 * P :, :], E4M3)
 
         w_grouped = sbuf("w_grouped", [P, N, PACK], BF16)
-        w_op = planes("w", N)
-        for j in range(PACK):
-            if j == 1:
-                quantize(v_op, 0, N, v_grouped[:], E4M3)
-            if j == 3:
-                x_lead = (sbuf("lead_codes", [P, P], U32, "w_plane2"), x_ops[0][1])
-                quantize(x_lead, 0, P, x_grouped[0][:, 0:P, :], E4M3)
-                score_passes(0, [v_op], True, False)
-            for slots in (WHOLE,) if j < PACK - 1 else (LATE, EARLY):
-                nc.vector.tensor_copy(w_grouped[:, slots[0] : slots[1], j], listed(w_planes[j][:], slots))
+        w_op = operand("w", N)
+
+        def gather_student(j, slots):
+            nc.vector.tensor_copy(w_grouped[:, slots[0] : slots[1], j], listed(w_planes[j][:], slots))
+
+        gather_student(0, WHOLE)
+        quantize(v_op, 0, N, v_grouped[:], E4M3)
+        gather_student(1, WHOLE)
+        gather_student(2, WHOLE)
+        x_lead = (sbuf("lead_codes", [P, P], U32, "w_plane2"), x_ops[0][1])
+        quantize(x_lead, 0, P, x_grouped[0][:, 0:P, :], E4M3)
+        score_passes(0, [v_op], True, False)
+        for slots in (LATE, EARLY):
+            gather_student(PACK - 1, slots)
         for s0, s1 in (LATE, EARLY):
             quantize(w_op, s0, s1, w_grouped[:, s0:s1, :], E4M3)
         score_passes(0, [w_op], False, True)
@@ -178,119 +178,116 @@ def tile_attend_gds_sq_kernel(tc, xT, wT, vT, wt, xm, offs, out):
             quantize(x_ops[1], 2 * u * P, (2 * u + 2) * P, x_grouped[1][:, 2 * u * P : (2 * u + 2) * P, :], E4M3)
         score_passes(1, [v_op, w_op], True, True)
 
-        g_op = planes("g", ROW_PASSES * N)
-        back_words = back[:].bitcast(BF16).rearrange("p (w j) -> p w j", j=PACK)
+        g_op = operand("g", ROW_PASSES * N)
+        early_words = back[:].bitcast(BF16).rearrange("p (w j) -> p w j", j=PACK)
         late_words = sbuf("late_words", [P, ROW_PASSES * HALF, PACK], BF16)
-        g0_late_rows = front[:, 0 : PACK * HALF // 2].bitcast(BF16).rearrange("p (t i) -> p t i", t=PACK)
-        first_grouped = sbuf("first_grouped", [P, 5 * P, PACK], BF16)
-        xm_grouped = [
-            first_grouped[:, 0 : 2 * P, :],
-            first_grouped[:, 2 * P : 4 * P, :],
-            first_grouped[:, 3 * P :, :],
-            first_grouped[:, 3 * P :, :],
-        ]
-        xm_ops = {}
+        g0_late_tiles = front[:, 0 : PACK * HALF // 2].bitcast(BF16).rearrange("p (t i) -> p t i", t=PACK)
 
         def g_words(c, h0, h1):
             w0 = (c % 2) * ROW_PASSES * P
-            return (back_words, late_words)[c // 2][:, w0 + h0 * P : w0 + h1 * P, :]
+            return (early_words, late_words)[c // 2][:, w0 + h0 * P : w0 + h1 * P, :]
 
-        def xm_place(b, h):
+        def weigh(h, c, factors):
+            scores = quarter_banks[h][c][:].rearrange("p t i -> p i t")
+            nc.vector.tensor_tensor(g_words(c, h, h + 1), scores, factors.to_broadcast([P, P, PACK]), MULT)
+
+        def quantize_g(c):
+            quantize(g_op, c * ROW_PASSES * P, (c + 1) * ROW_PASSES * P, g_words(c, 0, ROW_PASSES), E5M2)
+
+        xm_grouped = sbuf("xm_grouped", [P, 5 * P, PACK], BF16)
+        xm_first_place = (0, 2, 3, 3)
+        xm_ops = {}
+
+        def xm_column(b, h):
             return (1 - h if b == 2 else h) * P
 
         def xm_words(b, h):
-            return xm_grouped[b][:, xm_place(b, h) : xm_place(b, h) + P, :]
+            w0 = xm_first_place[b] * P + xm_column(b, h)
+            return xm_grouped[:, w0 : w0 + P, :]
 
-        def group_xm(copy, b, h):
-            interleave(copy, xm_words(b, h), xm_raw[b, h])
+        def group_xm_scalar(b, h):
+            words, rows = four_by_four(xm_words(b, h), xm_raw[b, h])
+            nc.scalar.copy(out=words, in_=rows)
 
         def group_xm_gpsimd(b, h):
             gpsimd_copy(xm_words(b, h), xm_raw[b, h].rearrange("p j d -> p d j"))
 
         def quantize_xm(b, codes_tag=None):
-            xm_ops[b] = planes(f"xm{b}", ROW_PASSES * P, codes_tag)
-            quantize(xm_ops[b], 0, ROW_PASSES * P, xm_grouped[b], E4M3)
+            w0 = xm_first_place[b] * P
+            xm_ops[b] = operand(f"xm{b}", ROW_PASSES * P, codes_tag)
+            quantize(xm_ops[b], 0, ROW_PASSES * P, xm_grouped[:, w0 : w0 + ROW_PASSES * P, :], E4M3)
 
-        def quantize_g(c):
-            quantize(g_op, c * ROW_PASSES * P, (c + 1) * ROW_PASSES * P, g_words(c, 0, ROW_PASSES), E5M2)
+        def product(name, bank, b, quarters, copy, grad):
+            acc = psum.tile([P, len(quarters) * P], F32, name=name, tag=f"bank{bank}")
+            for n, c in enumerate(quarters):
+                for h in range(ROW_PASSES):
+                    g0 = (c * ROW_PASSES + h) * P
+                    last = h == ROW_PASSES - 1
+                    matmul(acc[:, n * P : (n + 1) * P], xm_ops[b], xm_column(b, h), g_op, g0, g0 + P, E5M2, h == 0, last)
+            copy(out=grad, in_=acc[:])
 
-        def weigh_direct(h, c, factors):
-            nc.vector.tensor_tensor(
-                g_words(c, h, h + 1), direct[h][c][:].rearrange("p t i -> p i t"), factors.to_broadcast([P, P, PACK]), MULT
-            )
+        def half_tile(name):
+            return sbuf(name, [P, HALF], F32)[:]
 
-        def multiply(acc, b, c):
-            for h in range(ROW_PASSES):
-                g0 = (c * ROW_PASSES + h) * P
-                matmul(acc, xm_ops[b], xm_place(b, h), g_op, g0, g0 + P, E5M2, h == 0, h == ROW_PASSES - 1)
+        def scatter_early(b, grad):
+            nc.scalar.activation(out=listed(windows[b][:], EARLY), in_=grad, func=COPY)
 
-        def product(name, banks, b, slots, copy, grad=None):
-            if grad is None:
-                grad = sbuf(name + "_sb", [P, HALF], F32)[:]
-            width = HALF // len(banks)
-            for n, bank in enumerate(banks):
-                acc = psum.tile([P, width], F32, name=f"{name}_{n}", tag=f"bank{bank}")
-                for s0 in range(0, width, P):
-                    multiply(acc[:, s0 : s0 + P], b, (slots[0] + n * width + s0) // P)
-                copy(out=grad[:, n * width : (n + 1) * width], in_=acc[:])
-            return grad
-
-        def scatter_vector(b, grad, slots):
-            nc.vector.tensor_copy(listed(windows[b][:], slots), grad)
-
-        def scatter_scalar(b, grad, slots):
-            nc.scalar.activation(out=listed(windows[b][:], slots), in_=grad, func=COPY)
-
-        def store(b):
+        def scatter_late_and_store(b, grad):
+            nc.vector.tensor_copy(listed(windows[b][:], LATE), grad)
             nc.sync.dma_start(out[b * P : (b + 1) * P, :], windows[b][:])
 
         for t in range(PACK):
             nc.scalar.activation(
-                out=g0_late_rows[:, t, :], in_=paired[t // 2][:, t % 2, :], func=COPY, scale=weights[:, 0, t : t + 1]
+                out=g0_late_tiles[:, t, :], in_=pair_banks[t // 2][:, t % 2, :], func=COPY, scale=weights[:, 0, t : t + 1]
             )
         gpsimd_copy(
             late_words[:].rearrange("p (c h i) t -> p c h i t", c=2, h=ROW_PASSES)[:, :, 0],
-            g0_late_rows.rearrange("p t (c i) -> p c i t", c=2),
+            g0_late_tiles.rearrange("p t (c i) -> p c i t", c=2),
         )
-        for b, h in ((0, 0), (0, 1), (1, 0), (1, 1), (2, 0)):
-            group_xm(nc.scalar.copy, b, h)
+        for b, h in pieces[:5]:
+            group_xm_scalar(b, h)
 
         for c in range(2):
-            weigh_direct(0, c, weights[:, 0:1, :])
+            weigh(0, c, weights[:, 0:1, :])
         for c in range(2):
-            weigh_direct(1, c, early_weights[:])
+            weigh(1, c, early_weights[:])
         quantize_g(0)
         quantize_xm(0, "early_weights")
         quantize_g(1)
         quantize_xm(1)
-        early0 = product("early0", (0, 1), 0, EARLY, nc.scalar.copy)
-        scatter_scalar(0, early0, EARLY)
+
+        early0, early1 = half_tile("early0"), half_tile("early1")
+        for c in range(2):
+            product(f"early0_{c}", c, 0, [c], nc.scalar.copy, early0[:, c * P : (c + 1) * P])
+        product("early1_0", 2, 1, [0], nc.scalar.copy, early1[:, 0:P])
+        scatter_early(0, early0)
 
         group_xm_gpsimd(2, 1)
         for c in range(2, 4):
-            weigh_direct(1, c, weights[:, 1:2, :])
+            weigh(1, c, weights[:, 1:2, :])
         for c in range(2, 4):
             quantize_g(c)
         quantize_xm(2)
         for h in range(ROW_PASSES):
             group_xm_gpsimd(3, h)
-        early1 = product("early1", (2,), 1, EARLY, nc.vector.tensor_copy)
-        scatter_scalar(1, early1, EARLY)
-        late0 = product("late0", (4, 5), 0, LATE, nc.vector.tensor_copy)
-        scatter_vector(0, late0, LATE)
-        store(0)
+        product("early1_1", 3, 1, [1], nc.vector.tensor_copy, early1[:, P:HALF])
+        scatter_early(1, early1)
+        late0 = half_tile("late0")
+        for c in range(2):
+            product(f"late0_{c}", 4 + c, 0, [2 + c], nc.vector.tensor_copy, late0[:, c * P : (c + 1) * P])
+        scatter_late_and_store(0, late0)
 
-        late1 = product("late1", (3,), 1, LATE, nc.scalar.copy, last_piece[:, 0:HALF])
-        early2 = product("early2", (0,), 2, EARLY, nc.scalar.copy, last_piece[:, HALF : 2 * HALF])
+        late1, early2 = last_piece[:, 0:HALF], last_piece[:, HALF:]
+        product("late1", 3, 1, [2, 3], nc.scalar.copy, late1)
+        product("early2", 0, 2, [0, 1], nc.scalar.copy, early2)
         quantize_xm(3)
-        spent_words = xm_words(3, 0).rearrange("p w j -> p (w j)").bitcast(F32)
-        late2 = product("late2", (1,), 2, LATE, nc.scalar.copy, spent_words)
-        scatter_scalar(2, early2, EARLY)
-        scatter_vector(1, late1, LATE)
-        store(1)
-        early3 = product("early3", (6,), 3, EARLY, nc.vector.tensor_copy)
-        late3 = product("late3", (7,), 3, LATE, nc.scalar.copy)
-        scatter_scalar(3, early3, EARLY)
-        for b, late in ((2, late2), (3, late3)):
-            scatter_vector(b, late, LATE)
-            store(b)
+        late2 = xm_words(3, 0).rearrange("p w j -> p (w j)").bitcast(F32)
+        product("late2", 1, 2, [2, 3], nc.scalar.copy, late2)
+        scatter_early(2, early2)
+        scatter_late_and_store(1, late1)
+        early3, late3 = half_tile("early3"), half_tile("late3")
+        product("early3", 6, 3, [0, 1], nc.vector.tensor_copy, early3)
+        product("late3", 7, 3, [2, 3], nc.scalar.copy, late3)
+        scatter_early(3, early3)
+        scatter_late_and_store(2, late2)
+        scatter_late_and_store(3, late3)

@@ -36,7 +36,7 @@ def tile_attend_gds_sq_kernel(tc, xT, wT, vT, wt, xm, offs, out):
         psum = ctx.enter_context(tc.psum_pool(name="psum", bufs=1))
 
         def sbuf(name, shape, dtype, tag=None):
-            return keep.tile(shape, dtype, name=name, tag=tag or name, align_bytes=64)
+            return keep.tile(shape, dtype, name=name, tag=tag or name, align_bytes=256)
 
         def operand(name, width, codes_tag=None):
             return sbuf(name + "_codes", [P, width], U32, codes_tag), sbuf(name + "_scales", [P, width], U8)
@@ -111,7 +111,7 @@ def tile_attend_gds_sq_kernel(tc, xT, wT, vT, wt, xm, offs, out):
         for b, h in pieces:
             nc.sync.dma_start(xm_raw[b, h], xm_rows[h][:, :, b * P : (b + 1) * P])
 
-        windows = [keep.tile([P, T], F32, name=f"window{b}") for b in range(BLOCKS)]
+        windows = [sbuf(f"window{b}", [P, T], F32) for b in range(BLOCKS)]
         for b in range(BLOCKS):
             engine = nc.vector if b < BLOCKS // 2 else nc.gpsimd
             engine.memset(windows[b][:], 0.0)

@@ -77,13 +77,15 @@ def tile_attend_gds_sq_kernel(tc, xT, wT, vT, wt, xm, offs, out):
         x0_raw = sbuf("x0_raw", [P, PACK, K_PASS], F32)
         x_cut = K_PASS // 2
         front = sbuf("front", [P, PACK * x_cut], F32)
-        back = sbuf("back", [P, PACK * x_cut], F32)
+        run = P * PACK // 2
+        back = sbuf("back", [P, run + PACK * x_cut], F32)
+        back_words = back[:].bitcast(BF16).rearrange("p (w j) -> p w j", j=PACK)
         x1_front = front[:].rearrange("p (j r) -> p j r", j=PACK)
-        x1_back = back[:].rearrange("p (j r) -> p j r", j=PACK)
+        x1_back = back[:, run:].rearrange("p (j r) -> p j r", j=PACK)
         pieces = [(b, h) for b in range(BLOCKS) for h in range(ROW_PASSES)]
         xm_raw = {(b, h): sbuf(f"xm_raw{b}_{h}", [P, PACK, P], F32)[:] for b, h in pieces[:-1]}
-        last_piece = sbuf("last_piece", [P, PACK * P], F32)
-        xm_raw[pieces[-1]] = last_piece[:].rearrange("p (j d) -> p j d", j=PACK)
+        last_piece = sbuf("last_piece", [P, P + PACK * P + P], F32)
+        xm_raw[pieces[-1]] = last_piece[:, P : P + PACK * P].rearrange("p (j d) -> p j d", j=PACK)
 
         weights = sbuf("weights", [P, ROW_PASSES, PACK], F32)
         identity = sbuf("identity", [P, P], F32)
@@ -98,7 +100,9 @@ def tile_attend_gds_sq_kernel(tc, xT, wT, vT, wt, xm, offs, out):
             nc.tensor.transpose(turned[:, t, :], weight_rows[:, t::PACK], identity[:])
         nc.scalar.copy(out=weights[:], in_=turned[:, :, 0:ROW_PASSES].rearrange("p t h -> p h t"))
         early_weights = sbuf("early_weights", [P, 1, PACK], F32)
-        nc.scalar.copy(out=early_weights[:], in_=turned[:, :, 1:2].rearrange("p t h -> p h t"))
+        last_weights = sbuf("last_weights", [P, 1, PACK], F32)
+        for own in (early_weights, last_weights):
+            nc.scalar.copy(out=own[:], in_=turned[:, :, 1:2].rearrange("p t h -> p h t"))
 
         nc.sync.dma_start(v_pairs[0][:], v_rows[:, 0:2, :])
         nc.sync.dma_start(offsets[:], offs)
@@ -118,14 +122,14 @@ def tile_attend_gds_sq_kernel(tc, xT, wT, vT, wt, xm, offs, out):
 
         quarter_banks = [
             [psum.tile([P, PACK, P], F32, name=f"scores{h}_{c}", tag=f"bank{4 * h + c}") for c in range(quarters)]
-            for h, quarters in enumerate((2, 4))
+            for h, quarters in enumerate((2, 3))
         ]
         pair_banks = [psum.tile([P, 2, HALF], F32, name=f"late_scores{u}", tag=f"bank{2 + u}") for u in range(2)]
         x_grouped = [sbuf(f"x{h}_grouped", [P, K_PASS, PACK], BF16) for h in range(ROW_PASSES)]
         x_ops = [operand(f"x{h}", K_PASS) for h in range(ROW_PASSES)]
 
-        def score_passes(h, tables, start, stop):
-            banks = [(bank, range(PACK), c * P, (c + 1) * P) for c, bank in enumerate(quarter_banks[h])]
+        def score_passes(h, tables, start, stop, first=0):
+            banks = [(bank, range(PACK), c * P, (c + 1) * P) for c, bank in enumerate(quarter_banks[h])][first:]
             if h == 0:
                 banks = [(pair_banks[u], (2 * u, 2 * u + 1), HALF, N) for u in range(2)] + banks
             for bank, tiles, s0, s1 in banks:
@@ -179,13 +183,12 @@ def tile_attend_gds_sq_kernel(tc, xT, wT, vT, wt, xm, offs, out):
         score_passes(1, [v_op, w_op], True, True)
 
         g_op = operand("g", ROW_PASSES * N)
-        early_words = back[:].bitcast(BF16).rearrange("p (w j) -> p w j", j=PACK)
         late_words = sbuf("late_words", [P, ROW_PASSES * HALF, PACK], BF16)
         g0_late_tiles = front[:, 0 : PACK * HALF // 2].bitcast(BF16).rearrange("p (t i) -> p t i", t=PACK)
 
         def g_words(c, h0, h1):
-            w0 = (c % 2) * ROW_PASSES * P
-            return (early_words, late_words)[c // 2][:, w0 + h0 * P : w0 + h1 * P, :]
+            words, w0 = ((back_words, 3 * P), (back_words, P), (late_words, 0), (late_words, 2 * P))[c]
+            return words[:, w0 + h0 * P : w0 + h1 * P, :]
 
         def weigh(h, c, factors):
             scores = quarter_banks[h][c][:].rearrange("p t i -> p i t")
@@ -194,16 +197,12 @@ def tile_attend_gds_sq_kernel(tc, xT, wT, vT, wt, xm, offs, out):
         def quantize_g(c):
             quantize(g_op, c * ROW_PASSES * P, (c + 1) * ROW_PASSES * P, g_words(c, 0, ROW_PASSES), E5M2)
 
-        xm_grouped = sbuf("xm_grouped", [P, 5 * P, PACK], BF16)
-        xm_first_place = (0, 2, 3, 3)
+        xm_grouped = sbuf("xm_grouped", [P, 4 * P, PACK], BF16)
+        block_words = [xm_grouped[:, 0 : 2 * P, :], xm_grouped[:, 2 * P :, :], back_words[:, 0 : 2 * P, :], back_words[:, 0 : 2 * P, :]]
         xm_ops = {}
 
-        def xm_column(b, h):
-            return (1 - h if b == 2 else h) * P
-
         def xm_words(b, h):
-            w0 = xm_first_place[b] * P + xm_column(b, h)
-            return xm_grouped[:, w0 : w0 + P, :]
+            return block_words[b][:, h * P : (h + 1) * P, :]
 
         def group_xm_scalar(b, h):
             words, rows = four_by_four(xm_words(b, h), xm_raw[b, h])
@@ -213,9 +212,8 @@ def tile_attend_gds_sq_kernel(tc, xT, wT, vT, wt, xm, offs, out):
             gpsimd_copy(xm_words(b, h), xm_raw[b, h].rearrange("p j d -> p d j"))
 
         def quantize_xm(b, codes_tag=None):
-            w0 = xm_first_place[b] * P
             xm_ops[b] = operand(f"xm{b}", ROW_PASSES * P, codes_tag)
-            quantize(xm_ops[b], 0, ROW_PASSES * P, xm_grouped[:, w0 : w0 + ROW_PASSES * P, :], E4M3)
+            quantize(xm_ops[b], 0, ROW_PASSES * P, block_words[b], E4M3)
 
         def product(name, bank, b, quarters, copy, grad):
             acc = psum.tile([P, len(quarters) * P], F32, name=name, tag=f"bank{bank}")
@@ -223,17 +221,19 @@ def tile_attend_gds_sq_kernel(tc, xT, wT, vT, wt, xm, offs, out):
                 for h in range(ROW_PASSES):
                     g0 = (c * ROW_PASSES + h) * P
                     last = h == ROW_PASSES - 1
-                    matmul(acc[:, n * P : (n + 1) * P], xm_ops[b], xm_column(b, h), g_op, g0, g0 + P, E5M2, h == 0, last)
+                    matmul(acc[:, n * P : (n + 1) * P], xm_ops[b], h * P, g_op, g0, g0 + P, E5M2, h == 0, last)
             copy(out=grad, in_=acc[:])
 
         def half_tile(name):
             return sbuf(name, [P, HALF], F32)[:]
 
-        def scatter_early(b, grad):
-            nc.scalar.activation(out=listed(windows[b][:], EARLY), in_=grad, func=COPY)
+        def scatter_scalar(b, slots, grad):
+            nc.scalar.activation(out=listed(windows[b][:], slots), in_=grad, func=COPY)
 
-        def scatter_late_and_store(b, grad):
-            nc.vector.tensor_copy(listed(windows[b][:], LATE), grad)
+        def scatter_vector(b, slots, grad):
+            nc.vector.tensor_copy(listed(windows[b][:], slots), grad)
+
+        def store(b):
             nc.sync.dma_start(out[b * P : (b + 1) * P, :], windows[b][:])
 
         for t in range(PACK):
@@ -251,43 +251,49 @@ def tile_attend_gds_sq_kernel(tc, xT, wT, vT, wt, xm, offs, out):
             weigh(0, c, weights[:, 0:1, :])
         for c in range(2):
             weigh(1, c, early_weights[:])
+        quarter_banks[1].append(psum.tile([P, PACK, P], F32, name="scores1_3", tag="bank5"))
+        score_passes(1, [v_op, w_op], True, True, 3)
         quantize_g(0)
         quantize_xm(0, "early_weights")
         quantize_g(1)
-        quantize_xm(1)
 
-        early0, early1 = half_tile("early0"), half_tile("early1")
+        early0, late0 = half_tile("early0"), half_tile("late0")
         for c in range(2):
             product(f"early0_{c}", c, 0, [c], nc.scalar.copy, early0[:, c * P : (c + 1) * P])
-        product("early1_0", 2, 1, [0], nc.scalar.copy, early1[:, 0:P])
-        scatter_early(0, early0)
+        scatter_scalar(0, EARLY, early0)
 
         group_xm_gpsimd(2, 1)
-        for c in range(2, 4):
-            weigh(1, c, weights[:, 1:2, :])
+        weigh(1, 2, weights[:, 1:2, :])
+        weigh(1, 3, last_weights[:])
         for c in range(2, 4):
             quantize_g(c)
-        quantize_xm(2)
+        quantize_xm(1, "last_weights")
+        for c in range(2):
+            product(f"late0_{c}", 4 + 3 * c, 0, [2 + c], nc.vector.tensor_copy, late0[:, c * P : (c + 1) * P])
+        quantize_xm(2, "early_weights")
         for h in range(ROW_PASSES):
             group_xm_gpsimd(3, h)
-        product("early1_1", 3, 1, [1], nc.vector.tensor_copy, early1[:, P:HALF])
-        scatter_early(1, early1)
-        late0 = half_tile("late0")
-        for c in range(2):
-            product(f"late0_{c}", 4 + c, 0, [2 + c], nc.vector.tensor_copy, late0[:, c * P : (c + 1) * P])
-        scatter_late_and_store(0, late0)
+        scatter_vector(0, LATE, late0)
+        store(0)
 
-        late1, early2 = last_piece[:, 0:HALF], last_piece[:, HALF:]
-        product("late1", 3, 1, [2, 3], nc.scalar.copy, late1)
-        product("early2", 0, 2, [0, 1], nc.scalar.copy, early2)
+        early1, late1 = half_tile("early1"), last_piece[:, 0:HALF]
+        product("early1", 2, 1, [0, 1], nc.scalar.copy, early1)
+        product("late1_0", 3, 1, [2], nc.scalar.copy, late1[:, 0:P])
+        scatter_scalar(1, EARLY, early1)
+        product("late1_1", 0, 1, [3], nc.vector.tensor_copy, late1[:, P:HALF])
         quantize_xm(3)
-        late2 = xm_words(3, 0).rearrange("p w j -> p (w j)").bitcast(F32)
-        product("late2", 1, 2, [2, 3], nc.scalar.copy, late2)
-        scatter_early(2, early2)
-        scatter_late_and_store(1, late1)
+        scatter_vector(1, LATE, late1)
+        store(1)
+
+        early2, late2 = last_piece[:, HALF : 2 * HALF], last_piece[:, 2 * HALF :]
+        product("early2", 6, 2, [0, 1], nc.scalar.copy, early2)
+        product("late2", 5, 2, [2, 3], nc.scalar.copy, late2)
+        scatter_scalar(2, EARLY, early2)
+        scatter_scalar(2, LATE, late2)
+        store(2)
         early3, late3 = half_tile("early3"), half_tile("late3")
-        product("early3", 6, 3, [0, 1], nc.vector.tensor_copy, early3)
-        product("late3", 7, 3, [2, 3], nc.scalar.copy, late3)
-        scatter_early(3, early3)
-        scatter_late_and_store(2, late2)
-        scatter_late_and_store(3, late3)
+        product("early3", 1, 3, [0, 1], nc.vector.tensor_copy, early3)
+        product("late3", 2, 3, [2, 3], nc.vector.tensor_copy, late3)
+        scatter_vector(3, EARLY, early3)
+        scatter_vector(3, LATE, late3)
+        store(3)

@@ -117,7 +117,7 @@ def tile_attend_gds_sq_kernel(tc, xT, wT, vT, wt, xm, offs, out):
 
         windows = [sbuf(f"window{b}", [P, T], F32) for b in range(BLOCKS)]
         for b in range(BLOCKS):
-            engine = nc.vector if b < BLOCKS // 2 else nc.gpsimd
+            engine = nc.vector if b == 0 else nc.gpsimd
             engine.memset(windows[b][:], 0.0)
 
         quarter_banks = [
@@ -153,8 +153,7 @@ def tile_attend_gds_sq_kernel(tc, xT, wT, vT, wt, xm, offs, out):
         nc.scalar.activation(out=v_out, in_=v_in, func=COPY, scale=-1.0)
 
         group_x(nc.vector.tensor_copy, 0, x0_raw[:], 0, P, 0, PACK)
-        quantize(x_ops[0], P, 2 * P, x_grouped[0][:, P : 2 * P, :], E4M3)
-        quantize(x_ops[0], 2 * P, K_PASS, x_grouped[0][:, 2 * P :, :], E4M3)
+        quantize(x_ops[0], P, K_PASS, x_grouped[0][:, P:, :], E4M3)
 
         w_grouped = sbuf("w_grouped", [P, N, PACK], BF16)
         w_op = operand("w", N)
@@ -162,15 +161,18 @@ def tile_attend_gds_sq_kernel(tc, xT, wT, vT, wt, xm, offs, out):
         def gather_student(j, slots):
             nc.vector.tensor_copy(w_grouped[:, slots[0] : slots[1], j], listed(w_planes[j][:], slots))
 
+        def gather_halves(j):
+            nc.scalar.activation(out=w_grouped[:, HALF:, j], in_=listed(w_planes[j][:], LATE), func=COPY)
+            gather_student(j, EARLY)
+
         gather_student(0, WHOLE)
         quantize(v_op, 0, N, v_grouped[:], E4M3)
         gather_student(1, WHOLE)
-        gather_student(2, WHOLE)
+        gather_halves(2)
         x_lead = (sbuf("lead_codes", [P, P], U32, "w_plane2"), x_ops[0][1])
         quantize(x_lead, 0, P, x_grouped[0][:, 0:P, :], E4M3)
         score_passes(0, [v_op], True, False)
-        for slots in (LATE, EARLY):
-            gather_student(PACK - 1, slots)
+        gather_halves(3)
         for s0, s1 in (LATE, EARLY):
             quantize(w_op, s0, s1, w_grouped[:, s0:s1, :], E4M3)
         score_passes(0, [w_op], False, True)
@@ -268,11 +270,11 @@ def tile_attend_gds_sq_kernel(tc, xT, wT, vT, wt, xm, offs, out):
         for c in range(2, 4):
             quantize_g(c)
         quantize_xm(1, "last_weights")
-        for c in range(2):
-            product(f"late0_{c}", 4 + 3 * c, 0, [2 + c], nc.vector.tensor_copy, late0[:, c * P : (c + 1) * P])
-        quantize_xm(2, "early_weights")
+        quantize_xm(2)
         for h in range(ROW_PASSES):
             group_xm_gpsimd(3, h)
+        for c in range(2):
+            product(f"late0_{c}", 4 + 3 * c, 0, [2 + c], nc.vector.tensor_copy, late0[:, c * P : (c + 1) * P])
         scatter_vector(0, LATE, late0)
         store(0)
 

from contextlib import ExitStack

import concourse.mybir as mybir
from concourse.masks import make_identity

N, T, D, R = 512, 2048, 512, 1024
FLOPS = 3 * 2 * N * D * R

F32 = mybir.dt.float32
BF16 = mybir.dt.bfloat16
U32 = mybir.dt.uint32
U16 = mybir.dt.uint16
U8 = mybir.dt.uint8
E4M3 = mybir.dt.float8_e4m3fn_x4
E5M2 = mybir.dt.float8_e5m2_x4
COPY = mybir.ActivationFunctionType.Copy
MULT = mybir.AluOpType.mult
ADD = mybir.AluOpType.add

P = 128
PACK = 4
K_PASS = P * PACK
ROW_PASSES = R // K_PASS
BLOCKS = D // P
HALF = N // 2
LIST_ROWS = 16
EARLY = (0, HALF)
LATE = (HALF, N)
WHOLE = (0, N)


def tile_attend_gds_sq_kernel(tc, xT, wT, vT, wt, xm, offs, out):
    nc = tc.nc
    with ExitStack() as ctx:
        keep = ctx.enter_context(tc.tile_pool(name="keep", bufs=1))
        psum = ctx.enter_context(tc.psum_pool(name="psum", bufs=1))

        def sbuf(name, shape, dtype, tag=None):
            return keep.tile(shape, dtype, name=name, tag=tag or name, align_bytes=256)

        def operand(name, width, codes_tag=None):
            return sbuf(name + "_codes", [P, width], U32, codes_tag), sbuf(name + "_scales", [P, width], U8)

        def quantize(op, c0, c1, grouped, fmt):
            nc.vector.quantize_mx(
                out=op[0][:, c0:c1].bitcast(fmt), scales=op[1][:, c0:c1], in_=grouped.rearrange("p w j -> p (w j)")
            )

        def matmul(acc, lhs, l0, rhs, r0, r1, rhs_fmt, start, stop):
            nc.tensor.matmul_mx(
                out=acc,
                lhsT=lhs[0][:, l0 : l0 + P].bitcast(E4M3),
                lhsT_scale=lhs[1][:, l0 : l0 + P],
                rhs=rhs[0][:, r0:r1].bitcast(rhs_fmt),
                rhs_scale=rhs[1][:, r0:r1],
                start=start,
                stop=stop,
            )

        def listed(window, slots):
            return window.indirect(offsets[:, slots[0] // LIST_ROWS : slots[1] // LIST_ROWS])

        def four_by_four(grouped, rows):
            return grouped.rearrange("p (c i) j -> p c j i", i=PACK), rows.rearrange("p j (c i) -> p c j i", i=PACK)

        def gpsimd_copy(out, in_):
            nc.gpsimd.tensor_scalar(out=out, in0=in_, scalar1=1.0, scalar2=0.0, op0=MULT, op1=ADD)

        offsets = keep.tile([P, N // LIST_ROWS], U16, name="offsets")
        v_rows = vT.rearrange("(p j) t -> p j t", j=PACK)
        w_rows = wT.rearrange("(p j) t -> p j t", j=PACK)
        x_rows = xT[0].rearrange("(p j) r -> p j r", j=PACK)
        xm_rows = xm[0].rearrange("(h p j) d -> h p j d", p=P, j=PACK)

        v_pairs = [sbuf(f"v_pair{u}", [P, 2, T], F32) for u in range(2)]
        w_planes = [sbuf(f"w_plane{j}", [P, T], F32) for j in range(PACK)]
        x0_raw = sbuf("x0_raw", [P, PACK, K_PASS], F32)
        x_cut = K_PASS // 2
        front = sbuf("front", [P, PACK * x_cut], F32)
        run = P * PACK // 2
        back = sbuf("back", [P, run + PACK * x_cut], F32)
        back_words = back[:].bitcast(BF16).rearrange("p (w j) -> p w j", j=PACK)
        x1_front = front[:].rearrange("p (j r) -> p j r", j=PACK)
        x1_back = back[:, run:].rearrange("p (j r) -> p j r", j=PACK)
        pieces = [(b, h) for b in range(BLOCKS) for h in range(ROW_PASSES)]
        xm_raw = {(b, h): sbuf(f"xm_raw{b}_{h}", [P, PACK, P], F32)[:] for b, h in pieces[:-1]}
        last_piece = sbuf("last_piece", [P, P + PACK * P + P], F32)
        xm_raw[pieces[-1]] = last_piece[:, P : P + PACK * P].rearrange("p (j d) -> p j d", j=PACK)

        weights = sbuf("weights", [P, ROW_PASSES, PACK], F32)
        identity = sbuf("identity", [P, P], F32)
        make_identity(nc, identity[:])
        weight_rows = sbuf("weight_rows", [P, K_PASS], F32)
        weight_in = keep.tile([ROW_PASSES, K_PASS], F32, name="weight_in")
        nc.scalar.dma_start(weight_in[:], wt[0].rearrange("(h r) o -> h (r o)", h=ROW_PASSES))
        nc.gpsimd.memset(weight_rows[:], 0.0)
        nc.scalar.copy(out=weight_rows[0:ROW_PASSES, :], in_=weight_in[:])
        turned = psum.tile([P, PACK, P], F32, name="turned", tag="bank7")
        for t in range(PACK):
            nc.tensor.transpose(turned[:, t, :], weight_rows[:, t::PACK], identity[:])
        nc.scalar.copy(out=weights[:], in_=turned[:, :, 0:ROW_PASSES].rearrange("p t h -> p h t"))
        early_weights = sbuf("early_weights", [P, 1, PACK], F32)
        last_weights = sbuf("last_weights", [P, 1, PACK], F32)
        for own in (early_weights, last_weights):
            nc.scalar.copy(out=own[:], in_=turned[:, :, 1:2].rearrange("p t h -> p h t"))

        nc.sync.dma_start(v_pairs[0][:], v_rows[:, 0:2, :])
        nc.sync.dma_start(offsets[:], offs)
        nc.sync.dma_start(v_pairs[1][:], v_rows[:, 2:4, :])
        nc.sync.dma_start(x0_raw[:], x_rows[:, :, 0:K_PASS])
        for j in range(PACK):
            nc.sync.dma_start(w_planes[j][:], w_rows[:, j, :])
        nc.sync.dma_start(x1_front, x_rows[:, :, K_PASS : K_PASS + x_cut])
        nc.sync.dma_start(x1_back, x_rows[:, :, K_PASS + x_cut :])
        for b, h in pieces:
            nc.sync.dma_start(xm_raw[b, h], xm_rows[h][:, :, b * P : (b + 1) * P])

        windows = [sbuf(f"window{b}", [P, T], F32) for b in range(BLOCKS)]
        for b in range(BLOCKS):
            engine = nc.vector if b == 0 else nc.gpsimd
            engine.memset(windows[b][:], 0.0)

        quarter_banks = [
            [psum.tile([P, PACK, P], F32, name=f"scores{h}_{c}", tag=f"bank{4 * h + c}") for c in range(quarters)]
            for h, quarters in enumerate((2, 3))
        ]
        pair_banks = [psum.tile([P, 2, HALF], F32, name=f"late_scores{u}", tag=f"bank{2 + u}") for u in range(2)]
        x_grouped = [sbuf(f"x{h}_grouped", [P, K_PASS, PACK], BF16) for h in range(ROW_PASSES)]
        x_ops = [operand(f"x{h}", K_PASS) for h in range(ROW_PASSES)]

        def score_passes(h, tables, start, stop, first=0):
            banks = [(bank, range(PACK), c * P, (c + 1) * P) for c, bank in enumerate(quarter_banks[h])][first:]
            if h == 0:
                banks = [(pair_banks[u], (2 * u, 2 * u + 1), HALF, N) for u in range(2)] + banks
            for bank, tiles, s0, s1 in banks:
                passes = [(e, t, table) for e, t in enumerate(tiles) for table in tables]
                for n, (e, t, table) in enumerate(passes):
                    lhs = x_lead if (h, t) == (0, 0) else x_ops[h]
                    matmul(bank[:, e, :], lhs, t * P, table, s0, s1, E4M3, start and n == 0, stop and n == len(passes) - 1)

        def group_x(copy, h, raw, m0, m1, t0, t1):
            copy(
                out=x_grouped[h][:].rearrange("p (t m) j -> p m j t", t=PACK)[:, m0:m1, :, t0:t1],
                in_=raw.rearrange("p j (m t) -> p m j t", t=PACK)[:, :, :, t0:t1],
            )

        v_picked = sbuf("v_picked", [P, PACK, N], F32)
        v_grouped = sbuf("v_grouped", [P, N, PACK], BF16)
        v_op = operand("v", N, "w_plane0")
        for j in range(PACK):
            nc.vector.tensor_copy(v_picked[:, j, :], listed(v_pairs[j // 2][:, j % 2, :], WHOLE))
        v_out, v_in = four_by_four(v_grouped[:], v_picked[:])
        nc.scalar.activation(out=v_out, in_=v_in, func=COPY, scale=-1.0)

        group_x(nc.vector.tensor_copy, 0, x0_raw[:], 0, P, 0, PACK)
        quantize(x_ops[0], P, K_PASS, x_grouped[0][:, P:, :], E4M3)

        w_grouped = sbuf("w_grouped", [P, N, PACK], BF16)
        w_op = operand("w", N)

        def gather_student(j, slots):
            nc.vector.tensor_copy(w_grouped[:, slots[0] : slots[1], j], listed(w_planes[j][:], slots))

        def gather_halves(j):
            nc.scalar.activation(out=w_grouped[:, HALF:, j], in_=listed(w_planes[j][:], LATE), func=COPY)
            gather_student(j, EARLY)

        gather_student(0, WHOLE)
        quantize(v_op, 0, N, v_grouped[:], E4M3)
        gather_student(1, WHOLE)
        gather_halves(2)
        x_lead = (sbuf("lead_codes", [P, P], U32, "w_plane2"), x_ops[0][1])
        quantize(x_lead, 0, P, x_grouped[0][:, 0:P, :], E4M3)
        score_passes(0, [v_op], True, False)
        gather_halves(3)
        for s0, s1 in (LATE, EARLY):
            quantize(w_op, s0, s1, w_grouped[:, s0:s1, :], E4M3)
        score_passes(0, [w_op], False, True)

        group_x(nc.scalar.copy, 1, x1_front, 0, P // 2, 0, PACK)
        for u in range(2):
            group_x(nc.vector.tensor_copy, 1, x1_back, P // 2, P, 2 * u, 2 * u + 2)
        for u in range(2):
            quantize(x_ops[1], 2 * u * P, (2 * u + 2) * P, x_grouped[1][:, 2 * u * P : (2 * u + 2) * P, :], E4M3)
        score_passes(1, [v_op, w_op], True, True)

        g_op = operand("g", ROW_PASSES * N)
        late_words = sbuf("late_words", [P, ROW_PASSES * HALF, PACK], BF16)
        g0_late_tiles = front[:, 0 : PACK * HALF // 2].bitcast(BF16).rearrange("p (t i) -> p t i", t=PACK)

        def g_words(c, h0, h1):
            words, w0 = ((back_words, 3 * P), (back_words, P), (late_words, 0), (late_words, 2 * P))[c]
            return words[:, w0 + h0 * P : w0 + h1 * P, :]

        def weigh(h, c, factors):
            scores = quarter_banks[h][c][:].rearrange("p t i -> p i t")
            nc.vector.tensor_tensor(g_words(c, h, h + 1), scores, factors.to_broadcast([P, P, PACK]), MULT)

        def quantize_g(c):
            quantize(g_op, c * ROW_PASSES * P, (c + 1) * ROW_PASSES * P, g_words(c, 0, ROW_PASSES), E5M2)

        xm_grouped = sbuf("xm_grouped", [P, 4 * P, PACK], BF16)
        block_words = [xm_grouped[:, 0 : 2 * P, :], xm_grouped[:, 2 * P :, :], back_words[:, 0 : 2 * P, :], back_words[:, 0 : 2 * P, :]]
        xm_ops = {}

        def xm_words(b, h):
            return block_words[b][:, h * P : (h + 1) * P, :]

        def group_xm_scalar(b, h):
            words, rows = four_by_four(xm_words(b, h), xm_raw[b, h])
            nc.scalar.copy(out=words, in_=rows)

        def group_xm_gpsimd(b, h):
            gpsimd_copy(xm_words(b, h), xm_raw[b, h].rearrange("p j d -> p d j"))

        def quantize_xm(b, codes_tag=None):
            xm_ops[b] = operand(f"xm{b}", ROW_PASSES * P, codes_tag)
            quantize(xm_ops[b], 0, ROW_PASSES * P, block_words[b], E4M3)

        def product(name, bank, b, quarters, copy, grad):
            acc = psum.tile([P, len(quarters) * P], F32, name=name, tag=f"bank{bank}")
            for n, c in enumerate(quarters):
                for h in range(ROW_PASSES):
                    g0 = (c * ROW_PASSES + h) * P
                    last = h == ROW_PASSES - 1
                    matmul(acc[:, n * P : (n + 1) * P], xm_ops[b], h * P, g_op, g0, g0 + P, E5M2, h == 0, last)
            copy(out=grad, in_=acc[:])

        def half_tile(name):
            return sbuf(name, [P, HALF], F32)[:]

        def scatter_scalar(b, slots, grad):
            nc.scalar.activation(out=listed(windows[b][:], slots), in_=grad, func=COPY)

        def scatter_vector(b, slots, grad):
            nc.vector.tensor_copy(listed(windows[b][:], slots), grad)

        def store(b):
            nc.sync.dma_start(out[b * P : (b + 1) * P, :], windows[b][:])

        for t in range(PACK):
            nc.scalar.activation(
                out=g0_late_tiles[:, t, :], in_=pair_banks[t // 2][:, t % 2, :], func=COPY, scale=weights[:, 0, t : t + 1]
            )
        gpsimd_copy(
            late_words[:].rearrange("p (c h i) t -> p c h i t", c=2, h=ROW_PASSES)[:, :, 0],
            g0_late_tiles.rearrange("p t (c i) -> p c i t", c=2),
        )
        for b, h in pieces[:5]:
            group_xm_scalar(b, h)

        for c in range(2):
            weigh(0, c, weights[:, 0:1, :])
        for c in range(2):
            weigh(1, c, early_weights[:])
        quarter_banks[1].append(psum.tile([P, PACK, P], F32, name="scores1_3", tag="bank5"))
        score_passes(1, [v_op, w_op], True, True, 3)
        quantize_g(0)
        quantize_xm(0, "early_weights")
        quantize_g(1)

        early0, late0 = half_tile("early0"), half_tile("late0")
        for c in range(2):
            product(f"early0_{c}", c, 0, [c], nc.scalar.copy, early0[:, c * P : (c + 1) * P])
        scatter_scalar(0, EARLY, early0)

        group_xm_gpsimd(2, 1)
        weigh(1, 2, weights[:, 1:2, :])
        weigh(1, 3, last_weights[:])
        for c in range(2, 4):
            quantize_g(c)
        quantize_xm(1, "last_weights")
        quantize_xm(2)
        for h in range(ROW_PASSES):
            group_xm_gpsimd(3, h)
        for c in range(2):
            product(f"late0_{c}", 4 + 3 * c, 0, [2 + c], nc.vector.tensor_copy, late0[:, c * P : (c + 1) * P])
        scatter_vector(0, LATE, late0)
        store(0)

        early1, late1 = half_tile("early1"), last_piece[:, 0:HALF]
        product("early1", 2, 1, [0, 1], nc.scalar.copy, early1)
        product("late1_0", 3, 1, [2], nc.scalar.copy, late1[:, 0:P])
        scatter_scalar(1, EARLY, early1)
        product("late1_1", 0, 1, [3], nc.vector.tensor_copy, late1[:, P:HALF])
        quantize_xm(3)
        scatter_vector(1, LATE, late1)
        store(1)

        early2, late2 = last_piece[:, HALF : 2 * HALF], last_piece[:, 2 * HALF :]
        product("early2", 6, 2, [0, 1], nc.scalar.copy, early2)
        product("late2", 5, 2, [2, 3], nc.scalar.copy, late2)
        scatter_scalar(2, EARLY, early2)
        scatter_scalar(2, LATE, late2)
        store(2)
        early3, late3 = half_tile("early3"), half_tile("late3")
        product("early3", 1, 3, [0, 1], nc.vector.tensor_copy, early3)
        product("late3", 2, 3, [2, 3], nc.vector.tensor_copy, late3)
        scatter_vector(3, EARLY, early3)
        scatter_vector(3, LATE, late3)
        store(3)
